import numpy as np, ml_dtypes
CORES = [2,6,10,14,18,22,26,30]
N = 8
BF = ml_dtypes.bfloat16
V, K, H, G, W, Q, RO = 1536, 3, 512, 240, 3216, 2, 5
AL = 0.25
def parts(rng):
    nm = np.where(rng.random((N, 8, V, 16)) < 0.4, rng.integers(0, V, (N, 8, V, 16)), rng.integers(0, W, (N, 8, V, 16)))
    dl = rng.integers(0, 1024, (N, 8, V, 16)); ph = rng.integers(0, 1024, (N, 8, V)); rb = rng.integers(0, 1024, (N, 8, V))
    lo = np.exp2(rng.random((N, 8, V, 1)) + 3.0 * rng.random((N, 8, V, 16)) - 1.0)
    fa = 0.875 + 0.125 * rng.random((N, 8, V, 16))
    return nm, dl, ph, rb, lo, fa
def turn(x):
    return np.ascontiguousarray(x.transpose(0, 1, 3, 2)).reshape(N, 128, V)
def pack(nm, dl, ph, rb, lo, fa):
    return {"loud": turn(np.clip(lo, 0.5, 8.0)).astype(BF), "fade": turn(np.clip(fa, 0.875, 1.0)).astype(BF), "ph0": ph.astype(np.int32), "rb": rb.astype(np.int32),
            "nb": turn(nm + 4096 * dl).astype(np.int32)}
def setup_inputs(rng):
    return pack(*parts(rng))
def newl(way, l, x, f):
    if way == 1: l, x, f = l.astype(np.float64), x.astype(np.float64), f.astype(np.float64)
    if way == 2: return (np.float32(1.0 - AL) * l + np.float32(AL) * x) * f
    if way == 3: return l * f + (np.float32(AL) * (x - l)) * f
    v = (l + np.float32(AL) * (x - l)) * f
    if way == 4: v = (np.rint(v.astype(np.float64) * 2.0 ** 21) * 2.0 ** -21).astype(np.float32)
    return v
def rivals(rng):
    n = 2 ** 18
    def some(low, high):
        return (low + (high - low) * rng.random(n)).astype(BF).astype(np.float32)
    z, fz, y, fy, a, fa = some(0.5, 1.0), some(0.875, 1.0), some(0.5, 1.0), some(0.875, 1.0), some(4.5, 7.5), some(0.875, 1.0)
    val = []
    for way in range(5):
        z1 = newl(way, z, z, fz) if K > 1 else z
        val.append(newl(way, newl(way, a, y, fa), newl(way, y, z1, fy), fa))
    o = np.argsort(val[0]); i, j = o[:-1], o[1:]; same = val[0][i] == val[0][j]; kinds = []
    for way in range(1, 5):
        w = val[way]
        m = same & (w[i] != w[j]); b, c = i[m], j[m]; up = w[b] < w[c]
        kinds.append((np.where(up, b, c), np.where(up, c, b)))
        m = ~same & (w[j] <= w[i]); kinds.append((i[m], j[m]))
    kinds = [p for p in kinds if len(p[0]) > 0] or [(np.array([0]), np.array([1]))]
    return kinds, z, fz, y, fy, a, fa
def close(rng, nm, dl, ph, rb, lo, fa):
    kinds, z, fz, y, fy, a, ff = rivals(rng)
    ix = np.zeros((N, 8, 32, 16), np.int64)
    for s in range(16):
        first, second = kinds[s % len(kinds)]; c = rng.integers(0, len(first), (N, 8, 16))
        ix[:, :, s] = first[c]; ix[:, :, 16 + s] = second[c]
    d = int(rng.integers(1, N)); e = int(rng.integers(1, N))
    tw = K * np.arange(32); zs = K * (32 + np.arange(32)); ys = K * (np.arange(32) + (64 if K == 1 else 0)) + K - 1
    ju = K * (H - 1 - np.arange(64)) + (RO - 1) % K
    iy = np.roll(ix, (-d, 1), axis=(0, 1)); iz = np.roll(iy, (-e, 1), axis=(0, 1))
    lo[:, :, tw] = a[ix]; fa[:, :, tw] = ff[ix]
    lo[:, :, ys] = y[iy]; fa[:, :, ys] = fy[iy]
    lo[:, :, zs] = z[iz]; fa[:, :, zs] = fz[iz]
    nm[:, :, tw] = (V + (d - 1) * G + ys)[:, None]
    nm[:, :, ys] = (V + (e - 1) * G + zs)[:, None]
    nm[:, :, zs] = zs[:, None]
    st = np.arange(64) % 16; blk = rng.integers(0, N, (N, 8, 64, 1)); cut = rng.integers(2, 16, (N, 8, 64, 1)); k = np.arange(16)
    base = np.where(blk == 0, 0, V + (blk - 1) * G)
    pair = base + np.where(k < cut, tw[st][:, None], tw[16 + st][:, None])
    nm[:, :, ju] = np.where(k == 0, (V + (d - 1) * G + ys[st])[:, None], pair)
    every = np.concatenate([tw, ys, zs, ju]); wait = rng.integers(0, 1024, (N, 8, len(every)))
    dl[:, :, every] = wait[..., None]; rb[:, :, every] = (-wait) & 1023; ph[:, :, every] = int(rng.integers(0, 1024))
def setup_inputs_spread(rng):
    nm, dl, ph, rb, lo, fa = parts(rng)
    nm = np.where(rng.random(nm.shape) < 0.5, nm, np.minimum((W * rng.random(nm.shape) ** 3).astype(np.int64), W - 1))
    dl = np.minimum(np.exp2(10 * rng.random(dl.shape)).astype(np.int64), 1024) - 1
    ph = np.minimum(np.exp2(10 * rng.random(ph.shape)).astype(np.int64), 1023)
    rb = np.minimum((1024 * rng.random(rb.shape) ** 2).astype(np.int64), 1023)
    lo = 2.0 * np.exp2(rng.integers(-1, 2, (N, 8, V, 1))) * np.exp2(2.0 * rng.random(lo.shape) - 1.0)
    fa = np.where(rng.random(fa.shape) < 0.5, fa, 1.0)
    close(rng, nm, dl, ph, rb, lo, fa)
    return pack(nm, dl, ph, rb, lo, fa)
def setup_inputs_ends(rng):
    nm, dl, ph, rb, lo, fa = parts(rng)
    dl = np.where(rng.random(dl.shape) < 0.9, 1023 * rng.integers(0, 2, dl.shape), dl)
    u = rng.random(nm.shape); low, high = u < 0.35, u > 0.65
    nm = np.where(low, 0, np.where(high, W - 1, nm)); dl = np.where(low, 0, np.where(high, 1023, dl))
    ph = np.where(rng.random(ph.shape) < 0.9, 1023 * rng.integers(0, 2, ph.shape), ph); rb = np.where(rng.random(rb.shape) < 0.9, 1023 * rng.integers(0, 2, rb.shape), rb)
    lo = np.where(rng.random(lo.shape) < 0.75, np.where(rng.random(lo.shape) < 0.5, 0.5, 8.0), lo)
    fa = np.where(rng.random(fa.shape) < 0.8, np.where(rng.random(fa.shape) < 0.5, 0.875, 1.0), fa)
    ph[:, ::2, G - 1] = 0
    lad = V - 1 - K * np.arange(16, 0, -1); b = V - 1 - 17 * K
    lo[:, 3::4, lad] = (8.0 - 0.03125 * (15 - np.arange(16)))[:, None]
    ph[:, 3::4, lad] = 0; ph[:, 3::4, V - 1] = 0; ph[:, 3::4, b] = 0; rb[:, 3::4, V - 1] = 1023
    nm[:, 3::4, V - 1] = lad; dl[:, 3::4, V - 1] = 1008 + np.arange(16)
    nm[:, 3::4, b] = lad[15]; dl[:, 3::4, b] = 1023
    return pack(nm, dl, ph, rb, lo, fa)
def setup_inputs_crowd(rng):
    nm, dl, ph, rb, lo, fa = parts(rng)
    place = np.array([0, V - 1, V, W - 1]); one = np.arange(16)[None, None, :] == rng.integers(0, 16, (N, V, 1))
    nm[:, 0] = 0
    nm[:, 1] = np.where(one, nm[:, 1], W - 1)
    nm[:, 2] = rng.choice(place, (N, V, 1))
    nm[:, 3] = rng.choice(place, (N, V, 16)); dl[:, 3] = rng.choice(np.array([0, 1, 512, 1023]), (N, V, 16))
    nm[:, 4] = V - 1; dl[:, 4] = 1023
    nm[:, 5] = np.where(one, nm[:, 5], V - 1); dl[:, 5] = rng.integers(0, 1024, (N, V, 1))
    return pack(nm, dl, ph, rb, lo, fa)
def setup_inputs_bands(rng):
    nm, dl, ph, rb, lo, fa = parts(rng)
    lev = np.argsort(rng.random((N, 8, V, 16)), axis=3); nm = 16 * rng.integers(0, W // 16, (N, 8, V, 16)) + lev
    for g in (1, 4, 7): nm[:, g] = nm[:, g] % V
    way = rng.integers(0, 3, (N, 8, V, 1)); dl = np.where(way == 0, 64 * lev, np.where(way == 1, 64 * (15 - lev), rng.integers(0, 1024, (N, 8, V, 1))))
    ph[:] = rng.integers(0, 1024); o = rng.permutation(16); rise = 0.5 + 0.4375 * (np.arange(V) % 16)
    for g in range(8):
        n = (16, 16, Q, Q, Q, Q - 1, Q - 1, Q - 1)[g]
        lo[:, g] = 2.0
        for b in o[:n]: lo[:, g, :, b] = rise
    fa[:, 2:] = 1.0
    return pack(nm, dl, ph, rb, lo, fa)
def setup_inputs_calm(rng):
    nm, dl, ph, rb, lo, fa = parts(rng)
    for g in (1, 3): nm[:, g] = nm[:, g] % V
    d8 = np.array([8, 1023, 512, 3, 0, 1, 1023, 16])[None, :, None]; step = np.array([1, 0, 0, -1, 1, 1, 0, 1])[None, :, None]
    ph = rng.integers(0, 4, (N, 8, V)); ph[:, 0] = 0; ph[:, 4] = rng.integers(0, 2, (N, V)); ph[:, 2:4] = 1023 - rng.integers(0, 2, (N, 2, V))
    rb = (step * (rng.random((N, 8, V)) < 0.25) - d8) & 1023
    return pack(nm, np.zeros_like(dl) + d8[..., None], ph, rb, lo, fa)
def check_ranges(d):
    bad = []
    for k, lo, hi in (("loud", 0.5, 8.0), ("fade", 0.875, 1.0), ("ph0", 0, 1023), ("rb", 0, 1023), ("nb", 0, 4096 * 1023 + W - 1)):
        x = np.asarray(d[k], np.float64)
        if not (np.min(x) >= lo and np.max(x) <= hi): bad.append("range of " + k)
    if np.max(np.asarray(d["nb"]).astype(np.int64) & 4095) >= W: bad.append("a name in nb")
    return bad
def reference(loud, fade, ph0, rb, nb):
    L = np.ascontiguousarray(loud.astype(np.float32).reshape(N, 8, 16, V).transpose(0, 1, 3, 2))
    fd = np.ascontiguousarray(fade.astype(np.float32).reshape(N, 8, 16, V).transpose(0, 1, 3, 2))
    lst = np.ascontiguousarray(nb.astype(np.int64).reshape(N, 8, 16, V).transpose(0, 1, 3, 2))
    p = ph0.astype(np.int64); add = rb.astype(np.int64); E = np.zeros((N, 8, V, 16), np.float64)
    gi = np.arange(8)[:, None, None]; kk = np.arange(16)
    for t in range(RO):
        c = slice(t % K, V, K)
        L2, p2, lst2 = L.copy(), p.copy(), lst.copy()
        for r in range(N):
            wl = np.concatenate([L[r]] + [np.roll(L[(r - d) % N][:, :G], -1, axis=0) for d in range(1, N)], axis=1)
            wp = np.concatenate([p[r]] + [np.roll(p[(r - d) % N][:, :G], -1, axis=0) for d in range(1, N)], axis=1)
            mine = lst[r][:, c]
            nm = mine & 4095; a = (wp[gi, nm] + (mine >> 12) - p[r][:, c][:, :, None]) & 1023
            o = np.argsort(16 * a + kk, axis=2)
            nm = np.take_along_axis(nm, o, 2); a = np.take_along_axis(a, o, 2)
            x = wl[gi, nm]
            top = np.maximum.accumulate(x, axis=2); m = np.zeros_like(x); m[:, :, 1:] = top[:, :, :-1]
            free = np.count_nonzero(x > m, axis=3) >= Q
            xf = x[free].astype(np.float64); z = np.zeros(x.shape, np.float64)
            z[free] = xf * np.reciprocal(1.0 + np.exp(m[free].astype(np.float64) - xf))
            E[r][:, c] += np.add.reduce(z, axis=2)
            p2[r][:, c] = (p[r][:, c] + np.maximum.reduce(np.where(free, a, 0), axis=2) + add[r][:, c]) & 1023
            if t < RO - 1:
                own = L[r][:, c]; L2[r][:, c] = (own + np.float32(AL) * (top[:, :, 15] - own)) * fd[r][:, c]
            if t < RO - K:
                first = nm[:, :, 0]; got = lst[r][gi[:, :, 0], np.minimum(first, V - 1)]
                hid = np.zeros(free.shape, bool); np.put_along_axis(hid, o, ~free, 2)
                lst2[r][:, c] = np.where(hid & (first < V)[:, :, None], got, mine)
        L, p, lst = L2, p2, lst2
    return {"ye": np.ascontiguousarray(E.transpose(0, 1, 3, 2)).reshape(N, 128, V).astype(np.float32), "yp": np.asarray(p, np.float32)}

def check_inputs(d):
    bad = list(check_ranges(d))
    if not bad:
        for name, y in reference(**d).items():
            for q in range(N):
                v = np.abs(np.asarray(y[q], np.float64)); s = np.sqrt(np.mean(v * v))
                if v.max() > 6 * s or s < 2.0 ** 2: bad.append('%s of rank %d is uneven or too small' % (name, q))
    return bad

@@ -1,0 +1,661 @@
+import math
+import numpy as np
+from concourse.bass import DstId, RemoteDMATransfer
+from concourse.mybir import AluOpType as A, AxisListType, ActivationFunctionType as AF
+
+N, V, H, GH, W, RO = 8, 1536, 512, 240, 3216, 5
+CH = 256
+NCH = H // CH
+B = 16 * CH
+NTH = 9
+NB = 2
+MP = 1024
+GP = 1024
+SP = 1024
+EG = 4
+HS = 1
+QS = 1
+GC = 1
+NG = GH // 3
+MAGIC = 1.5 * 2.0 ** 33
+f32, bf, f16, i32, u16 = "float32", "bfloat16", "float16", "int32", "uint16"
+
+SCRATCH = {
+    "Lw": ("sbuf", [128, W], f32), "Lb": ("sbuf", [128, W], bf), "Pw": ("sbuf", [128, W], bf),
+    "Rw": ("sbuf", [128, V], bf), "Fd": ("sbuf", [128, V], bf), "Nw": ("sbuf", [128, V], i32),
+    "E": ("sbuf", [128, V], f32), "YP": ("sbuf", [128, V], f32),
+    "R": ("sbuf", [128, 288], i32), "Rh": ("sbuf", [128, 288], bf), "Rl": ("sbuf", [128, 288], bf),
+    "S0L": ("sbuf", [128, GH], bf), "S0P": ("sbuf", [128, GH], bf),
+    "SB": ("sbuf", [128, 4 * 2 * NG], f32), "ST": ("sbuf", [128, 4 * 7, 2 * NG], f32),
+    "NM": ("sbuf", [128, 3 * H], u16), "DL": ("sbuf", [128, 3 * H], f16),
+    "LO": ("sbuf", [128, 3 * H], i32), "HI": ("sbuf", [128, 3 * H], i32), "MN": ("sbuf", [128, 2 * H], i32),
+    "NT": ("sbuf", [128, H], i32),
+    "TH": ("sbuf", [128, NTH * 2 * CH], f16), "MASK": ("sbuf", [128, MP], bf),
+    "ROW": ("sbuf", [128, 256], bf), "ROWG": ("sbuf", [128, 128], bf), "VR": ("sbuf", [128, 256], bf),
+    "IP": ("sbuf", [128, 4], i32), "IT": ("sbuf", [128, 32], i32), "C": ("sbuf", [128, 32], f32),
+    "TG": ("sbuf", [128, 16], f32), "BS": ("sbuf", [128, 16], f32), "QT": ("sbuf", [128, 16], f32),
+    "PT": ("sbuf", [128, 16], f32), "VT": ("sbuf", [128, 64], f32),
+    "Dm": ("sbuf", [128, 8 * 128], f16), "Km": ("sbuf", [128, 8 * 128], bf), "Qm": ("sbuf", [128, 16 * 136], bf),
+    "Hm": ("sbuf", [128, 3 * 128], f16), "Bm": ("sbuf", [128, 4 * 128], bf), "Fm": ("sbuf", [128, 2 * 128], f32),
+    "Wb": ("sbuf", [128, 2 * 144], bf), "Wh": ("sbuf", [128, 5 * 144], f16), "KK": ("sbuf", [128, 2 * CH], f16),
+    "pA0": ("psum", [128, 512], f32), "pA1": ("psum", [128, 512], f32), "pD0": ("psum", [128, 512], f32),
+    "pD1": ("psum", [128, 512], f32), "pB": ("psum", [128, 512], f32), "pE": ("psum", [128, 512], f32),
+    "pM": ("psum", [128, 1024], f32),
+}
+for _b in range(NB):
+    SCRATCH["X%d" % _b] = ("sbuf", [128, B + 8], f32)
+    SCRATCH["D%d" % _b] = ("sbuf", [128, B], f32)
+    SCRATCH["OF%d" % _b] = ("sbuf", [128, CH], u16)
+for _b in range(2):
+    for _n, _c, _d in (("G", B, bf), ("SG", 8 * CH, bf), ("RR", CH, f32), ("A16", CH, f16),
+                       ("VAL", 2 * CH, f16), ("POW", CH, bf), ("SN", CH, u16), ("N16", CH, f16), ("F", CH, bf),
+                       ("EA", CH, f16), ("HB", CH, bf), ("SI", CH, i32), ("HQ", CH, i32), ("GD", CH, f32),
+                       ("CT", 64, f32), ("CO", 16, u16)):
+        SCRATCH["%s%d" % (_n, _b)] = ("sbuf", [128, _c], _d)
+NDMA = 16
+SEMAPHORES = ["cv", "cs", "ct", "cg", "left", "arL", "arP"] + ["ar%d" % _b for _b in range(4)] + \
+             ["d%d" % _b for _b in range(NDMA)]
+
+CYC = 0.83 * 1.25
+PCYC = 0.42 * 1.25
+GAM = 1.56
+VO = 25.0
+SCEN = [(VO, GAM), (VO, 1.15), (VO, 1.95)]
+LAT_X, LAT_S = 120.0, 80.0
+
+
+def masks(topo, T, src):
+    far = [c for c in T.cores if topo.chip(c) != topo.chip(src)]
+    near = [c for c in T.cores if c != src and topo.chip(c) == topo.chip(src)]
+    fe = topo.engines(src, far[0])
+    ne = [e for e in topo.engines(src, near[0]) if e not in fe]
+    return far, near, fe, ne
+
+
+def build(g, core, T, topo):
+    rank = T.rank_of(core)
+    ops = []
+    lastw, readers, lastbank = {}, {}, {}
+    ndma = [0]
+
+    def op(eng, cost, fn, r=(), w=(), banks=(), sem=None, val=0, lat=0.0, after=()):
+        me = len(ops)
+        hard, soft = set(after), set()
+        asyn = sem is not None
+        for k in r:
+            if k in lastw: hard.add(lastw[k])
+        for k in w:
+            for o in readers.get(k, []) + ([lastw[k]] if k in lastw else []):
+                if eng == "t" and ops[o]["eng"] == "t": soft.add(o)
+                else: hard.add(o)
+        for b in banks:
+            for e, o in lastbank.setdefault(b, {}).items():
+                (soft if e == eng else hard).add(o)
+            lastbank[b][eng] = me
+        for k in r: readers.setdefault(k, []).append(me)
+        for k in w:
+            lastw[k] = me
+            readers[k] = []
+        if not isinstance(cost, list): cost = [cost] * len(SCEN)
+        ops.append({"eng": eng, "cost": cost[0], "costs": cost, "fn": fn, "hard": hard, "soft": soft - hard, "sem": sem, "val": val, "lat": lat,
+                    "name": w[-1] if w else None})
+        return me
+
+    def vcost(n, f=1.0):
+        if f == GAM: return [50 + n * ga * CYC for vo, ga in SCEN]
+        return [vo + max(64, n * f) * CYC for vo, ga in SCEN]
+
+    def ts(out, in0, s1, s2, o0, o1, n, r, w, banks=(), f=1.0):
+        if o1 is None:
+            return op("v", vcost(n, f), lambda: g.vector.tensor_scalar(out, in0, s1, None, o0), r, w, banks)
+        return op("v", vcost(n, f), lambda: g.vector.tensor_scalar(out, in0, s1, s2, o0, o1), r, w, banks)
+
+    def tt(out, a, b, o, n, r, w, banks=(), f=None):
+        if f is None: f = 1.0 if banks else 2.0
+        return op("v", vcost(n, f), lambda: g.vector.tensor_tensor(out, a, b, o), r, w, banks)
+
+    def cp(out, a, n, r, w, banks=(), f=1.0):
+        return op("v", vcost(n, f), lambda: g.vector.tensor_copy(out, a), r, w, banks)
+
+    def ms(out, c, n, w):
+        return op("v", vcost(n), lambda: g.vector.memset(out, c), (), w)
+
+    def act(out, a, func, n, r, w, banks=(), f=1.0, bias=None, scale=None):
+        kw = {}
+        if bias is not None: kw["bias"] = bias
+        if scale is not None: kw["scale"] = scale
+        cost = [65 + n * (ga if f == GAM else f) * CYC for vo, ga in SCEN]
+        return op("s", cost, lambda: g.scalar.activation(out, a, func, **kw), r, w, banks)
+
+    def mm(items, r, w, banks):
+        def fn():
+            ins = None
+            for o, l, x, st, sp, _ in items:
+                ins = g.tensor.matmul(o, l, x, st, sp)
+            return ins
+        return op("t", 30 + sum(max(64, it[5]) for it in items) * PCYC, fn, r, w, banks)
+
+    def grp(out, pairs, n, first=True, last=True):
+        return [(out, l, x, first and i == 0, last and i == len(pairs) - 1, n) for i, (l, x) in enumerate(pairs)]
+
+    def gcopy(out, a, n, r, w):
+        return op("g", 170 + 2 * n * CYC, lambda: g.affine_select(out, a, [[0, n]], A.is_ge, 0.0, 0, 0), r, w)
+
+    def iota(out, pat, base, cm, n, w, flag):
+        if flag:
+            return op("g", 130 + 2 * n * CYC,
+                      lambda: g.iota(out, pat, base, cm, allow_small_or_imprecise_dtypes=True), (), w)
+        return op("g", 130 + 2 * n * CYC, lambda: g.iota(out, pat, base, cm), (), w)
+
+    def dma(pairs, r, w, lat=2200.0, eng="y"):
+        sem = T.sem["d%d" % ndma[0]]
+        ndma[0] += 1
+        q = g.sync if eng == "y" else g.scalar
+
+        def fn():
+            for o, a in pairs: q.dma_start(o, a).then_inc(sem, 16)
+        return op(eng, 60.0 * len(pairs), fn, r, w, sem=sem, val=16 * len(pairs), lat=lat)
+
+    far, near, fe, ne = masks(topo, T, core)
+    nleft = [0]
+
+    sent = []
+
+    def send(src, dst_of, sem, r, w, lat, parts=((far, fe), (near, ne))):
+        trs = []
+        for cs, en in parts:
+            ids = [DstId(rid=topo.addr(c)[0], pnc=topo.addr(c)[1]) for c in cs]
+            ds = [dst_of((T.rank_of(c) - rank) % N) for c in cs]
+            trs.append(RemoteDMATransfer(dst_ids=ids, dma_engine_mask=sum(1 << e for e in en), remote_sem=sem,
+                                         srcs=[src], dsts=ds))
+            nleft[0] += len(en)
+
+        def fn():
+            g.remote_dma_fused(trs, local_sem=T.sem.left)
+        s = op("g", 400.0, fn, r, (), sem=T.sem.left, val=-1, lat=0.0)
+        ops[s]["soft"] |= set(sent)
+        sent.append(s)
+        if not w: return s
+        got = 0
+        for c in T.cores:
+            if c != core:
+                cf, cn, cfe, cne = masks(topo, T, c)
+                got += len(cfe) if core in cf else len(cne)
+        return op("x", 0.0, None, (), w, sem=sem, val=got, lat=lat, after=[s])
+
+    col = lambda j: T.C[:, j:j + 1]
+    PF, PM, G16, G15, M01, NM01, M0, ODD, OCOL, CC, WC, SH, G2, PM3, T1, T2 = range(16)
+    Lk = lambda: [("L", c, q) for c in range(3) for q in range(NCH)] + [("Lg", c) for c in range(3)]
+    Pk = lambda: [("P", c, q) for c in range(3) for q in range(NCH)] + [("Pg", c) for c in range(3)]
+    Nk = lambda: [("N", c, q) for c in range(3) for q in range(NCH)]
+
+    dma([(T.R[0:112, 96:192], T.ph0[1:8, :]), (T.R[112:128, 96:192], T.ph0[0:1, :]), (T.R[:, 0:96], T.ph0[:, :])],
+        (), ["Rph"])
+    dma([(T.S0L[0:112, :], T.loud[16:128, 0:GH]), (T.S0L[112:128, :], T.loud[0:16, 0:GH])], (), ["S0L"], eng="s")
+    dma([(T.Nw[:, :], T.nb[:, :])], (), Nk(), lat=3200.0, eng="s")
+    dma([(T.R[:, 192:288], T.rb[:, :])], (), ["Rrb"])
+    dma([(T.Lb[:, 0:V], T.loud[:, :])], (), ["Lb"], lat=3000.0)
+    dma([(T.Fd[:, :], T.fade[:, :])], (), ["Fd"], lat=3000.0)
+    lghost = lambda d: T.Lb[:, V + (d - 1) * GH:V + d * GH]
+    send(T.S0L[:, :], lghost, T.sem.arL, ["S0L"], (), 0.0, [(near, ne)])
+
+    iota(T.IP[:, 0:1], [[0, 1]], 0, 1, 1, ["IP"], False)
+    iota(T.ROW[:, :], [[1, 256]], 0, 0, 256, ["ROW"], True)
+    iota(T.ROWG[:, :], [[16, 8], [0, 16]], 0, 0, 128, ["ROWG"], True)
+    iota(T.IT[:, 0:16], [[-1, 16]], 16, 1, 16, ["IT"], False)
+    iota(T.VT[:, :], [[1, 2], [48, 32]], -V, 0, 64, ["VT"], True)
+    ts(T.IP[:, 1:2], T.IP[:, 0:1], 15, None, A.bitwise_and, None, 1, ["IP"], ["IP1"])
+    cp(col(PM), T.IP[:, 1:2], 1, ["IP1"], [PM])
+    cp(col(PF), T.IP[:, 0:1], 1, ["IP"], [PF])
+    ts(col(G16), col(PF), col(PM), None, A.subtract, None, 1, [PF, PM], [G16])
+    ts(col(G2), col(G16), 2.0, None, A.add, None, 1, [G16], [G2])
+    ts(T.QT[:, :], T.ROW[:, 0:16], col(PM), col(G2), A.is_equal, A.mult, 16, ["ROW", PM, G2], ["QT"])
+    for s in range(16):
+        ts(T.Qm[:, 136 * s:136 * s + 130], T.ROW[:, 1:131], T.QT[:, s:s + 1], None, A.is_equal, None, 130,
+           ["ROW", "QT"], [("Q", s)], f=0.5)
+    Qhi = lambda s: T.Qm[:, 136 * s + 1:136 * s + 129]
+    Qlo = lambda s: T.Qm[:, 136 * s:136 * s + 128]
+    ts(col(G15), col(G16), 15.0, None, A.add, None, 1, [G16], [G15])
+    ts(col(M01), col(PM), 2.0, None, A.is_lt, None, 1, [PM], [M01])
+    ts(col(NM01), col(PM), 2.0, -1.0, A.is_lt, A.mult, 1, [PM], [NM01])
+    ts(col(M0), col(PM), 0.0, None, A.is_equal, None, 1, [PM], [M0])
+    ts(col(ODD), col(PM), 1.0, None, A.is_equal, None, 1, [PM], [ODD])
+    ts(col(OCOL), col(PM), 8.0 - 8192.0, None, A.add, None, 1, [PM], [OCOL])
+    ts(col(PM3), col(PM), 3.0, None, A.mult, None, 1, [PM], [PM3])
+    ts(T.VT[:, :], T.VT[:, :], col(PM3), None, A.add, None, 64, ["VT", PM3], ["VT"])
+    ts(col(T1), col(PM), 1.0, 8320.0, A.add, A.mult, 1, [PM], [T1])
+    ts(col(T2), col(PM), 15.0, -1131520.0, A.is_equal, A.mult, 1, [PM], [T2])
+    ts(col(CC), col(T1), col(T2), None, A.add, None, 1, [T1, T2], [CC])
+    ts(T.PT[:, :], T.ROW[:, 0:16], col(PM), 1.0, A.is_lt, A.add, 16, ["ROW", PM], ["PT"])
+    op("v", vcost(16), lambda: g.vector.tensor_reduce(col(16), T.PT[:, :], AxisListType.X, A.mult), ["PT"], [16])
+    ts(col(17), col(M0), 0.5, col(16), A.mult, A.add, 1, [M0, 16], [17])
+    ts(col(WC), col(17), 2.0 ** 23, None, A.mult, None, 1, [17], [WC])
+    ts(col(18), col(PF), 16.0, 128.0, A.is_lt, A.mult, 1, [PF], [18])
+    ts(col(SH), col(PF), -16.0, col(18), A.add, A.add, 1, [PF, 18], [SH])
+    ts(T.IT[:, 16:32], T.IT[:, 0:16], 15, None, A.bitwise_and, None, 16, ["IT"], ["IT1"])
+    ts(T.TG[:, :], T.IT[:, 16:32], col(G16), None, A.add, None, 16, ["IT1", G16], ["TG"])
+    ts(T.BS[:, :], T.ROW[:, 0:16], col(PM), 16.0, A.add, A.is_ge, 16, ["ROW", PM], ["BS"])
+    ts(T.BS[:, :], T.BS[:, :], -0.5, None, A.add, None, 16, ["BS"], ["BS"])
+    r128 = T.ROW[:, 0:128]
+    blk = lambda t, j, n=128: t[:, n * j:n * j + n]
+    I16, I64h, BD16 = blk(T.Hm, 0), blk(T.Hm, 1), blk(T.Hm, 2)
+    S01, N01, Wm, Shb = [blk(T.Bm, j) for j in range(4)]
+    If, Shf = blk(T.Fm, 0), blk(T.Fm, 1)
+    I64b = blk(T.Km, 7)
+    ts(I16, r128, col(PF), None, A.is_equal, None, 128, ["ROW", PF], ["I16"], f=0.5)
+    ts(I64h, r128, col(PF), 64.0, A.is_equal, A.mult, 128, ["ROW", PF], ["I64h"], f=0.5)
+    ts(I64b, r128, col(PF), 64.0, A.is_equal, A.mult, 128, ["ROW", PF], [("K", 8)], f=0.5)
+    ts(If, r128, col(PF), None, A.is_equal, None, 128, ["ROW", PF], ["If"])
+    ts(Shf, r128, col(SH), None, A.is_equal, None, 128, ["ROW", SH], ["Shf"])
+    ts(Shb, r128, col(SH), None, A.is_equal, None, 128, ["ROW", SH], ["Shb"], f=0.5)
+    ts(BD16, T.ROWG[:, :], col(G16), None, A.is_equal, None, 128, ["ROWG", G16], ["BD16"], f=0.5)
+    for m, c, k in ((S01, M01, "S01"), (N01, NM01, "N01"), (Wm, WC, "Wm")):
+        ts(m, T.ROWG[:, :], col(G16), col(c), A.is_equal, A.mult, 128, ["ROWG", G16, c], [k], f=0.5)
+    for s in range(1, 9):
+        ts(blk(T.Dm, s - 1), r128, T.TG[:, s:s + 1], -64.0, A.is_equal, A.mult, 128, ["ROW", "TG"], [("Dm", s)], f=0.5)
+        tt(blk(T.Dm, s - 1), blk(T.Dm, s - 1), I64h, A.add, 128, [("Dm", s), "I64h"], [("Dm", s)])
+    for s in range(1, 8):
+        ts(blk(T.Km, s - 1), r128, T.TG[:, 16 - s:17 - s], -64.0, A.is_equal, A.mult, 128, ["ROW", "TG"], [("K", s)], f=0.5)
+        tt(blk(T.Km, s - 1), blk(T.Km, s - 1), I64b, A.add, 128, [("K", s), ("K", 8)], [("K", s)])
+    r144 = T.ROW[:, 0:144]
+    for t_, j, c, k, rd in ((T.Wb, 0, 1.0, "Cw", []), (T.Wb, 1, col(M01), "Cw01", [M01]), (T.Wh, 0, 1.0, "C16", []),
+                            (T.Wh, 1, 64.0, "C64", []), (T.Wh, 2, col(M0), "Cw0", [M0])):
+        ts(blk(t_, j, 144), r144, col(G15), c, A.is_equal, A.mult, 144, ["ROW", G15] + rd, [k], f=0.5)
+    for j, k in ((0, "C16"), (1, "C64")):
+        tt(T.Wh[:, 144 * (3 + j):144 * (3 + j) + 143], T.Wh[:, 144 * j:144 * j + 143],
+           T.Wh[:, 144 * j + 1:144 * j + 144], A.subtract, 143, [k], ["P" + k])
+    wide = lambda t_, j, k: t_[:, 144 * j + 15 - k:144 * j + 143 - k]
+    ts(T.VR[:, :], T.ROW[:, :], 0.25, None, A.mult, None, 256, ["ROW"], ["VR"], f=0.5)
+    ts(T.KK[:, 0:CH], T.ROW[:, 0:CH], 0.0, -512.5, A.mult, A.add, CH, ["ROW"], ["K1"], f=0.5)
+    ts(T.KK[:, CH:2 * CH], T.ROW[:, 0:CH], 0.0, 511.5, A.mult, A.add, CH, ["ROW"], ["K2"], f=0.5)
+    ms(T.MASK[:, :], 1.0, MP // 2, ["MASK"])
+    op("v", vcost(MP // 16), lambda: g.vector.memset(T.MASK[:, 0:MP:16], 0.0), ["MASK"], ["MASK"])
+    for b in range(NB):
+        ms(T["X%d" % b][:, 0:8], 0.0, 8, [("X0", b)])
+
+    cp(T.Rh[:, 0:192], T.R[:, 0:192], 192, ["Rph"], ["Rh"])
+    tt(T.Rl[:, 0:192], T.R[:, 0:192], T.Rh[:, 0:192], A.subtract, 192, ["Rph", "Rh"], ["Rl"])
+    its = []
+    for s, n in ((0, 96), (1, 96), (2, 48)):
+        its += grp(T.pB[:, 96 * s:96 * s + n], [(Qhi(s), T.Rh[:, 96:96 + n]), (Qlo(s), T.Rl[:, 96:96 + n])], n)
+    mm(its, ["Rh", "Rl"] + [("Q", s) for s in range(3)], ["pB"], ["B"])
+    act(T.S0P[:, :], T.pB[:, 0:GH], AF.Copy, GH, ["pB"], ["S0P"], ["B"])
+    send(T.S0P[:, :], lambda d: T.Pw[:, V + (d - 1) * GH:V + d * GH], T.sem.arP, ["S0P"],
+         [("Pg", c) for c in range(3)], 5000.0)
+    send(T.S0L[:, :], lghost, T.sem.arL, ["S0L"], ["Lbg"], 8000.0, [(far, fe)])
+    cp(T.Rh[:, 192:288], T.R[:, 192:288], 96, ["Rrb"], ["Rh2"])
+    tt(T.Rl[:, 192:288], T.R[:, 192:288], T.Rh[:, 192:288], A.subtract, 96, ["Rrb", "Rh2"], ["Rl2"])
+    own = [("P", c, q) for c in range(3) for q in range(NCH)]
+    for o, dst, ks, keys in ((0, T.Pw, ["Rh", "Rl"], own), (192, T.Rw, ["Rh2", "Rl2"], ["Rw"])):
+        for j in range(4):
+            bank = ("D0", "D1")[j % 2]
+            its = []
+            for s in range(4 * j, 4 * j + 4):
+                its += grp(T["p" + bank][:, 96 * (s % 4):96 * (s % 4) + 96],
+                           [(Qhi(s), T.Rh[:, o:o + 96]), (Qlo(s), T.Rl[:, o:o + 96])], 96)
+            mm(its, ks + [("Q", s) for s in range(4 * j, 4 * j + 4)], ["p" + bank], [bank])
+            kw = [("init", o, j)] + (keys if j == 3 else [])
+            kr = ["p" + bank] + ([("init", o, i) for i in range(3)] if j == 3 else [])
+            if o == 0 and j % 2 == 0:
+                act(dst[:, 384 * j:384 * j + 384], T["p" + bank][:, 0:384], AF.Copy, 384, kr, kw, [bank])
+            else:
+                cp(dst[:, 384 * j:384 * j + 384], T["p" + bank][:, 0:384], 384, kr, kw, [bank])
+    for c in range(2):
+        gcopy(T.MN[:, H * c:H * (c + 1)], T.Nw[:, c:V:3], H, [("N", c, q) for q in range(NCH)], [("MN", c)])
+    gcopy(T.Lw[:, 0:V], T.Lb[:, 0:V], V, ["Lb"], [("L", c, q) for c in range(3) for q in range(NCH)])
+    gcopy(T.Lw[:, V:W], T.Lb[:, V:W], W - V, ["Lbg"], [("Lg", c) for c in range(3)])
+
+    def derive(t, q):
+        c = t % 3
+        src = T.Nw[:, c + 3 * CH * q:3 * CH * (q + 1):3]
+        sl = slice(H * c + CH * q, H * c + CH * (q + 1))
+        nt = T.NT[:, CH * q:CH * (q + 1)]
+        k = [("N", c, q)]
+        ts(nt, src, 4095, None, A.bitwise_and, None, CH, k, [("NT", q)])
+        (gcopy if GC > 1 and t else cp)(T.NM[:, sl], nt, CH, [("NT", q)], [("NM", c, q)])
+        ts(T.DL[:, sl], src, 2.0 ** -12, 1024.6, A.mult, A.add, CH, k, [("DL", c, q)])
+        ts(T.LO[:, sl], src, 63, None, A.bitwise_and, None, CH, k, [("LO", c, q)])
+        ts(T.HI[:, sl], src, 6, 63, A.logical_shift_right, A.bitwise_and, CH, k, [("HI", c, q)])
+
+    for t in range(3):
+        for q in range(NCH): derive(t, q)
+
+    def front(t, q):
+        c, z = t % 3, q % 2
+        bA = "A%d" % z
+        pA = T["p" + bA]
+        lo, hi = pA[:, 0:CH], pA[:, 256:256 + CH]
+        o = H * c + CH * q
+        vs = slice(c + 3 * CH * q, 3 * CH * (q + 1), 3)
+        G, SG, RR, A16, VAL = T["G%d" % z], T["SG%d" % z], T["RR%d" % z], T["A16%d" % z], T["VAL%d" % z]
+        n = GP // 16
+        gk = lambda j: [("IND", z, i) for i in range(j * GP // SP, ((j + 1) * GP - 1) // SP + 1)]
+        for j in range(B // GP):
+            act(G[:, GP * j:GP * (j + 1)], T.Pw[:, 0:W].indirect(T.NM[:, o + n * j:o + n * (j + 1)]), AF.Copy, GP,
+                Pk() + [("NM", c, q)], gk(j), f=GAM)
+            pairs = [(wide(T.Wb, 1, k), G[:, GP * j + k:GP * (j + 1):16]) for k in range(16)]
+            pairs += [(I16, T.DL[:, o + n * j:o + n * (j + 1)]), (I16, T.KK[:, 0:n]),
+                      (N01, T.Pw[:, c + 3 * (CH * q + n * j):3 * (CH * q + n * (j + 1)):3])]
+            mm(grp(pA[:, n * j:n * (j + 1)], pairs, n),
+               gk(j) + ["Cw01", "I16", ("DL", c, q), "K1", "N01", ("P", c, q)], [bA + "l"], [bA])
+        ts(RR[:, :], lo, MAGIC, MAGIC, A.add, A.subtract, CH, [bA + "l"], [("RR", z)], [bA])
+        tt(A16[:, :], lo, RR[:, :], A.subtract, CH, [bA + "l", ("RR", z)], [("A16", z)], [bA])
+        per = 512 // CH
+        for j in range(8 // per):
+            bank = ("D0", "D1")[j % 2]
+            its = []
+            for i in range(per):
+                its += grp(T["p" + bank][:, CH * i:CH * (i + 1)], [(blk(T.Dm, per * j + i), A16[:, :])], CH)
+            mm(its, [("A16", z)] + [("Dm", per * j + i + 1) for i in range(per)], ["p" + bank], [bank])
+            for i in range(per):
+                s = per * j + i + 1
+                act(blk(SG, s - 1, CH), T["p" + bank][:, CH * i:CH * (i + 1)], AF.Sign, CH, ["p" + bank, "BS"],
+                    [("SG", z, s)], [bank], bias=T.BS[:, s:s + 1])
+        for j in range(2):
+            ss = range(4 * j + 1, 4 * j + 5)
+            mm(grp(hi, [(blk(T.Km, s - 1), blk(SG, s - 1, CH)) for s in ss], CH, j == 0, j == 1),
+               [("SG", z, s) for s in ss] + [("K", s) for s in ss], [bA + "h"], [bA])
+        tt(VAL[:, 0:CH], hi, T.LO[:, o:o + CH], A.add, CH, [bA + "h", ("LO", c, q)], [("VL", z)], [bA])
+        tt(VAL[:, CH:2 * CH], hi, T.HI[:, o:o + CH], A.add, CH, [bA + "h", ("HI", c, q)], [("VH", z)], [bA])
+        act(T["POW%d" % z][:, :], hi, AF.Sigmoid, CH, [bA + "h"], [("POW", z)], [bA],
+            bias=-37.5 * math.log(2.0), scale=-math.log(2.0) / 128.0)
+        mm(grp(lo, [(wide(T.Wh, 0, 0), VAL[:, 0:CH]), (wide(T.Wh, 1, 0), VAL[:, CH:2 * CH])], CH, True, False),
+           [("VL", z), ("VH", z), "C16", "C64"], [bA + "l"], [bA])
+        for m in range(1, 16):
+            th = blk(T.TH, (m - 1) % NTH, 2 * CH)
+            ts(th, VAL[:, :], 128.0 * (m - 7.5), None, A.max, None, 2 * CH, [("VL", z), ("VH", z)],
+               [("TH", (m - 1) % NTH)], f=0.5)
+            if m % 3 == 0:
+                pairs = []
+                for i in range(m - 2, m + 1):
+                    b0 = 2 * CH * ((i - 1) % NTH)
+                    pairs += [(wide(T.Wh, 3, i), T.TH[:, b0:b0 + CH]), (wide(T.Wh, 4, i), T.TH[:, b0 + CH:b0 + 2 * CH])]
+                mm(grp(lo, pairs, CH, False, m == 15),
+                   [("TH", (i - 1) % NTH) for i in range(m - 2, m + 1)] + ["PC16", "PC64"],
+                   [bA + "l"], [bA])
+        ts(T["SN%d" % z][:, :], lo, col(CC), None, A.add, None, CH, [bA + "l", CC], [("SN", z)], [bA])
+        if t < 2:
+            N16, CT, U = T["N16%d" % z], T["CT%d" % z], CH // 16
+            ts(N16[:, :], lo, col(CC), float(V), A.add, A.min, CH, [bA + "l", CC], [("N16", z)], [bA])
+            mm(grp(pA[:, 0:U], [(wide(T.Wh, 2, i), N16[:, i:CH:16]) for i in range(16)], U),
+               [("N16", z), "Cw0"], [bA + "l"], [bA])
+            ts(CT[:, 0:U], pA[:, 0:U], float(V), None, A.is_equal, None, U, [bA + "l"], [("CT", z)], [bA])
+            tt(CT[:, 16:16 + U], CT[:, 0:U], T.VT[:, 32 * c + U * q:32 * c + U * (q + 1)], A.mult, U,
+               [("CT", z), "VT"], [("CT1", z)])
+            tt(CT[:, 32:32 + U], pA[:, 0:U], CT[:, 16:16 + U], A.add, U, [bA + "l", ("CT1", z)], [("CT2", z)], [bA])
+            cp(T["CO%d" % z][:, 0:U], CT[:, 32:32 + U], U, [("CT2", z)], [("CO", z)])
+            tt(T["GD%d" % z][:, :], T.Nw[:, 0:V].indirect(T["CO%d" % z][:, 0:U]), T.MN[:, o:o + CH], A.subtract, CH,
+               Nk() + [("CO", z), ("MN", c)], [("GD", z)], f=GAM)
+
+    def gather(t, q):
+        z, b = q % 2, (t * NCH + q) % NB
+        X = T["X%d" % b]
+        n = GP // 16
+        win, keys = (T.Lb, ["Lb", "Lbg"]) if t == 0 else (T.Lw, Lk())
+        for j in range(B // GP):
+            act(X[:, 8 + GP * j:8 + GP * (j + 1)], win[:, 0:W].indirect(T["SN%d" % z][:, n * j:n * (j + 1)]), AF.Copy,
+                GP, keys + [("SN", z)], [("X", b, i) for i in range(j * GP // SP, ((j + 1) * GP - 1) // SP + 1)], f=GAM)
+
+    def back(t, q):
+        c, z, b = t % 3, q % 2, (t * NCH + q) % NB
+        bA = "A%d" % z
+        pA, X, D, IND = T["p" + bA], T["X%d" % b], T["D%d" % b], T["G%d" % z]
+        top = pA[:, 256:256 + CH]
+        vs = slice(c + 3 * CH * q, 3 * CH * (q + 1), 3)
+        nm = 1024 // MP
+        for j in range(B // MP):
+            o = MP * j
+            M = T.pM[:, MP * (j % nm):MP * (j % nm + 1)]
+            bM = ["M0", "M1"] if nm == 1 else ["M%d" % (j % nm)]
+            kx = [("X", b, i) for i in range(max(o - 1, 0) // SP, (o + MP - 1) // SP + 1)] + [("X0", b)]
+            op("v", vcost(MP), lambda M=M, o=o: g.vector.tensor_tensor_scan(
+                M, X[:, 7 + o:7 + o + MP], T.MASK[:, :], 0.0, A.max, A.mult), kx + ["MASK"], bM, bM)
+            tt(D[:, o:o + MP], X[:, 8 + o:8 + o + MP], M, A.subtract, MP, kx + bM, [("D", b, j)], bM)
+            if t < RO - 1:
+                u = MP // 16
+                tt(pA[:, 256 + u * j:256 + u * (j + 1)], T.pM[:, MP * (j % nm) + 15:MP * (j % nm + 1):16],
+                   X[:, 8 + o + 15:8 + o + MP:16], A.max, u, kx + bM, [bA + "h"], bM + [bA])
+        dk = lambda j: [("D", b, i) for i in range(j * SP // MP, ((j + 1) * SP - 1) // MP + 1)]
+        lo, hi = T.pB[:, 0:CH], T.pB[:, 256:256 + CH]
+        u = SP // 16
+        for j in range(B // SP):
+            o = SP * j
+            act(IND[:, o:o + SP], D[:, o:o + SP], AF.Sign, SP, dk(j), [("IND", z, j)], bias=-2.0 ** -27)
+            mm(grp(T.pB[:, u * j:u * (j + 1)], [(wide(T.Wb, 0, k), IND[:, o + k:o + SP:16]) for k in range(16)], u),
+               [("IND", z, j), "Cw"], ["Bl"], ["B"])
+        F, EA, HB, SI, HQ, GD = [T["%s%d" % (k, z)][:, :] for k in ("F", "EA", "HB", "SI", "HQ", "GD")]
+        ts(F, lo, -13.0, 128.0, A.is_ge, A.mult, CH, ["Bl"], [("F", z)], ["B"])
+        mm(grp(hi, [(Wm, F)], CH), [("F", z), "Wm"], ["Bh"], ["B"])
+        tt(hi, hi, T["POW%d" % z][:, :], A.mult, CH, ["Bh", ("POW", z)], ["Bh"], ["B"])
+        ts(lo, hi, 2.0 ** 23 - 0.5, 2.0 ** 23 + 1.0, A.add, A.is_equal, CH, ["Bh"], ["Bl"], ["B"])
+        tt(EA, lo, T["A16%d" % z][:, :], A.mult, CH, ["Bl", ("A16", z)], [("EA", z)], ["B"])
+        if t < 2:
+            ts(HQ, hi, 0.5, None, A.add, None, CH, ["Bh"], [("HQ", z)], ["B"])
+        mm(grp(lo, [(S01, T.Pw[:, vs]), (S01, T.Rw[:, vs]), (I16, T.KK[:, CH:2 * CH]), (BD16, EA)], CH),
+           [("EA", z), "S01", ("P", c, q), "Rw", "I16", "K2", "BD16"], ["Bl"], ["B"])
+        if t < RO - 1:
+            if HS: act(HB, lo, AF.Identity, CH, ["Bl", ODD], [("HB", z)], ["B"], scale=col(ODD))
+            else: ts(HB, lo, col(ODD), None, A.mult, None, CH, ["Bl", ODD], [("HB", z)], ["B"])
+            tt(T.Pw[:, vs], lo, HB, A.subtract, CH, ["Bl", ("HB", z)], [("P", c, q)], ["B"])
+        if t >= 2:
+            cp(SI, lo, CH, ["Bl"], [("SI", z)], ["B"])
+        mm(grp(hi, [(I64b, F), (I64b, T.VR[:, 0:CH])], CH), [("F", z), ("K", 8), "VR"], ["Bh"], ["B"])
+        ts(T["OF%d" % b][:, :], hi, col(OCOL), None, A.add, None, CH, ["Bh", OCOL], [("OF", b)], ["B"])
+        if t >= 2:
+            ts(SI, SI, 1023, None, A.bitwise_and, None, CH, [("SI", z)], [("SI", z)])
+            (gcopy if GC and t < RO - 1 else cp)(T.YP[:, vs], SI, CH, [("SI", z)], [("YP", c, q)])
+        if t < RO - 1:
+            Lo, lk = (T.Lb[:, vs], "Lb") if t == 0 else (T.Lw[:, vs], ("L", c, q))
+            tt(top, top, Lo, A.subtract, CH, [bA + "h", lk], [bA + "h"], [bA])
+            if QS: act(top, top, AF.Copy, CH, [bA + "h"], [bA + "h"], [bA], scale=0.25)
+            else: ts(top, top, 0.25, None, A.mult, None, CH, [bA + "h"], [bA + "h"], [bA])
+            tt(top, top, Lo, A.add, CH, [bA + "h", lk], [bA + "h"], [bA])
+            tt(T.Lw[:, vs], top, T.Fd[:, vs], A.mult, CH, [bA + "h", "Fd"], [("L", c, q)], [bA])
+            if q == 0:
+                sb = T.SB[:, 2 * NG * t:2 * NG * (t + 1)]
+                mm(grp(pA[:, 0:NG], [(Shf, T.Lw[:, c:GH:3])], 4 * NG) + grp(pA[:, NG:2 * NG], [(Shb, T.Pw[:, c:GH:3])], NG),
+                   [("L", c, 0), ("P", c, 0), "Shf", "Shb"], [bA + "l"], [bA])
+                act(sb, pA[:, 0:2 * NG], AF.Copy, 2 * NG, [bA + "l"], [("SB", t)], [bA])
+                send(sb, lambda d: T.ST[:, 7 * t + d - 1, :], T.sem["ar%d" % t], [("SB", t)], [("ST", t)], 6000.0)
+
+    def rest(t, q):
+        c, z, b = t % 3, q % 2, (t * NCH + q) % NB
+        X, D, OF = T["X%d" % b], T["D%d" % b], T["OF%d" % b]
+        vs = slice(c + 3 * CH * q, 3 * CH * (q + 1), 3)
+        HQ, GD = T["HQ%d" % z][:, :], T["GD%d" % z][:, :]
+        if t < 2:
+            ts(HQ, HQ, 1, None, A.bitwise_and, None, CH, [("HQ", z)], [("HQ", z)])
+            tt(GD, GD, HQ, A.mult, CH, [("GD", z), ("HQ", z)], [("GD", z)])
+            tt(T.Nw[:, vs], T.Nw[:, vs], GD, A.add, CH, [("GD", z), ("N", c, q)], [("N", c, q)])
+            derive(t + 3, q)
+        lo = T.pE[:, 0:CH]
+        dk = lambda j: [("D", b, i) for i in range(j * SP // MP, ((j + 1) * SP - 1) // MP + 1)]
+        u = SP // 16
+        xk = [("X", b, i) for i in range(B // SP)] + [("X0", b)]
+        for j in range(B // SP):
+            o = SP * j
+            d = D[:, o:o + SP]
+            act(d, d, AF.Sigmoid, SP, dk(j), dk(j))
+            tt(d, X[:, 0:B + 8].indirect(OF[:, u * j:u * (j + 1)]), d, A.mult, SP, dk(j) + xk + [("OF", b)], dk(j), f=GAM)
+            for k0 in range(0, 16, EG):
+                mm(grp(T.pE[:, u * j:u * (j + 1)], [(If, D[:, o + k:o + SP:16]) for k in range(k0, k0 + EG)], 4 * u,
+                       k0 == 0, k0 + EG == 16), dk(j) + ["If"], ["El"], ["E"])
+        if t < 3:
+            act(T.E[:, vs], lo, AF.Copy, CH, ["El"], [("E", c, q)], ["E"])
+        else:
+            tt(T.E[:, vs], lo, T.E[:, vs], A.add, CH, ["El", ("E", c, q)], [("E", c, q)], ["E"])
+
+    for t in range(RO):
+        c = t % 3
+        for q in range(NCH): front(t, q)
+        for q in range(NCH): gather(t, q)
+        for q in range(NCH): back(t, q)
+        if t < RO - 1:
+            gcopy(T.Pw[:, V + c:W:3], T.ST[:, 7 * t:7 * t + 7, NG:2 * NG], 7 * NG, [("ST", t)], [("Pg", c)])
+            gcopy(T.Lw[:, V + c:W:3], T.ST[:, 7 * t:7 * t + 7, 0:NG], 7 * NG, [("ST", t)], [("Lg", c)])
+        for q in range(NCH): rest(t, q)
+    for q in range(NCH):
+        cs = slice(3 * CH * q, 3 * CH * (q + 1))
+        dma([(T.yp[:, cs], T.YP[0:128:16, cs])], [("YP", c, q) for c in range(3)], (), lat=2500.0)
+        dma([(T.ye[:, cs], T.E[:, cs])], [("E", c, q) for c in range(3)], (), lat=2800.0)
+    return ops, nleft[0]
+
+
+def schedule(ops):
+    n = len(ops)
+    succ = [[] for _ in range(n)]
+    for i, o in enumerate(ops):
+        for d in o["hard"]: succ[d].append((i, LAT_S if ops[d]["eng"] == o["eng"] else LAT_X))
+        for d in o["soft"]: succ[d].append((i, 0.0))
+    prio = [0.0] * n
+    for i in range(n - 1, -1, -1):
+        prio[i] = ops[i]["cost"] + ops[i]["lat"] + max([prio[j] + l for j, l in succ[i]] + [0.0])
+    left = [len(o["hard"]) + len(o["soft"]) for o in ops]
+    est = [0.0] * n
+    free = {e: 0.0 for e in "vstgyx"}
+    ready = {e: [] for e in free}
+    for i in range(n):
+        if left[i] == 0: ready[ops[i]["eng"]].append(i)
+    order, end, start = [], 0.0, [0.0] * n
+    while len(order) < n:
+        best = None
+        for e in free:
+            if ready[e]:
+                s0 = max(free[e], min(est[i] for i in ready[e]))
+                if best is None or s0 < best[0]: best = (s0, e)
+        s0, e = best
+        i = max((j for j in ready[e] if est[j] <= s0 + SLACK), key=lambda j: (prio[j], -j))
+        ready[e].remove(i)
+        s = max(free[e], est[i])
+        start[i] = s
+        free[e] = s + ops[i]["cost"]
+        fin = free[e] + ops[i]["lat"]
+        end = max(end, fin)
+        order.append(i)
+        for j, l in succ[i]:
+            est[j] = max(est[j], (fin + l) if l else free[e])
+            left[j] -= 1
+            if left[j] == 0: ready[ops[j]["eng"]].append(j)
+    return order, end, start
+
+
+def place(ops, seq, pred, back):
+    n = len(ops)
+    start, fin = [0.0] * n, [0.0] * n
+    lines = {e: [] for e in "vstgyx"}
+    for i in seq:
+        o = ops[i]
+        cost, s = o["cost"], 0.0
+        for d, l in pred[i]:
+            lat = (o["lat"] if back else ops[d]["lat"]) if l else 0.0
+            s = max(s, fin[d] + l + lat)
+        if back and not pred[i]: s = o["lat"]
+        line = lines[o["eng"]]
+        k = len(line)
+        while k > 0 and line[k - 1][1] > s: k -= 1
+        while k < len(line) and line[k][0] < s + cost:
+            s = max(s, line[k][1])
+            k += 1
+        line.insert(k, (s, s + cost))
+        start[i], fin[i] = s, s + cost
+    end = max(fin[i] + (0.0 if back else ops[i]["lat"]) for i in range(n))
+    return start, fin, end
+
+
+def refine(ops):
+    n = len(ops)
+    pred, succ = [[] for _ in range(n)], [[] for _ in range(n)]
+    for i, o in enumerate(ops):
+        for d in o["hard"] | o["soft"]:
+            l = 0.0 if d in o["soft"] else (LAT_S if ops[d]["eng"] == o["eng"] else LAT_X)
+            pred[i].append((d, l))
+            succ[d].append((i, l))
+    order, end, start = schedule(ops)
+
+    def score(order):
+        tot = 0.0
+        for k in range(len(SCEN)):
+            fin, free, last = [0.0] * n, {}, 0.0
+            for i in order:
+                o = ops[i]
+                s = free.get(o["eng"], 0.0)
+                for d, l in pred[i]:
+                    if l and fin[d] + l > s: s = fin[d] + l
+                s += o["costs"][k]
+                free[o["eng"]] = s
+                fin[i] = s + o["lat"]
+                if fin[i] > last: last = fin[i]
+            tot += last / ref[k]
+        return tot
+
+    def shaken(key, links, amp):
+        key = list(key + amp * rng.random(n))
+        for i in (range(n) if links is pred else range(n - 1, -1, -1)):
+            for d, l in links[i]:
+                if key[d] >= key[i]: key[i] = key[d] + 1e-3
+        return sorted(range(n), key=lambda i: key[i])
+
+    rng = np.random.default_rng(1)
+    ref = [sum(o["costs"][k] for o in ops if o["eng"] in "vs") for k in range(len(SCEN))]
+    best = (score(order), order, start, end)
+    for it in range(PASSES):
+        amp = 0.0
+        if it % REP == 0:
+            start = best[2]
+            t0 = (best[3] + SPAN) * rng.random() - SPAN
+            amp = AMP * rng.random() * np.array([1.0 if t0 <= s <= t0 + SPAN else 0.0 for s in start])
+        fin = np.array([start[i] + ops[i]["cost"] for i in range(n)])
+        bs, bf_, _e = place(ops, shaken(-fin, succ, amp), succ, True)
+        start, fin, end = place(ops, shaken(-np.array(bf_), pred, 0.0), pred, False)
+        order = sorted(range(n), key=lambda i: (start[i], i))
+        sc = score(order)
+        if sc < best[0]: best = (sc, order, start, end)
+    return best[1], best[3], best[2]
+
+
+SLACK = 150.0
+PASSES = 1500
+AMP = 8000.0
+REP = 1
+SPAN = 20000.0
+ORDER = {}
+
+
+def rank_program(g, core, T, topo):
+    if T.rank_of(core) is None:
+        return
+    ops, nleft = build(g, core, T, topo)
+    if not ORDER: ORDER[0] = refine(ops)[0]
+    order = ORDER[0]
+    queue = {"v": g.vector, "s": g.scalar, "t": g.tensor, "g": g, "y": g.sync}
+    csem = {"v": "cv", "s": "cs", "t": "ct", "g": "cg"}
+    need = set()
+    for o in ops: need |= o["hard"]
+    count = {e: 0 for e in csem}
+    tick = {}
+    for i in order:
+        o = ops[i]
+        if o["sem"] is None and i in need:
+            count[o["eng"]] += 1
+            tick[i] = (csem[o["eng"]], T.sem[csem[o["eng"]]], count[o["eng"]])
+        elif o["sem"] is not None and o["val"] > 0:
+            tick[i] = ("a%d" % i, o["sem"], o["val"])
+    seen = {e: {} for e in queue}
+    for i in order:
+        o = ops[i]
+        e = o["eng"]
+        if e == "x": continue
+        want = {}
+        for d in o["hard"]:
+            k, sem, v = tick[d]
+            if v > seen[e].get(k, 0) and v > want.get(k, (None, 0))[1]: want[k] = (sem, v)
+        for k in sorted(want):
+            queue[e].wait_ge(want[k][0], want[k][1])
+            seen[e][k] = want[k][1]
+        ins = o["fn"]()
+        if o["sem"] is None and i in tick: ins.then_inc(tick[i][1], 1)
+    for e in csem:
+        if count[e]: g.sync.wait_ge(T.sem[csem[e]], count[e])
+    for i in order:
+        if ops[i]["sem"] is not None and ops[i]["val"] > 0: g.sync.wait_ge(ops[i]["sem"], ops[i]["val"])
+    g.sync.wait_ge(T.sem.left, nleft)

@@ -7,18 +7,23 @@ N, V, H, GH, W, RO = 8, 1536, 512, 240, 3216, 5
 CH = 256
 NCH = H // CH
 B = 16 * CH
-NTH = 9
 NB = 2
 MP = 1024
-GP = 1024
-SP = 1024
+NP = B // MP
+U = MP // 16
 EG = 4
-HS = 1
-QS = 1
-GC = 1
 NG = GH // 3
-MAGIC = 1.5 * 2.0 ** 33
+OFF = 1.5 * 2.0 ** 17
+UNIT = [2.0 ** (6 * r - 104) for r in range(16)]
 f32, bf, f16, i32, u16 = "float32", "bfloat16", "float16", "int32", "uint16"
+
+P_ON_V = {(t, 0, j) for t in range(RO) for j in (1, 3)} | {(0, 1, 1), (0, 1, 3)}
+L_ON_V = set()
+SIGN_S = {(t, q, j) for t in range(RO) for q in range(NCH) for j in (1, 2, 3)}
+D_ON_T = set()
+FINE = {(RO - 1, 1)}
+F_ON_S = True
+E_ON_T = True
 
 SCRATCH = {
     "Lw": ("sbuf", [128, W], f32), "Lb": ("sbuf", [128, W], bf), "Pw": ("sbuf", [128, W], bf),
@@ -28,16 +33,21 @@ SCRATCH = {
     "S0L": ("sbuf", [128, GH], bf), "S0P": ("sbuf", [128, GH], bf),
     "SB": ("sbuf", [128, 4 * 2 * NG], f32), "ST": ("sbuf", [128, 4 * 7, 2 * NG], f32),
     "NM": ("sbuf", [128, 3 * H], u16), "DL": ("sbuf", [128, 3 * H], f16),
-    "LO": ("sbuf", [128, 3 * H], i32), "HI": ("sbuf", [128, 3 * H], i32), "MN": ("sbuf", [128, 2 * H], i32),
-    "NT": ("sbuf", [128, H], i32),
-    "TH": ("sbuf", [128, NTH * 2 * CH], f16), "MASK": ("sbuf", [128, MP], bf),
+    "LO": ("sbuf", [128, 3 * H], bf), "HI": ("sbuf", [128, 3 * H], bf), "MN": ("sbuf", [128, 2 * H], i32),
+    "NT": ("sbuf", [128, H], i32), "LT": ("sbuf", [128, H], i32),
+    "TH": ("sbuf", [128, 5 * 2 * CH], bf), "MASK": ("sbuf", [128, MP], bf),
     "ROW": ("sbuf", [128, 256], bf), "ROWG": ("sbuf", [128, 128], bf), "VR": ("sbuf", [128, 256], bf),
-    "IP": ("sbuf", [128, 4], i32), "IT": ("sbuf", [128, 32], i32), "C": ("sbuf", [128, 32], f32),
+    "JR": ("sbuf", [128, 128], i32),
+    "IP": ("sbuf", [128, 4], i32), "IT": ("sbuf", [128, 32], i32), "C": ("sbuf", [128, 64], f32),
     "TG": ("sbuf", [128, 16], f32), "BS": ("sbuf", [128, 16], f32), "QT": ("sbuf", [128, 16], f32),
-    "PT": ("sbuf", [128, 16], f32), "VT": ("sbuf", [128, 64], f32),
-    "Dm": ("sbuf", [128, 8 * 128], f16), "Km": ("sbuf", [128, 8 * 128], bf), "Qm": ("sbuf", [128, 16 * 136], bf),
-    "Hm": ("sbuf", [128, 3 * 128], f16), "Bm": ("sbuf", [128, 4 * 128], bf), "Fm": ("sbuf", [128, 2 * 128], f32),
-    "Wb": ("sbuf", [128, 2 * 144], bf), "Wh": ("sbuf", [128, 5 * 144], f16), "KK": ("sbuf", [128, 2 * CH], f16),
+    "PT": ("sbuf", [128, 16], f32), "PJ": ("sbuf", [128, 8], f32), "VT": ("sbuf", [128, 64], f32),
+    "Dm": ("sbuf", [128, 8 * 128], bf), "Km": ("sbuf", [128, 8 * 128], bf), "Qm": ("sbuf", [128, 16 * 136], bf),
+    "Bm": ("sbuf", [128, 6 * 128], bf), "Fm": ("sbuf", [128, 6 * 128], f32), "Pm": ("sbuf", [128, 6 * 128], bf),
+    "ZR": ("sbuf", [128, 160], bf), "WI": ("sbuf", [128, 160], bf),
+    "Wb": ("sbuf", [128, 4 * 144], bf), "KK": ("sbuf", [128, U + CH], f16),
+    "CK": ("sbuf", [128, 2 * CH], bf), "KB": ("sbuf", [128, CH], bf),
+    "SN": ("sbuf", [128, H], u16), "N16": ("sbuf", [128, H], f16), "GD": ("sbuf", [128, H], f32),
+    "CT": ("sbuf", [128, 96], f32), "CO": ("sbuf", [128, 32], u16),
     "pA0": ("psum", [128, 512], f32), "pA1": ("psum", [128, 512], f32), "pD0": ("psum", [128, 512], f32),
     "pD1": ("psum", [128, 512], f32), "pB": ("psum", [128, 512], f32), "pE": ("psum", [128, 512], f32),
     "pM": ("psum", [128, 1024], f32),
@@ -47,19 +57,18 @@ for _b in range(NB):
     SCRATCH["D%d" % _b] = ("sbuf", [128, B], f32)
     SCRATCH["OF%d" % _b] = ("sbuf", [128, CH], u16)
 for _b in range(2):
-    for _n, _c, _d in (("G", B, bf), ("SG", 8 * CH, bf), ("RR", CH, f32), ("A16", CH, f16),
-                       ("VAL", 2 * CH, f16), ("POW", CH, bf), ("SN", CH, u16), ("N16", CH, f16), ("F", CH, bf),
-                       ("EA", CH, f16), ("HB", CH, bf), ("SI", CH, i32), ("HQ", CH, i32), ("GD", CH, f32),
-                       ("CT", 64, f32), ("CO", 16, u16)):
+    for _n, _c, _d in (("G", B, bf), ("SG", 8 * CH, bf), ("RR", CH, bf), ("A16", CH, f16), ("VAL", 2 * CH, bf),
+                       ("RS", 2 * CH, f32), ("POW", CH, bf), ("F", CH, bf), ("EA", CH, f16), ("HB", CH, bf),
+                       ("HQ", CH, f32), ("TP", CH, f32)):
         SCRATCH["%s%d" % (_n, _b)] = ("sbuf", [128, _c], _d)
 NDMA = 16
 SEMAPHORES = ["cv", "cs", "ct", "cg", "left", "arL", "arP"] + ["ar%d" % _b for _b in range(4)] + \
              ["d%d" % _b for _b in range(NDMA)]
 
-CYC = 0.83 * 1.25
-PCYC = 0.42 * 1.25
+CYC = 0.83
+PCYC = 0.42
 GAM = 1.56
-VO = 25.0
+VO = 55.0
 SCEN = [(VO, GAM), (VO, 1.15), (VO, 1.95)]
 LAT_X, LAT_S = 120.0, 80.0
 
@@ -81,7 +90,6 @@ def build(g, core, T, topo):
     def op(eng, cost, fn, r=(), w=(), banks=(), sem=None, val=0, lat=0.0, after=()):
         me = len(ops)
         hard, soft = set(after), set()
-        asyn = sem is not None
         for k in r:
             if k in lastw: hard.add(lastw[k])
         for k in w:
@@ -97,8 +105,8 @@ def build(g, core, T, topo):
             lastw[k] = me
             readers[k] = []
         if not isinstance(cost, list): cost = [cost] * len(SCEN)
-        ops.append({"eng": eng, "cost": cost[0], "costs": cost, "fn": fn, "hard": hard, "soft": soft - hard, "sem": sem, "val": val, "lat": lat,
-                    "name": w[-1] if w else None})
+        ops.append({"eng": eng, "cost": cost[0], "costs": cost, "fn": fn, "hard": hard, "soft": soft - hard, "sem": sem,
+                    "val": val, "lat": lat, "name": w[-1] if w else None})
         return me
 
     def vcost(n, f=1.0):
@@ -163,9 +171,9 @@ def build(g, core, T, topo):
 
     def send(src, dst_of, sem, r, w, lat, parts=((far, fe), (near, ne))):
         trs = []
-        for cs, en in parts:
-            ids = [DstId(rid=topo.addr(c)[0], pnc=topo.addr(c)[1]) for c in cs]
-            ds = [dst_of((T.rank_of(c) - rank) % N) for c in cs]
+        for cores, en in parts:
+            ids = [DstId(rid=topo.addr(c)[0], pnc=topo.addr(c)[1]) for c in cores]
+            ds = [dst_of((T.rank_of(c) - rank) % N) for c in cores]
             trs.append(RemoteDMATransfer(dst_ids=ids, dma_engine_mask=sum(1 << e for e in en), remote_sem=sem,
                                          srcs=[src], dsts=ds))
             nleft[0] += len(en)
@@ -184,7 +192,31 @@ def build(g, core, T, topo):
         return op("x", 0.0, None, (), w, sem=sem, val=got, lat=lat, after=[s])
 
     col = lambda j: T.C[:, j:j + 1]
-    PF, PM, G16, G15, M01, NM01, M0, ODD, OCOL, CC, WC, SH, G2, PM3, T1, T2 = range(16)
+    (PF, PM, G16, G15, M01, NM01, M0, OCOL, CC, WC, SH, M1, PM3, J3, PI, I1, I2, I12, L15, P64, PIV, MG1, MG2,
+     SUB, CKC, M02, KC, KBC, HS, HBI, P2) = range(31)
+    tmp = list(range(31, 64))
+
+    def cs(out, a, s1, s2, o0, o1=None):
+        sc = lambda x: col(x[0]) if isinstance(x, tuple) else x
+        if out is None: out = tmp.pop()
+        ts(col(out), col(a), sc(s1), sc(s2), o0, o1, 1, [a] + [x[0] for x in (s1, s2) if isinstance(x, tuple)], [out])
+        return out
+
+    def ln(out, a, s, b=0.0):
+        sc = lambda x: col(x[0]) if isinstance(x, tuple) else x
+        if out is None: out = tmp.pop()
+        act(col(out), col(a), AF.Identity, 1, [a] + [x[0] for x in (s, b) if isinstance(x, tuple)], [out],
+            scale=sc(s), bias=sc(b))
+        return out
+
+    def scaled(out, a, s, n, r, w):
+        if isinstance(s, tuple): act(out, a, AF.Identity, n, r + [s[0]], w, scale=col(s[0]))
+        else: act(out, a, AF.Identity, n, r, w, scale=s)
+
+    def diag(out, c, n, base, w):
+        op("g", 170 + 2 * n * CYC, lambda: g.affine_select(out, T.ZR[:, 0:n], [[-1, n]], A.not_equal, c, base, 1),
+           ["ZR"], w)
+
     Lk = lambda: [("L", c, q) for c in range(3) for q in range(NCH)] + [("Lg", c) for c in range(3)]
     Pk = lambda: [("P", c, q) for c in range(3) for q in range(NCH)] + [("Pg", c) for c in range(3)]
     Nk = lambda: [("N", c, q) for c in range(3) for q in range(NCH)]
@@ -204,74 +236,108 @@ def build(g, core, T, topo):
     iota(T.ROWG[:, :], [[16, 8], [0, 16]], 0, 0, 128, ["ROWG"], True)
     iota(T.IT[:, 0:16], [[-1, 16]], 16, 1, 16, ["IT"], False)
     iota(T.VT[:, :], [[1, 2], [48, 32]], -V, 0, 64, ["VT"], True)
+    iota(T.JR[:, :], [[48, 8], [1, 16]], 0, 0, 128, ["JR"], False)
     ts(T.IP[:, 1:2], T.IP[:, 0:1], 15, None, A.bitwise_and, None, 1, ["IP"], ["IP1"])
     cp(col(PM), T.IP[:, 1:2], 1, ["IP1"], [PM])
     cp(col(PF), T.IP[:, 0:1], 1, ["IP"], [PF])
-    ts(col(G16), col(PF), col(PM), None, A.subtract, None, 1, [PF, PM], [G16])
-    ts(col(G2), col(G16), 2.0, None, A.add, None, 1, [G16], [G2])
-    ts(T.QT[:, :], T.ROW[:, 0:16], col(PM), col(G2), A.is_equal, A.mult, 16, ["ROW", PM, G2], ["QT"])
+    blk = lambda t, j, n=128: t[:, n * j:n * j + n]
+    ms(T.ZR[:, :], 0.0, 80, ["ZR"])
+    diag(T.WI[:, :], 1.0, 160, 16, ["Ib"])
+    Ib = T.WI[:, 16:144]
+    ln(G16, PM, -1.0, (PF,))
+    ts(T.QT[:, :], T.ROW[:, 0:16], col(PM), None, A.is_equal, None, 16, ["ROW", PM], ["QT"])
     for s in range(16):
-        ts(T.Qm[:, 136 * s:136 * s + 130], T.ROW[:, 1:131], T.QT[:, s:s + 1], None, A.is_equal, None, 130,
-           ["ROW", "QT"], [("Q", s)], f=0.5)
+        act(T.Qm[:, 136 * s:136 * s + 130], T.WI[:, 15 + s:145 + s], AF.Identity, 130, ["Ib", "QT"], [("Q", s)],
+            scale=T.QT[:, s:s + 1])
     Qhi = lambda s: T.Qm[:, 136 * s + 1:136 * s + 129]
     Qlo = lambda s: T.Qm[:, 136 * s:136 * s + 128]
-    ts(col(G15), col(G16), 15.0, None, A.add, None, 1, [G16], [G15])
-    ts(col(M01), col(PM), 2.0, None, A.is_lt, None, 1, [PM], [M01])
-    ts(col(NM01), col(PM), 2.0, -1.0, A.is_lt, A.mult, 1, [PM], [NM01])
-    ts(col(M0), col(PM), 0.0, None, A.is_equal, None, 1, [PM], [M0])
-    ts(col(ODD), col(PM), 1.0, None, A.is_equal, None, 1, [PM], [ODD])
-    ts(col(OCOL), col(PM), 8.0 - 8192.0, None, A.add, None, 1, [PM], [OCOL])
-    ts(col(PM3), col(PM), 3.0, None, A.mult, None, 1, [PM], [PM3])
-    ts(T.VT[:, :], T.VT[:, :], col(PM3), None, A.add, None, 64, ["VT", PM3], ["VT"])
-    ts(col(T1), col(PM), 1.0, 8320.0, A.add, A.mult, 1, [PM], [T1])
-    ts(col(T2), col(PM), 15.0, -1131520.0, A.is_equal, A.mult, 1, [PM], [T2])
-    ts(col(CC), col(T1), col(T2), None, A.add, None, 1, [T1, T2], [CC])
+    for k, s in ((M0, 0), (M1, 1), (M02, 2), (L15, 15)):
+        act(col(k), T.QT[:, s:s + 1], AF.Copy, 1, ["QT"], [k])
+    ln(G15, G16, 1.0, 15.0)
+    ln(M01, M0, 1.0, (M1,))
+    ln(NM01, M01, -1.0)
+    ln(OCOL, PM, 1.0, 8.0 - 8192.0)
+    ln(PM3, PM, 3.0)
+    act(T.VT[:, :], T.VT[:, :], AF.Identity, 64, ["VT", PM3], ["VT"], bias=col(PM3))
     ts(T.PT[:, :], T.ROW[:, 0:16], col(PM), 1.0, A.is_lt, A.add, 16, ["ROW", PM], ["PT"])
-    op("v", vcost(16), lambda: g.vector.tensor_reduce(col(16), T.PT[:, :], AxisListType.X, A.mult), ["PT"], [16])
-    ts(col(17), col(M0), 0.5, col(16), A.mult, A.add, 1, [M0, 16], [17])
-    ts(col(WC), col(17), 2.0 ** 23, None, A.mult, None, 1, [17], [WC])
-    ts(col(18), col(PF), 16.0, 128.0, A.is_lt, A.mult, 1, [PF], [18])
-    ts(col(SH), col(PF), -16.0, col(18), A.add, A.add, 1, [PF, 18], [SH])
+    op("v", vcost(16), lambda: g.vector.tensor_reduce(col(P2), T.PT[:, :], AxisListType.X, A.mult), ["PT"], [P2])
+    ln(WC, ln(None, M0, 0.5, (P2,)), 2.0 ** 30)
+    ln(SH, cs(None, PF, 16.0, 128.0, A.is_lt, A.mult), 1.0, (ln(None, PF, 1.0, -16.0),))
+    ln(KC, M0, 15.5 - 13072.0, 13072.0)
+    ln(KBC, M02, OFF / 64.0)
+    ln(HBI, M02, -511.5)
+    ln(HS, M1, 1.0, (M02,))
+    ts(T.IP[:, 2:3], col(PM), 1.0 / 3.0, -1.0 / 3.0, A.mult, A.add, 1, [PM], ["IP2"])
+    ts(col(J3), T.IP[:, 2:3], 3.0, None, A.mult, None, 1, ["IP2"], [J3])
+    ln(PI, J3, -1.0, (PM,))
+    cs(I1, PI, 1.0, None, A.is_equal)
+    cs(I2, PI, 2.0, None, A.is_equal)
+    ln(I12, I1, 1.0, (I2,))
+    for out, k in ((P64, 64.0), (PIV, 1.0 / 64.0)):
+        ln(out, L15, k ** 3 - 1.0, (ln(None, I2, k ** 2 - 1.0, (ln(None, I1, k - 1.0, 1.0),)),))
+    a = ln(None, L15, 2.0 ** 22, 2.0 ** 23)
+    ln(MG2, a, (P64,))
+    ln(MG1, ln(None, I12, -0.5, (a,)), (P64,))
+    ln(SUB, ln(None, I12, -64.0), (PIV,))
+    ln(CKC, ln(None, I2, 64.0, (ln(None, ln(None, J3, 1.0, 0.5), (I12,)),)), -1.0 / 64.0)
+    a = ln(None, L15, -16.0, (ln(None, ln(None, I12, -1.0, 1.0), (J3,), 1.0),))
+    ln(CC, ln(None, ln(None, J3, -64.0, 64.0 * 13.0), (I2,), (a,)), -65.0)
     ts(T.IT[:, 16:32], T.IT[:, 0:16], 15, None, A.bitwise_and, None, 16, ["IT"], ["IT1"])
     ts(T.TG[:, :], T.IT[:, 16:32], col(G16), None, A.add, None, 16, ["IT1", G16], ["TG"])
     ts(T.BS[:, :], T.ROW[:, 0:16], col(PM), 16.0, A.add, A.is_ge, 16, ["ROW", PM], ["BS"])
-    ts(T.BS[:, :], T.BS[:, :], -0.5, None, A.add, None, 16, ["BS"], ["BS"])
+    act(T.BS[:, :], T.BS[:, :], AF.Identity, 16, ["BS"], ["BS"], bias=-0.5)
     r128 = T.ROW[:, 0:128]
-    blk = lambda t, j, n=128: t[:, n * j:n * j + n]
-    I16, I64h, BD16 = blk(T.Hm, 0), blk(T.Hm, 1), blk(T.Hm, 2)
-    S01, N01, Wm, Shb = [blk(T.Bm, j) for j in range(4)]
-    If, Shf = blk(T.Fm, 0), blk(T.Fm, 1)
+    S01, N01, Wm, Shb, BD, Inq = [blk(T.Bm, j) for j in range(6)]
+    If, Shf, Iq, S2l, S2h, Inf = [blk(T.Fm, j) for j in range(6)]
     I64b = blk(T.Km, 7)
-    ts(I16, r128, col(PF), None, A.is_equal, None, 128, ["ROW", PF], ["I16"], f=0.5)
-    ts(I64h, r128, col(PF), 64.0, A.is_equal, A.mult, 128, ["ROW", PF], ["I64h"], f=0.5)
-    ts(I64b, r128, col(PF), 64.0, A.is_equal, A.mult, 128, ["ROW", PF], [("K", 8)], f=0.5)
-    ts(If, r128, col(PF), None, A.is_equal, None, 128, ["ROW", PF], ["If"])
-    ts(Shf, r128, col(SH), None, A.is_equal, None, 128, ["ROW", SH], ["Shf"])
+    for m, c, k in ((I64b, 64.0, ("K", 8)), (If, 1.0, "If"), (Inq, -0.25, "Inq"), (Iq, 0.25, "Iq"), (Inf, -1.0, "Inf")):
+        scaled(m, Ib, c, 128, ["Ib"], [k])
     ts(Shb, r128, col(SH), None, A.is_equal, None, 128, ["ROW", SH], ["Shb"], f=0.5)
-    ts(BD16, T.ROWG[:, :], col(G16), None, A.is_equal, None, 128, ["ROWG", G16], ["BD16"], f=0.5)
+    scaled(Shf, Shb, 1.0, 128, ["Shb"], ["Shf"])
+    ts(BD, T.ROWG[:, :], col(G16), None, A.is_equal, None, 128, ["ROWG", G16], ["BD"], f=0.5)
     for m, c, k in ((S01, M01, "S01"), (N01, NM01, "N01"), (Wm, WC, "Wm")):
-        ts(m, T.ROWG[:, :], col(G16), col(c), A.is_equal, A.mult, 128, ["ROWG", G16, c], [k], f=0.5)
-    for s in range(1, 9):
-        ts(blk(T.Dm, s - 1), r128, T.TG[:, s:s + 1], -64.0, A.is_equal, A.mult, 128, ["ROW", "TG"], [("Dm", s)], f=0.5)
-        tt(blk(T.Dm, s - 1), blk(T.Dm, s - 1), I64h, A.add, 128, [("Dm", s), "I64h"], [("Dm", s)])
-    for s in range(1, 8):
-        ts(blk(T.Km, s - 1), r128, T.TG[:, 16 - s:17 - s], -64.0, A.is_equal, A.mult, 128, ["ROW", "TG"], [("K", s)], f=0.5)
-        tt(blk(T.Km, s - 1), blk(T.Km, s - 1), I64b, A.add, 128, [("K", s), ("K", 8)], [("K", s)])
-    r144 = T.ROW[:, 0:144]
-    for t_, j, c, k, rd in ((T.Wb, 0, 1.0, "Cw", []), (T.Wb, 1, col(M01), "Cw01", [M01]), (T.Wh, 0, 1.0, "C16", []),
-                            (T.Wh, 1, 64.0, "C64", []), (T.Wh, 2, col(M0), "Cw0", [M0])):
-        ts(blk(t_, j, 144), r144, col(G15), c, A.is_equal, A.mult, 144, ["ROW", G15] + rd, [k], f=0.5)
-    for j, k in ((0, "C16"), (1, "C64")):
-        tt(T.Wh[:, 144 * (3 + j):144 * (3 + j) + 143], T.Wh[:, 144 * j:144 * j + 143],
-           T.Wh[:, 144 * j + 1:144 * j + 144], A.subtract, 143, [k], ["P" + k])
-    wide = lambda t_, j, k: t_[:, 144 * j + 15 - k:144 * j + 143 - k]
-    ts(T.VR[:, :], T.ROW[:, :], 0.25, None, A.mult, None, 256, ["ROW"], ["VR"], f=0.5)
-    ts(T.KK[:, 0:CH], T.ROW[:, 0:CH], 0.0, -512.5, A.mult, A.add, CH, ["ROW"], ["K1"], f=0.5)
-    ts(T.KK[:, CH:2 * CH], T.ROW[:, 0:CH], 0.0, 511.5, A.mult, A.add, CH, ["ROW"], ["K2"], f=0.5)
+        scaled(m, BD, (c,), 128, ["BD"], [k])
+    for j, (dst, k, ss) in enumerate(((T.Dm, "Dm", (1, 2, 3, 4)), (T.Dm, "Dm", (5, 6, 7, 8)),
+                                      (T.Km, "K", (1, 2, 3, 4)), (T.Km, "K", (5, 6, 7)))):
+        bank, its = "D%d" % (j % 2), []
+        for i, s in enumerate(ss):
+            u = s if k == "Dm" else 16 - s
+            ts(blk(T.TH, 4 * j + i), r128, T.TG[:, u:u + 1], -64.0, A.is_equal, A.mult, 128, ["ROW", "TG"],
+               [("sh", j, i)], f=0.5)
+            its += grp(blk(T["p" + bank], i), [(Ib, blk(T.TH, 4 * j + i)), (Ib, I64b)], 128)
+        mm(its, ["Ib", ("K", 8), ("TH", j)] + [("sh", j, i) for i in range(len(ss))], ["p" + bank], [bank])
+        n = 128 * len(ss)
+        act(dst[:, 128 * (ss[0] - 1):128 * ss[-1]], T["p" + bank][:, 0:n], AF.Copy, n, ["p" + bank], [(k, s) for s in ss],
+            [bank])
+    scaled(S2l, Ib, (PIV,), 128, ["Ib"], ["S2l"])
+    scaled(S2h, T.WI[:, 17:145], (SUB,), 128, ["Ib"], ["S2h"])
+    tt(S2l, S2l, S2h, A.add, 128, ["S2l", "S2h"], ["S2l"])
+    scaled(S2h, S2l, 64.0, 128, ["S2l"], ["S2h"])
+    ts(T.JR[:, :], T.JR[:, :], 1.0 / 3.0, -1.0 / 3.0, A.mult, A.add, 128, ["JR"], ["JR"])
+    act(T.PJ[:, :], T.ROW[:, 0:8], AF.Identity, 8, ["ROW", G16], ["PJ"], bias=col(G16))
+    for j in range(6):
+        w_ = 1.0 / UNIT[3 * min(j, 4)]
+        ts(blk(T.Pm, j), T.JR[:, :], T.PJ[:, j:j + 1], w_ if j else math.sqrt(w_), A.is_equal, A.mult, 128,
+           ["JR", "PJ"], [("Pm", j)])
+    scaled(blk(T.Pm, 0), blk(T.Pm, 0), math.sqrt(1.0 / UNIT[0]), 128, [("Pm", 0)], [("Pm", 0)])
+    tt(blk(T.Pm, 4), blk(T.Pm, 4), blk(T.Pm, 5), A.subtract, 128, [("Pm", 4), ("Pm", 5)], [("Pm", 4)])
+    ts(blk(T.Wb, 0, 144), T.ROW[:, 0:144], col(G15), None, A.is_equal, None, 144, ["ROW", G15], ["Cw"], f=0.5)
+    for j, c, k in ((1, (M01,), "Cw01"), (2, 2.0, "Cw2"), (3, (M0,), "Cw0")):
+        scaled(blk(T.Wb, j, 144), blk(T.Wb, 0, 144), c, 144, ["Cw"], [k])
+    wide = lambda j, k: T.Wb[:, 144 * j + 15 - k:144 * j + 143 - k]
+    scaled(T.VR[:, :], T.ROW[:, :], 1.0 / 512.0, 256, ["ROW"], ["VR"])
+    ts(T.KK[:, 0:U], T.ROW[:, 0:U], 0.0, col(KC), A.mult, A.add, U, ["ROW", KC], ["K1"], f=0.5)
+    ms(T.KK[:, U:U + CH], 511.5, CH // 2, ["K2"])
+    act(T.KB[:, :], T.ROW[:, 0:CH], AF.Identity, CH, ["ROW", KBC], ["KB"], scale=0.0, bias=col(KBC))
+    for j in range(2):
+        act(blk(T.CK, j, CH), T.ROW[:, 0:CH], AF.Identity, CH, ["ROW", CKC], [("CK", j)], scale=0.0, bias=col(CKC))
     ms(T.MASK[:, :], 1.0, MP // 2, ["MASK"])
     op("v", vcost(MP // 16), lambda: g.vector.memset(T.MASK[:, 0:MP:16], 0.0), ["MASK"], ["MASK"])
     for b in range(NB):
         ms(T["X%d" % b][:, 0:8], 0.0, 8, [("X0", b)])
+    if D_ON_T:
+        mm([(blk(T.pM, j, 512), Ib, T.MASK[:, 0:512], True, False, 512) for j in range(2)], ["Ib", "MASK"], ["M0", "M1"],
+           ["M0", "M1"])
 
     cp(T.Rh[:, 0:192], T.R[:, 0:192], 192, ["Rph"], ["Rh"])
     tt(T.Rl[:, 0:192], T.R[:, 0:192], T.Rh[:, 0:192], A.subtract, 192, ["Rph", "Rh"], ["Rl"])
@@ -296,29 +362,33 @@ def build(g, core, T, topo):
             mm(its, ks + [("Q", s) for s in range(4 * j, 4 * j + 4)], ["p" + bank], [bank])
             kw = [("init", o, j)] + (keys if j == 3 else [])
             kr = ["p" + bank] + ([("init", o, i) for i in range(3)] if j == 3 else [])
-            if o == 0 and j % 2 == 0:
-                act(dst[:, 384 * j:384 * j + 384], T["p" + bank][:, 0:384], AF.Copy, 384, kr, kw, [bank])
-            else:
-                cp(dst[:, 384 * j:384 * j + 384], T["p" + bank][:, 0:384], 384, kr, kw, [bank])
+            act(dst[:, 384 * j:384 * j + 384], T["p" + bank][:, 0:384], AF.Copy, 384, kr, kw, [bank])
     for c in range(2):
         gcopy(T.MN[:, H * c:H * (c + 1)], T.Nw[:, c:V:3], H, [("N", c, q) for q in range(NCH)], [("MN", c)])
     gcopy(T.Lw[:, 0:V], T.Lb[:, 0:V], V, ["Lb"], [("L", c, q) for c in range(3) for q in range(NCH)])
     gcopy(T.Lw[:, V:W], T.Lb[:, V:W], W - V, ["Lbg"], [("Lg", c) for c in range(3)])
 
-    def derive(t, q):
-        c = t % 3
-        src = T.Nw[:, c + 3 * CH * q:3 * CH * (q + 1):3]
-        sl = slice(H * c + CH * q, H * c + CH * (q + 1))
-        nt = T.NT[:, CH * q:CH * (q + 1)]
-        k = [("N", c, q)]
-        ts(nt, src, 4095, None, A.bitwise_and, None, CH, k, [("NT", q)])
-        (gcopy if GC > 1 and t else cp)(T.NM[:, sl], nt, CH, [("NT", q)], [("NM", c, q)])
-        ts(T.DL[:, sl], src, 2.0 ** -12, 1024.6, A.mult, A.add, CH, k, [("DL", c, q)])
-        ts(T.LO[:, sl], src, 63, None, A.bitwise_and, None, CH, k, [("LO", c, q)])
-        ts(T.HI[:, sl], src, 6, 63, A.logical_shift_right, A.bitwise_and, CH, k, [("HI", c, q)])
+    def derive(t, qs):
+        c, q0, n = t % 3, qs[0], CH * len(qs)
+        src = T.Nw[:, c + 3 * CH * q0:3 * (CH * q0 + n):3]
+        sl = slice(H * c + CH * q0, H * c + CH * q0 + n)
+        nt, lt = T.NT[:, CH * q0:CH * q0 + n], T.LT[:, CH * q0:CH * q0 + n]
+        k = lambda name: [(name, c, q) for q in qs]
+        kt = lambda name: [(name, q) for q in qs]
+        ts(nt, src, 4095, None, A.bitwise_and, None, n, k("N"), kt("NT"))
+        cp(T.NM[:, sl], nt, n, kt("NT"), k("NM"))
+        ts(T.DL[:, sl], src, 2.0 ** -12, 1024.6, A.mult, A.add, n, k("N"), k("DL"))
+        ts(T.HI[:, sl], T.NM[:, sl], 2.0 ** -6, 128.0 + 65.0 / 128.0, A.mult, A.add, n, k("NM"), k("HI"), f=0.5)
+        act(T.HI[:, sl], T.HI[:, sl], AF.Identity, n, k("HI"), k("HI"), bias=-128.0)
+        ts(lt, src, 63, None, A.bitwise_and, None, n, k("N"), kt("LT"))
+        gcopy(T.LO[:, sl], lt, n, kt("LT"), k("LO"))
+        act(T.LO[:, sl], T.LO[:, sl], AF.Identity, n, k("LO"), k("LO"), bias=1.0)
 
-    for t in range(3):
-        for q in range(NCH): derive(t, q)
+    for t in range(3): derive(t, list(range(NCH)))
+
+    def pick(on_v, out, win, r, w):
+        if on_v: cp(out, win, MP, r, w, f=GAM)
+        else: act(out, win, AF.Copy, MP, r, w, f=GAM)
 
     def front(t, q):
         c, z = t % 3, q % 2
@@ -326,19 +396,16 @@ def build(g, core, T, topo):
         pA = T["p" + bA]
         lo, hi = pA[:, 0:CH], pA[:, 256:256 + CH]
         o = H * c + CH * q
-        vs = slice(c + 3 * CH * q, 3 * CH * (q + 1), 3)
-        G, SG, RR, A16, VAL = T["G%d" % z], T["SG%d" % z], T["RR%d" % z], T["A16%d" % z], T["VAL%d" % z]
-        n = GP // 16
-        gk = lambda j: [("IND", z, i) for i in range(j * GP // SP, ((j + 1) * GP - 1) // SP + 1)]
-        for j in range(B // GP):
-            act(G[:, GP * j:GP * (j + 1)], T.Pw[:, 0:W].indirect(T.NM[:, o + n * j:o + n * (j + 1)]), AF.Copy, GP,
-                Pk() + [("NM", c, q)], gk(j), f=GAM)
-            pairs = [(wide(T.Wb, 1, k), G[:, GP * j + k:GP * (j + 1):16]) for k in range(16)]
-            pairs += [(I16, T.DL[:, o + n * j:o + n * (j + 1)]), (I16, T.KK[:, 0:n]),
-                      (N01, T.Pw[:, c + 3 * (CH * q + n * j):3 * (CH * q + n * (j + 1)):3])]
-            mm(grp(pA[:, n * j:n * (j + 1)], pairs, n),
-               gk(j) + ["Cw01", "I16", ("DL", c, q), "K1", "N01", ("P", c, q)], [bA + "l"], [bA])
-        ts(RR[:, :], lo, MAGIC, MAGIC, A.add, A.subtract, CH, [bA + "l"], [("RR", z)], [bA])
+        G, SG, RR, A16, VAL, RS = [T["%s%d" % (k, z)] for k in ("G", "SG", "RR", "A16", "VAL", "RS")]
+        for j in range(NP):
+            pick((t, q, j) in P_ON_V, G[:, MP * j:MP * (j + 1)], T.Pw[:, 0:W].indirect(T.NM[:, o + U * j:o + U * (j + 1)]),
+                 Pk() + [("NM", c, q)], [("IND", z, j)])
+            pairs = [(wide(1, k), G[:, MP * j + k:MP * (j + 1):16]) for k in range(16)]
+            pairs += [(Ib, T.DL[:, o + U * j:o + U * (j + 1)]), (BD, T.KK[:, 0:U]),
+                      (N01, T.Pw[:, c + 3 * (CH * q + U * j):3 * (CH * q + U * (j + 1)):3])]
+            mm(grp(pA[:, U * j:U * (j + 1)], pairs, U),
+               [("IND", z, j), "Cw01", "Ib", "BD", ("DL", c, q), "K1", "N01", ("P", c, q)], [bA + "l"], [bA])
+        act(RR[:, :], lo, AF.Copy, CH, [bA + "l"], [("RR", z)], [bA])
         tt(A16[:, :], lo, RR[:, :], A.subtract, CH, [bA + "l", ("RR", z)], [("A16", z)], [bA])
         per = 512 // CH
         for j in range(8 // per):
@@ -355,101 +422,123 @@ def build(g, core, T, topo):
             ss = range(4 * j + 1, 4 * j + 5)
             mm(grp(hi, [(blk(T.Km, s - 1), blk(SG, s - 1, CH)) for s in ss], CH, j == 0, j == 1),
                [("SG", z, s) for s in ss] + [("K", s) for s in ss], [bA + "h"], [bA])
-        tt(VAL[:, 0:CH], hi, T.LO[:, o:o + CH], A.add, CH, [bA + "h", ("LO", c, q)], [("VL", z)], [bA])
-        tt(VAL[:, CH:2 * CH], hi, T.HI[:, o:o + CH], A.add, CH, [bA + "h", ("HI", c, q)], [("VH", z)], [bA])
+        act(lo, hi, AF.Sigmoid, CH, [bA + "h"], [bA + "l"], [bA],
+            bias=-59.0 * math.log(2.0), scale=6.0 * math.log(2.0) / 128.0)
         act(T["POW%d" % z][:, :], hi, AF.Sigmoid, CH, [bA + "h"], [("POW", z)], [bA],
             bias=-37.5 * math.log(2.0), scale=-math.log(2.0) / 128.0)
-        mm(grp(lo, [(wide(T.Wh, 0, 0), VAL[:, 0:CH]), (wide(T.Wh, 1, 0), VAL[:, CH:2 * CH])], CH, True, False),
-           [("VL", z), ("VH", z), "C16", "C64"], [bA + "l"], [bA])
-        for m in range(1, 16):
-            th = blk(T.TH, (m - 1) % NTH, 2 * CH)
-            ts(th, VAL[:, :], 128.0 * (m - 7.5), None, A.max, None, 2 * CH, [("VL", z), ("VH", z)],
-               [("TH", (m - 1) % NTH)], f=0.5)
-            if m % 3 == 0:
-                pairs = []
-                for i in range(m - 2, m + 1):
-                    b0 = 2 * CH * ((i - 1) % NTH)
-                    pairs += [(wide(T.Wh, 3, i), T.TH[:, b0:b0 + CH]), (wide(T.Wh, 4, i), T.TH[:, b0 + CH:b0 + 2 * CH])]
-                mm(grp(lo, pairs, CH, False, m == 15),
-                   [("TH", (i - 1) % NTH) for i in range(m - 2, m + 1)] + ["PC16", "PC64"],
-                   [bA + "l"], [bA])
-        ts(T["SN%d" % z][:, :], lo, col(CC), None, A.add, None, CH, [bA + "l", CC], [("SN", z)], [bA])
-        if t < 2:
-            N16, CT, U = T["N16%d" % z], T["CT%d" % z], CH // 16
-            ts(N16[:, :], lo, col(CC), float(V), A.add, A.min, CH, [bA + "l", CC], [("N16", z)], [bA])
-            mm(grp(pA[:, 0:U], [(wide(T.Wh, 2, i), N16[:, i:CH:16]) for i in range(16)], U),
-               [("N16", z), "Cw0"], [bA + "l"], [bA])
-            ts(CT[:, 0:U], pA[:, 0:U], float(V), None, A.is_equal, None, U, [bA + "l"], [("CT", z)], [bA])
-            tt(CT[:, 16:16 + U], CT[:, 0:U], T.VT[:, 32 * c + U * q:32 * c + U * (q + 1)], A.mult, U,
-               [("CT", z), "VT"], [("CT1", z)])
-            tt(CT[:, 32:32 + U], pA[:, 0:U], CT[:, 16:16 + U], A.add, U, [bA + "l", ("CT1", z)], [("CT2", z)], [bA])
-            cp(T["CO%d" % z][:, 0:U], CT[:, 32:32 + U], U, [("CT2", z)], [("CO", z)])
-            tt(T["GD%d" % z][:, :], T.Nw[:, 0:V].indirect(T["CO%d" % z][:, 0:U]), T.MN[:, o:o + CH], A.subtract, CH,
-               Nk() + [("CO", z), ("MN", c)], [("GD", z)], f=GAM)
+        tt(VAL[:, 0:CH], lo, T.LO[:, o:o + CH], A.mult, CH, [bA + "l", ("LO", c, q)], [("VL", z)], [bA])
+        tt(VAL[:, CH:2 * CH], lo, T.HI[:, o:o + CH], A.mult, CH, [bA + "l", ("HI", c, q)], [("VH", z)], [bA])
+        bank = "D%d" % z
+        pS = T["p" + bank][:, :]
+        mm(grp(pS, [(I64b, T.CK[:, :]), (blk(T.Pm, 5), VAL[:, :])], 2 * CH, True, False),
+           [("VL", z), ("VH", z), ("K", 8), ("CK", 0), ("CK", 1), ("Pm", 5)], ["p" + bank], [bank])
+        for j in range(5):
+            th = blk(T.TH, j, 2 * CH)
+            ts(th, VAL[:, :], UNIT[3 * j], UNIT[3 * j + 3], A.max, A.min, 2 * CH, [("VL", z), ("VH", z)], [("TH", j)], f=0.5)
+            mm(grp(pS, [(blk(T.Pm, j), th)], 2 * CH, False, j == 4), [("TH", j), ("Pm", j)], ["p" + bank], [bank])
+        ts(RS[:, :], pS, col(MG1), col(MG2), A.add, A.subtract, 2 * CH, ["p" + bank, MG1, MG2], [("RS", z)], [bank])
+        mm(grp(lo, [(S2h, RS[:, CH:2 * CH]), (S2l, RS[:, 0:CH])], 4 * CH), [("RS", z), "S2l", "S2h"], [bA + "l"], [bA])
+        ts(T.SN[:, CH * q:CH * (q + 1)], lo, col(CC), None, A.add, None, CH, [bA + "l", CC], [("SN", q)], [bA])
+
+    def first(t):
+        c, n = t % 3, H // 16
+        ts(T.N16[:, :], T.SN[:, :], float(V), None, A.min, None, H, [("SN", q) for q in range(NCH)], ["N16"], f=0.5)
+        p = T.pD0[:, 0:n]
+        mm(grp(p, [(wide(3, i), T.N16[:, i:H:16]) for i in range(16)], n), ["N16", "Cw0"], ["pD0"], ["D0"])
+        ts(T.CT[:, 0:n], p, float(V), None, A.is_equal, None, n, ["pD0"], ["CT"], ["D0"])
+        tt(T.CT[:, n:2 * n], T.CT[:, 0:n], T.VT[:, n * c:n * (c + 1)], A.mult, n, ["CT", "VT"], ["CT1"])
+        tt(T.CT[:, 2 * n:3 * n], p, T.CT[:, n:2 * n], A.add, n, ["pD0", "CT1"], ["CT2"], ["D0"])
+        cp(T.CO[:, :], T.CT[:, 2 * n:3 * n], n, ["CT2"], ["CO"])
+        tt(T.GD[:, :], T.Nw[:, 0:V].indirect(T.CO[:, :]), T.MN[:, H * c:H * (c + 1)], A.subtract, H,
+           Nk() + ["CO", ("MN", c)], [("GD", q) for q in range(NCH)], f=GAM)
 
     def gather(t, q):
-        z, b = q % 2, (t * NCH + q) % NB
+        b = (t * NCH + q) % NB
         X = T["X%d" % b]
-        n = GP // 16
         win, keys = (T.Lb, ["Lb", "Lbg"]) if t == 0 else (T.Lw, Lk())
-        for j in range(B // GP):
-            act(X[:, 8 + GP * j:8 + GP * (j + 1)], win[:, 0:W].indirect(T["SN%d" % z][:, n * j:n * (j + 1)]), AF.Copy,
-                GP, keys + [("SN", z)], [("X", b, i) for i in range(j * GP // SP, ((j + 1) * GP - 1) // SP + 1)], f=GAM)
+        for j in range(NP):
+            pick((t, q, j) in L_ON_V, X[:, 8 + MP * j:8 + MP * (j + 1)],
+                 win[:, 0:W].indirect(T.SN[:, CH * q + U * j:CH * q + U * (j + 1)]), keys + [("SN", q)], [("X", b, j)])
 
     def back(t, q):
         c, z, b = t % 3, q % 2, (t * NCH + q) % NB
         bA = "A%d" % z
         pA, X, D, IND = T["p" + bA], T["X%d" % b], T["D%d" % b], T["G%d" % z]
-        top = pA[:, 256:256 + CH]
+        top, TP = pA[:, 256:256 + CH], T["TP%d" % z]
         vs = slice(c + 3 * CH * q, 3 * CH * (q + 1), 3)
-        nm = 1024 // MP
-        for j in range(B // MP):
-            o = MP * j
-            M = T.pM[:, MP * (j % nm):MP * (j % nm + 1)]
-            bM = ["M0", "M1"] if nm == 1 else ["M%d" % (j % nm)]
-            kx = [("X", b, i) for i in range(max(o - 1, 0) // SP, (o + MP - 1) // SP + 1)] + [("X0", b)]
-            op("v", vcost(MP), lambda M=M, o=o: g.vector.tensor_tensor_scan(
-                M, X[:, 7 + o:7 + o + MP], T.MASK[:, :], 0.0, A.max, A.mult), kx + ["MASK"], bM, bM)
-            tt(D[:, o:o + MP], X[:, 8 + o:8 + o + MP], M, A.subtract, MP, kx + bM, [("D", b, j)], bM)
-            if t < RO - 1:
-                u = MP // 16
-                tt(pA[:, 256 + u * j:256 + u * (j + 1)], T.pM[:, MP * (j % nm) + 15:MP * (j % nm + 1):16],
-                   X[:, 8 + o + 15:8 + o + MP:16], A.max, u, kx + bM, [bA + "h"], bM + [bA])
-        dk = lambda j: [("D", b, i) for i in range(j * SP // MP, ((j + 1) * SP - 1) // MP + 1)]
+        bM = ["M0", "M1"]
         lo, hi = T.pB[:, 0:CH], T.pB[:, 256:256 + CH]
-        u = SP // 16
-        for j in range(B // SP):
-            o = SP * j
-            act(IND[:, o:o + SP], D[:, o:o + SP], AF.Sign, SP, dk(j), [("IND", z, j)], bias=-2.0 ** -27)
-            mm(grp(T.pB[:, u * j:u * (j + 1)], [(wide(T.Wb, 0, k), IND[:, o + k:o + SP:16]) for k in range(16)], u),
-               [("IND", z, j), "Cw"], ["Bl"], ["B"])
-        F, EA, HB, SI, HQ, GD = [T["%s%d" % (k, z)][:, :] for k in ("F", "EA", "HB", "SI", "HQ", "GD")]
-        ts(F, lo, -13.0, 128.0, A.is_ge, A.mult, CH, ["Bl"], [("F", z)], ["B"])
-        mm(grp(hi, [(Wm, F)], CH), [("F", z), "Wm"], ["Bh"], ["B"])
+        F, OF = T["F%d" % z], T["OF%d" % b]
+
+        def mask(js):
+            sl = slice(U * js[0], U * (js[-1] + 1))
+            n, kf = U * len(js), [("F", z, j) for j in js]
+            if F_ON_S: act(F[:, sl], T.pB[:, sl], AF.Sigmoid, n, ["Bl"], kf, ["B"], bias=1300.0, scale=100.0)
+            else: ts(F[:, sl], T.pB[:, sl], -13.0, None, A.is_ge, None, n, ["Bl"], kf, ["B"])
+            mm(grp(pA[:, sl], [(I64b, F[:, sl]), (I64b, T.VR[:, sl])], n), kf + [("K", 8), "VR"], [bA + "l"], [bA])
+            ts(OF[:, sl], pA[:, sl], 128.0, col(OCOL), A.mult, A.add, n, [bA + "l", OCOL], [("OF", b, j) for j in js], [bA])
+
+        for j in range(NP):
+            o = MP * j
+            M = T.pM[:, :]
+            kx = [("X", b, i) for i in range(max(j - 1, 0), j + 1)] + [("X0", b)]
+            op("v", vcost(MP), lambda o=o: g.vector.tensor_tensor_scan(
+                M, X[:, 7 + o:7 + o + MP], T.MASK[:, :], 0.0, A.max, A.mult), kx + ["MASK"], bM, bM)
+            if (t, q, j) not in D_ON_T:
+                tt(D[:, o:o + MP], X[:, 8 + o:8 + o + MP], M, A.subtract, MP, kx + bM, [("D", b, j)], bM)
+            if t < 3:
+                tt(TP[:, U * j:U * (j + 1)], T.pM[:, 15:MP:16], X[:, 8 + o + 15:8 + o + MP:16], A.max, U, kx + bM,
+                   [("TP", z)], bM)
+            elif t < RO - 1:
+                tt(pA[:, 256 + U * j:256 + U * (j + 1)], T.pM[:, 15:MP:16], X[:, 8 + o + 15:8 + o + MP:16], A.max, U,
+                   kx + bM, [bA + "h"], bM + [bA])
+            ind = IND[:, o:o + MP]
+            wk = 0
+            if (t, q, j) in D_ON_T:
+                for i in range(2):
+                    mm([(blk(T.pM, i, 512), Inf, X[:, 8 + o + 512 * i:8 + o + 512 * (i + 1)], False, False, 2048)],
+                       kx + ["Inf", bM[i]], [bM[i]], [bM[i]])
+                act(ind, M, AF.Sign, MP, bM, [("IND", z, j)], bM, bias=-2.0 ** -27, scale=-1.0)
+                act(D[:, o:o + MP], M, AF.Sigmoid, MP, bM, [("D", b, j)], bM, scale=-1.0)
+            elif (t, q, j) in SIGN_S:
+                act(ind, D[:, o:o + MP], AF.Sign, MP, [("D", b, j)], [("IND", z, j)], bias=-2.0 ** -27)
+            else:
+                gcopy(ind, D[:, o:o + MP], MP, [("D", b, j)], [("IND", z, j)])
+                ts(ind, ind, 0.0, 0.5, A.is_gt, A.subtract, MP, [("IND", z, j)], [("IND", z, j)], f=0.5)
+                wk = 2
+            mm(grp(T.pB[:, U * j:U * (j + 1)], [(wide(wk, k), IND[:, o + k:o + MP:16]) for k in range(16)], U),
+               [("IND", z, j), "Cw", "Cw2"], ["Bl"], ["B"])
+            if (t, q) in FINE: mask([j])
+        if (t, q) not in FINE: mask(list(range(NP)))
+        EA, HB, HQ = [T["%s%d" % (k, z)][:, :] for k in ("EA", "HB", "HQ")]
+        mm(grp(hi, [(Wm, F[:, :])], CH), [("F", z, j) for j in range(NP)] + ["Wm"], ["Bh"], ["B"])
         tt(hi, hi, T["POW%d" % z][:, :], A.mult, CH, ["Bh", ("POW", z)], ["Bh"], ["B"])
         ts(lo, hi, 2.0 ** 23 - 0.5, 2.0 ** 23 + 1.0, A.add, A.is_equal, CH, ["Bh"], ["Bl"], ["B"])
         tt(EA, lo, T["A16%d" % z][:, :], A.mult, CH, ["Bl", ("A16", z)], [("EA", z)], ["B"])
-        if t < 2:
-            ts(HQ, hi, 0.5, None, A.add, None, CH, ["Bh"], [("HQ", z)], ["B"])
-        mm(grp(lo, [(S01, T.Pw[:, vs]), (S01, T.Rw[:, vs]), (I16, T.KK[:, CH:2 * CH]), (BD16, EA)], CH),
-           [("EA", z), "S01", ("P", c, q), "Rw", "I16", "K2", "BD16"], ["Bl"], ["B"])
+        pairs = [(S01, T.Pw[:, vs]), (S01, T.Rw[:, vs]), (Ib, T.KK[:, U:U + CH])] + ([(I64b, T.KB[:, :])] if t >= 2 else [])
+        mm(grp(lo, pairs + [(BD, EA)], CH),
+           [("EA", z), "S01", ("P", c, q), "Rw", "Ib", "K2", "BD", "KB", ("K", 8)], ["Bl"], ["B"])
+        act(HB, lo, AF.Identity, CH, ["Bl", HS, HBI], [("HB", z)], ["B"], scale=col(HS), bias=col(HBI))
         if t < RO - 1:
-            if HS: act(HB, lo, AF.Identity, CH, ["Bl", ODD], [("HB", z)], ["B"], scale=col(ODD))
-            else: ts(HB, lo, col(ODD), None, A.mult, None, CH, ["Bl", ODD], [("HB", z)], ["B"])
             tt(T.Pw[:, vs], lo, HB, A.subtract, CH, ["Bl", ("HB", z)], [("P", c, q)], ["B"])
         if t >= 2:
-            cp(SI, lo, CH, ["Bl"], [("SI", z)], ["B"])
-        mm(grp(hi, [(I64b, F), (I64b, T.VR[:, 0:CH])], CH), [("F", z), ("K", 8), "VR"], ["Bh"], ["B"])
-        ts(T["OF%d" % b][:, :], hi, col(OCOL), None, A.add, None, CH, ["Bh", OCOL], [("OF", b)], ["B"])
-        if t >= 2:
-            ts(SI, SI, 1023, None, A.bitwise_and, None, CH, [("SI", z)], [("SI", z)])
-            (gcopy if GC and t < RO - 1 else cp)(T.YP[:, vs], SI, CH, [("SI", z)], [("YP", c, q)])
+            tt(T.YP[:, vs], lo, HB, A.subtract, CH, ["Bl", ("HB", z)], [("YP", c, q)], ["B"])
+        if t < 2:
+            hid, GD = T.pE[:, 256:256 + CH], T.GD[:, CH * q:CH * (q + 1)]
+            ts(HQ, hi, 1.5 * 2.0 ** 24, 1.5 * 2.0 ** 24, A.add, A.subtract, CH, ["Bh"], [("HQ", z)], ["B"])
+            tt(hid, hi, HQ, A.is_gt, CH, ["Bh", ("HQ", z)], ["Eh"], ["B", "E"])
+            tt(hid, hid, GD, A.mult, CH, ["Eh", ("GD", q)], ["Eh"], ["E"])
+            tt(T.Nw[:, vs], hid, T.Nw[:, vs], A.add, CH, ["Eh", ("N", c, q)], [("N", c, q)], ["E"])
         if t < RO - 1:
-            Lo, lk = (T.Lb[:, vs], "Lb") if t == 0 else (T.Lw[:, vs], ("L", c, q))
-            tt(top, top, Lo, A.subtract, CH, [bA + "h", lk], [bA + "h"], [bA])
-            if QS: act(top, top, AF.Copy, CH, [bA + "h"], [bA + "h"], [bA], scale=0.25)
-            else: ts(top, top, 0.25, None, A.mult, None, CH, [bA + "h"], [bA + "h"], [bA])
-            tt(top, top, Lo, A.add, CH, [bA + "h", lk], [bA + "h"], [bA])
+            if t < 3:
+                Lo = T.Lb[:, vs]
+                mm(grp(top, [(Iq, TP[:, :])], 4 * CH, True, False) + grp(top, [(Inq, Lo), (Ib, Lo)], CH, False, True),
+                   [("TP", z), "Lb", "Iq", "Inq", "Ib"], [bA + "h"], [bA])
+            else:
+                Lo, lk = T.Lw[:, vs], ("L", c, q)
+                tt(top, top, Lo, A.subtract, CH, [bA + "h", lk], [bA + "h"], [bA])
+                act(top, top, AF.Copy, CH, [bA + "h"], [bA + "h"], [bA], scale=0.25)
+                tt(top, top, Lo, A.add, CH, [bA + "h", lk], [bA + "h"], [bA])
             tt(T.Lw[:, vs], top, T.Fd[:, vs], A.mult, CH, [bA + "h", "Fd"], [("L", c, q)], [bA])
             if q == 0:
                 sb = T.SB[:, 2 * NG * t:2 * NG * (t + 1)]
@@ -459,28 +548,26 @@ def build(g, core, T, topo):
                 send(sb, lambda d: T.ST[:, 7 * t + d - 1, :], T.sem["ar%d" % t], [("SB", t)], [("ST", t)], 6000.0)
 
     def rest(t, q):
-        c, z, b = t % 3, q % 2, (t * NCH + q) % NB
+        c, b = t % 3, (t * NCH + q) % NB
         X, D, OF = T["X%d" % b], T["D%d" % b], T["OF%d" % b]
         vs = slice(c + 3 * CH * q, 3 * CH * (q + 1), 3)
-        HQ, GD = T["HQ%d" % z][:, :], T["GD%d" % z][:, :]
-        if t < 2:
-            ts(HQ, HQ, 1, None, A.bitwise_and, None, CH, [("HQ", z)], [("HQ", z)])
-            tt(GD, GD, HQ, A.mult, CH, [("GD", z), ("HQ", z)], [("GD", z)])
-            tt(T.Nw[:, vs], T.Nw[:, vs], GD, A.add, CH, [("GD", z), ("N", c, q)], [("N", c, q)])
-            derive(t + 3, q)
+        if t < 2: derive(t + 3, [q])
         lo = T.pE[:, 0:CH]
-        dk = lambda j: [("D", b, i) for i in range(j * SP // MP, ((j + 1) * SP - 1) // MP + 1)]
-        u = SP // 16
-        xk = [("X", b, i) for i in range(B // SP)] + [("X0", b)]
-        for j in range(B // SP):
-            o = SP * j
-            d = D[:, o:o + SP]
-            act(d, d, AF.Sigmoid, SP, dk(j), dk(j))
-            tt(d, X[:, 0:B + 8].indirect(OF[:, u * j:u * (j + 1)]), d, A.mult, SP, dk(j) + xk + [("OF", b)], dk(j), f=GAM)
+        xk = [("X", b, i) for i in range(NP)] + [("X0", b)]
+        old = t >= 3 and E_ON_T
+        for j in range(NP):
+            o, dk = MP * j, [("D", b, j)]
+            d, p = D[:, o:o + MP], T.pE[:, U * j:U * (j + 1)]
+            if (t, q, j) not in D_ON_T: act(d, d, AF.Sigmoid, MP, dk, dk)
+            win, wk = (X[:, 0:8 + o + MP], xk[:j + 1] + xk[-1:])
+            tt(d, win.indirect(OF[:, U * j:U * (j + 1)]), d, A.mult, MP, dk + wk + [("OF", b, j)], dk, f=GAM)
+            if old:
+                e = T.E[:, c + 3 * (CH * q + U * j):3 * (CH * q + U * (j + 1)):3]
+                mm(grp(p, [(If, e)], 4 * U, True, False), [("E", c, q), "If"], ["El"], ["E"])
             for k0 in range(0, 16, EG):
-                mm(grp(T.pE[:, u * j:u * (j + 1)], [(If, D[:, o + k:o + SP:16]) for k in range(k0, k0 + EG)], 4 * u,
-                       k0 == 0, k0 + EG == 16), dk(j) + ["If"], ["El"], ["E"])
-        if t < 3:
+                mm(grp(p, [(If, D[:, o + k:o + MP:16]) for k in range(k0, k0 + EG)], 4 * U,
+                       k0 == 0 and not old, k0 + EG == 16), dk + ["If"], ["El"], ["E"])
+        if t < 3 or old:
             act(T.E[:, vs], lo, AF.Copy, CH, ["El"], [("E", c, q)], ["E"])
         else:
             tt(T.E[:, vs], lo, T.E[:, vs], A.add, CH, ["El", ("E", c, q)], [("E", c, q)], ["E"])
@@ -488,16 +575,18 @@ def build(g, core, T, topo):
     for t in range(RO):
         c = t % 3
         for q in range(NCH): front(t, q)
+        if t < 2: first(t)
         for q in range(NCH): gather(t, q)
-        for q in range(NCH): back(t, q)
+        for q in range(NCH):
+            back(t, q)
+            rest(t, q)
         if t < RO - 1:
             gcopy(T.Pw[:, V + c:W:3], T.ST[:, 7 * t:7 * t + 7, NG:2 * NG], 7 * NG, [("ST", t)], [("Pg", c)])
             gcopy(T.Lw[:, V + c:W:3], T.ST[:, 7 * t:7 * t + 7, 0:NG], 7 * NG, [("ST", t)], [("Lg", c)])
-        for q in range(NCH): rest(t, q)
     for q in range(NCH):
-        cs = slice(3 * CH * q, 3 * CH * (q + 1))
-        dma([(T.yp[:, cs], T.YP[0:128:16, cs])], [("YP", c, q) for c in range(3)], (), lat=2500.0)
-        dma([(T.ye[:, cs], T.E[:, cs])], [("E", c, q) for c in range(3)], (), lat=2800.0)
+        sl = slice(3 * CH * q, 3 * CH * (q + 1))
+        dma([(T.yp[:, sl], T.YP[2:128:16, sl])], [("YP", c, q) for c in range(3)], (), lat=2500.0)
+        dma([(T.ye[:, sl], T.E[:, sl])], [("E", c, q) for c in range(3)], (), lat=2800.0)
     return ops, nleft[0]
 
 
@@ -599,11 +688,9 @@ def refine(ops):
     ref = [sum(o["costs"][k] for o in ops if o["eng"] in "vs") for k in range(len(SCEN))]
     best = (score(order), order, start, end)
     for it in range(PASSES):
-        amp = 0.0
-        if it % REP == 0:
-            start = best[2]
-            t0 = (best[3] + SPAN) * rng.random() - SPAN
-            amp = AMP * rng.random() * np.array([1.0 if t0 <= s <= t0 + SPAN else 0.0 for s in start])
+        start = best[2]
+        t0 = (best[3] + SPAN) * rng.random() - SPAN
+        amp = AMP * rng.random() * np.array([1.0 if t0 <= s <= t0 + SPAN else 0.0 for s in start])
         fin = np.array([start[i] + ops[i]["cost"] for i in range(n)])
         bs, bf_, _e = place(ops, shaken(-fin, succ, amp), succ, True)
         start, fin, end = place(ops, shaken(-np.array(bf_), pred, 0.0), pred, False)
@@ -616,7 +703,6 @@ def refine(ops):
 SLACK = 150.0
 PASSES = 1500
 AMP = 8000.0
-REP = 1
 SPAN = 20000.0
 ORDER = {}
 

@@ -4,26 +4,31 @@ from concourse.bass import DstId, RemoteDMATransfer
 from concourse.mybir import AluOpType as A, AxisListType, ActivationFunctionType as AF
 
 N, V, H, GH, W, RO = 8, 1536, 512, 240, 3216, 5
+U = 64
+MP = 16 * U
+NP = H // U
+XS = MP + 16
 CH = 256
-NCH = H // CH
-B = 16 * CH
-NB = 2
-MP = 1024
-NP = B // MP
-U = MP // 16
 EG = 4
 NG = GH // 3
 OFF = 1.5 * 2.0 ** 17
 UNIT = [2.0 ** (6 * r - 104) for r in range(16)]
 f32, bf, f16, i32, u16 = "float32", "bfloat16", "float16", "int32", "uint16"
 
-P_ON_V = {(t, 0, j) for t in range(RO) for j in (1, 3)} | {(0, 1, 1), (0, 1, 3)}
-L_ON_V = set()
-SIGN_S = {(t, q, j) for t in range(RO) for q in range(NCH) for j in (1, 2, 3)}
-D_ON_T = set()
+FRONTS = [(4, 4)] * RO
+BACKS = [(2, 2, 4)] * (RO - 1) + [(4, 4)]
+BANK = [(0, 0, 1)] * (RO - 1) + [(0, 1)]
+RESTS = [(4, 4)] * RO
+P_ON_V = {(t, j) for t in range(RO) for j in (1, 3)} | {(0, 5), (0, 7)}
+L_ON_V = {(0, j) for j in (1, 3, 5, 7)}
+SIGN_S = {(t, j) for t in range(RO) for j in range(NP) if j % 4 or t in (0, RO - 1)}
+D_ON_T = True
+SPLIT = {(t, j) for t in range(RO) for j in range(0, NP, 2)} - {(RO - 1, 4), (RO - 1, 6)}
+LAT_A = 4000.0
+M_IN_D = {(t, j) for t in range(RO) for j in (4, 6)} | {(0, 2)}
+B_IN_D = set()
 FINE = {(RO - 1, 1)}
 F_ON_S = True
-E_ON_T = True
 
 SCRATCH = {
     "Lw": ("sbuf", [128, W], f32), "Lb": ("sbuf", [128, W], bf), "Pw": ("sbuf", [128, W], bf),
@@ -31,46 +36,42 @@ SCRATCH = {
     "E": ("sbuf", [128, V], f32), "YP": ("sbuf", [128, V], f32),
     "R": ("sbuf", [128, 288], i32), "Rh": ("sbuf", [128, 288], bf), "Rl": ("sbuf", [128, 288], bf),
     "S0L": ("sbuf", [128, GH], bf), "S0P": ("sbuf", [128, GH], bf),
-    "SB": ("sbuf", [128, 4 * 2 * NG], f32), "ST": ("sbuf", [128, 4 * 7, 2 * NG], f32),
+    "SB": ("sbuf", [128, 4 * 2 * NG], f32), "ST": ("sbuf", [128, 2 * 7, 2 * NG], f32), "LN": ("sbuf", [128, CH], f32),
     "NM": ("sbuf", [128, 3 * H], u16), "DL": ("sbuf", [128, 3 * H], f16),
     "LO": ("sbuf", [128, 3 * H], bf), "HI": ("sbuf", [128, 3 * H], bf), "MN": ("sbuf", [128, 2 * H], i32),
     "NT": ("sbuf", [128, H], i32), "LT": ("sbuf", [128, H], i32),
     "TH": ("sbuf", [128, 5 * 2 * CH], bf), "MASK": ("sbuf", [128, MP], bf),
-    "ROW": ("sbuf", [128, 256], bf), "ROWG": ("sbuf", [128, 128], bf), "VR": ("sbuf", [128, 256], bf),
-    "JR": ("sbuf", [128, 128], i32),
+    "ROW": ("sbuf", [128, 256], bf), "ROWG": ("sbuf", [128, 128], bf), "VR": ("sbuf", [128, CH], bf),
+    "JR": ("sbuf", [128, 128], i32), "HQ": ("sbuf", [128, CH], f32),
     "IP": ("sbuf", [128, 4], i32), "IT": ("sbuf", [128, 32], i32), "C": ("sbuf", [128, 64], f32),
     "TG": ("sbuf", [128, 16], f32), "BS": ("sbuf", [128, 16], f32), "QT": ("sbuf", [128, 16], f32),
     "PT": ("sbuf", [128, 16], f32), "PJ": ("sbuf", [128, 8], f32), "VT": ("sbuf", [128, 64], f32),
-    "Dm": ("sbuf", [128, 8 * 128], bf), "Km": ("sbuf", [128, 8 * 128], bf), "Qm": ("sbuf", [128, 16 * 136], bf),
-    "Bm": ("sbuf", [128, 6 * 128], bf), "Fm": ("sbuf", [128, 6 * 128], f32), "Pm": ("sbuf", [128, 6 * 128], bf),
+    "Dm": ("sbuf", [128, 8 * 128], bf), "Km": ("sbuf", [128, 8 * 128], bf), "Xb": ("sbuf", [128, NP * XS], bf),
+    "Bm": ("sbuf", [128, 8 * 128], bf), "Fm": ("sbuf", [128, 5 * 128], f32), "Pm": ("sbuf", [128, 6 * 128], bf),
     "ZR": ("sbuf", [128, 160], bf), "WI": ("sbuf", [128, 160], bf),
     "Wb": ("sbuf", [128, 4 * 144], bf), "KK": ("sbuf", [128, U + CH], f16),
     "CK": ("sbuf", [128, 2 * CH], bf), "KB": ("sbuf", [128, CH], bf),
-    "SN": ("sbuf", [128, H], u16), "N16": ("sbuf", [128, H], f16), "GD": ("sbuf", [128, H], f32),
-    "CT": ("sbuf", [128, 96], f32), "CO": ("sbuf", [128, 32], u16),
-    "pA0": ("psum", [128, 512], f32), "pA1": ("psum", [128, 512], f32), "pD0": ("psum", [128, 512], f32),
-    "pD1": ("psum", [128, 512], f32), "pB": ("psum", [128, 512], f32), "pE": ("psum", [128, 512], f32),
-    "pM": ("psum", [128, 1024], f32),
+    "GD": ("sbuf", [128, H], f32), "CT": ("sbuf", [128, 96], f32), "CO": ("sbuf", [128, 32], u16),
+    "X": ("sbuf", [128, NP * XS], f32), "D": ("sbuf", [128, (NP + 2) * MP], f32), "G": ("sbuf", [128, NP * MP], bf),
+    "Wp": ("sbuf", [128, 2 * 136], bf), "VI": ("sbuf", [128, U], f32), "V2": ("sbuf", [128, 2 * U], f16),
+    "SG": ("sbuf", [128, 8 * CH], bf), "VAL": ("sbuf", [128, 2 * H], bf), "RS": ("sbuf", [128, 2 * CH], f32),
+    "pA0": ("psum", [128, 512], f32), "pA1": ("psum", [128, 512], f32), "pB": ("psum", [128, 512], f32),
+    "pE": ("psum", [128, 512], f32), "pD": ("psum", [128, 1024], f32), "pM": ("psum", [128, 1024], f32),
 }
-for _b in range(NB):
-    SCRATCH["X%d" % _b] = ("sbuf", [128, B + 8], f32)
-    SCRATCH["D%d" % _b] = ("sbuf", [128, B], f32)
-    SCRATCH["OF%d" % _b] = ("sbuf", [128, CH], u16)
-for _b in range(2):
-    for _n, _c, _d in (("G", B, bf), ("SG", 8 * CH, bf), ("RR", CH, bf), ("A16", CH, f16), ("VAL", 2 * CH, bf),
-                       ("RS", 2 * CH, f32), ("POW", CH, bf), ("F", CH, bf), ("EA", CH, f16), ("HB", CH, bf),
-                       ("HQ", CH, f32), ("TP", CH, f32)):
-        SCRATCH["%s%d" % (_n, _b)] = ("sbuf", [128, _c], _d)
-NDMA = 16
+for _n, _d in (("SN", u16), ("OF", u16), ("N16", f16), ("RR", bf), ("A16", f16), ("POW", bf), ("F", bf), ("EA", f16),
+               ("HB", bf), ("TOP", f32)):
+    SCRATCH[_n] = ("sbuf", [128, H], _d)
+NDMA = 32
 SEMAPHORES = ["cv", "cs", "ct", "cg", "left", "arL", "arP"] + ["ar%d" % _b for _b in range(4)] + \
              ["d%d" % _b for _b in range(NDMA)]
 
 CYC = 0.83
-PCYC = 0.42
+PCYC = [0.42, 0.52, 0.42]
 GAM = 1.56
-VO = 55.0
+VO, SO = 55.0, 80.0
 SCEN = [(VO, GAM), (VO, 1.15), (VO, 1.95)]
-LAT_X, LAT_S = 120.0, 80.0
+LAT_X, LAT_S = 160.0, 90.0
+LAT_P, LAT_L, LAT_R = 5000.0, 14000.0, 16000.0
 
 
 def masks(topo, T, src):
@@ -86,9 +87,11 @@ def build(g, core, T, topo):
     ops = []
     lastw, readers, lastbank = {}, {}, {}
     ndma = [0]
+    alias = {}
 
     def op(eng, cost, fn, r=(), w=(), banks=(), sem=None, val=0, lat=0.0, after=()):
         me = len(ops)
+        r, w, banks = [[alias.get(k, k) for k in x] for x in (r, w, banks)]
         hard, soft = set(after), set()
         for k in r:
             if k in lastw: hard.add(lastw[k])
@@ -125,14 +128,14 @@ def build(g, core, T, topo):
     def cp(out, a, n, r, w, banks=(), f=1.0):
         return op("v", vcost(n, f), lambda: g.vector.tensor_copy(out, a), r, w, banks)
 
-    def ms(out, c, n, w):
-        return op("v", vcost(n), lambda: g.vector.memset(out, c), (), w)
+    def ms(out, c, n, w, r=()):
+        return op("v", vcost(n), lambda: g.vector.memset(out, c), r, w)
 
     def act(out, a, func, n, r, w, banks=(), f=1.0, bias=None, scale=None):
         kw = {}
         if bias is not None: kw["bias"] = bias
         if scale is not None: kw["scale"] = scale
-        cost = [65 + n * (ga if f == GAM else f) * CYC for vo, ga in SCEN]
+        cost = [SO + n * (ga if f == GAM else f) * CYC for vo, ga in SCEN]
         return op("s", cost, lambda: g.scalar.activation(out, a, func, **kw), r, w, banks)
 
     def mm(items, r, w, banks):
@@ -141,7 +144,7 @@ def build(g, core, T, topo):
             for o, l, x, st, sp, _ in items:
                 ins = g.tensor.matmul(o, l, x, st, sp)
             return ins
-        return op("t", 30 + sum(max(64, it[5]) for it in items) * PCYC, fn, r, w, banks)
+        return op("t", [30 + sum(max(64, it[5]) for it in items) * pc for pc in PCYC], fn, r, w, banks)
 
     def grp(out, pairs, n, first=True, last=True):
         return [(out, l, x, first and i == 0, last and i == len(pairs) - 1, n) for i, (l, x) in enumerate(pairs)]
@@ -161,12 +164,12 @@ def build(g, core, T, topo):
         q = g.sync if eng == "y" else g.scalar
 
         def fn():
-            for o, a in pairs: q.dma_start(o, a).then_inc(sem, 16)
-        return op(eng, 60.0 * len(pairs), fn, r, w, sem=sem, val=16 * len(pairs), lat=lat)
+            for o, a in pairs:
+                (g.dma_start(o, a, accum_op=A.add) if eng == "g" else q.dma_start(o, a)).then_inc(sem, 16)
+        return op(eng, (1000.0 if eng == "g" else 60.0) * len(pairs), fn, r, w, sem=sem, val=16 * len(pairs), lat=lat)
 
     far, near, fe, ne = masks(topo, T, core)
     nleft = [0]
-
     sent = []
 
     def send(src, dst_of, sem, r, w, lat, parts=((far, fe), (near, ne))):
@@ -195,36 +198,37 @@ def build(g, core, T, topo):
     (PF, PM, G16, G15, M01, NM01, M0, OCOL, CC, WC, SH, M1, PM3, J3, PI, I1, I2, I12, L15, P64, PIV, MG1, MG2,
      SUB, CKC, M02, KC, KBC, HS, HBI, P2) = range(31)
     tmp = list(range(31, 64))
+    sc = lambda x: col(x[0]) if isinstance(x, tuple) else x
 
     def cs(out, a, s1, s2, o0, o1=None):
-        sc = lambda x: col(x[0]) if isinstance(x, tuple) else x
         if out is None: out = tmp.pop()
         ts(col(out), col(a), sc(s1), sc(s2), o0, o1, 1, [a] + [x[0] for x in (s1, s2) if isinstance(x, tuple)], [out])
         return out
 
     def ln(out, a, s, b=0.0):
-        sc = lambda x: col(x[0]) if isinstance(x, tuple) else x
         if out is None: out = tmp.pop()
         act(col(out), col(a), AF.Identity, 1, [a] + [x[0] for x in (s, b) if isinstance(x, tuple)], [out],
             scale=sc(s), bias=sc(b))
         return out
 
     def scaled(out, a, s, n, r, w):
-        if isinstance(s, tuple): act(out, a, AF.Identity, n, r + [s[0]], w, scale=col(s[0]))
-        else: act(out, a, AF.Identity, n, r, w, scale=s)
+        act(out, a, AF.Identity, n, r + ([s[0]] if isinstance(s, tuple) else []), w, scale=sc(s))
 
     def diag(out, c, n, base, w):
         op("g", 170 + 2 * n * CYC, lambda: g.affine_select(out, T.ZR[:, 0:n], [[-1, n]], A.not_equal, c, base, 1),
            ["ZR"], w)
 
-    Lk = lambda: [("L", c, q) for c in range(3) for q in range(NCH)] + [("Lg", c) for c in range(3)]
-    Pk = lambda: [("P", c, q) for c in range(3) for q in range(NCH)] + [("Pg", c) for c in range(3)]
-    Nk = lambda: [("N", c, q) for c in range(3) for q in range(NCH)]
+    pd = lambda bank, a, n: T.pD[:, 512 * int(bank[1]) + a:512 * int(bank[1]) + a + n]
+    every = range(NP)
+    ks = lambda name, js: [(name, j) for j in js]
+    kc = lambda name, c, js: [(name, c, j) for j in js]
+    own = lambda name: [(name, c, j) for c in range(3) for j in every]
+    Lk, Pk = own("L") + ks("Lg", range(3)), own("P") + ks("Pg", range(3))
 
     dma([(T.R[0:112, 96:192], T.ph0[1:8, :]), (T.R[112:128, 96:192], T.ph0[0:1, :]), (T.R[:, 0:96], T.ph0[:, :])],
         (), ["Rph"])
     dma([(T.S0L[0:112, :], T.loud[16:128, 0:GH]), (T.S0L[112:128, :], T.loud[0:16, 0:GH])], (), ["S0L"], eng="s")
-    dma([(T.Nw[:, :], T.nb[:, :])], (), Nk(), lat=3200.0, eng="s")
+    dma([(T.Nw[:, :], T.nb[:, :])], (), own("N"), lat=3200.0, eng="s")
     dma([(T.R[:, 192:288], T.rb[:, :])], (), ["Rrb"])
     dma([(T.Lb[:, 0:V], T.loud[:, :])], (), ["Lb"], lat=3000.0)
     dma([(T.Fd[:, :], T.fade[:, :])], (), ["Fd"], lat=3000.0)
@@ -237,6 +241,8 @@ def build(g, core, T, topo):
     iota(T.IT[:, 0:16], [[-1, 16]], 16, 1, 16, ["IT"], False)
     iota(T.VT[:, :], [[1, 2], [48, 32]], -V, 0, 64, ["VT"], True)
     iota(T.JR[:, :], [[48, 8], [1, 16]], 0, 0, 128, ["JR"], False)
+    iota(T.VR[:, :], [[0, CH // U], [1, U]], 0, 0, CH, ["VR"], True)
+    iota(T.VI[:, :], [[U + 1, 2], [2, U // 2]], 0, 0, U, ["VI"], True)
     ts(T.IP[:, 1:2], T.IP[:, 0:1], 15, None, A.bitwise_and, None, 1, ["IP"], ["IP1"])
     cp(col(PM), T.IP[:, 1:2], 1, ["IP1"], [PM])
     cp(col(PF), T.IP[:, 0:1], 1, ["IP"], [PF])
@@ -247,16 +253,16 @@ def build(g, core, T, topo):
     ln(G16, PM, -1.0, (PF,))
     ts(T.QT[:, :], T.ROW[:, 0:16], col(PM), None, A.is_equal, None, 16, ["ROW", PM], ["QT"])
     for s in range(16):
-        act(T.Qm[:, 136 * s:136 * s + 130], T.WI[:, 15 + s:145 + s], AF.Identity, 130, ["Ib", "QT"], [("Q", s)],
+        act(T.Xb[:, 136 * s:136 * s + 130], T.WI[:, 15 + s:145 + s], AF.Identity, 130, ["Ib", "QT"], [("Q", s)],
             scale=T.QT[:, s:s + 1])
-    Qhi = lambda s: T.Qm[:, 136 * s + 1:136 * s + 129]
-    Qlo = lambda s: T.Qm[:, 136 * s:136 * s + 128]
+    Qhi = lambda s: T.Xb[:, 136 * s + 1:136 * s + 129]
+    Qlo = lambda s: T.Xb[:, 136 * s:136 * s + 128]
     for k, s in ((M0, 0), (M1, 1), (M02, 2), (L15, 15)):
         act(col(k), T.QT[:, s:s + 1], AF.Copy, 1, ["QT"], [k])
     ln(G15, G16, 1.0, 15.0)
     ln(M01, M0, 1.0, (M1,))
     ln(NM01, M01, -1.0)
-    ln(OCOL, PM, 1.0, 8.0 - 8192.0)
+    ln(OCOL, PM, 1.0, 16.0 - 8192.0)
     ln(PM3, PM, 3.0)
     act(T.VT[:, :], T.VT[:, :], AF.Identity, 64, ["VT", PM3], ["VT"], bias=col(PM3))
     ts(T.PT[:, :], T.ROW[:, 0:16], col(PM), 1.0, A.is_lt, A.add, 16, ["ROW", PM], ["PT"])
@@ -287,13 +293,14 @@ def build(g, core, T, topo):
     ts(T.BS[:, :], T.ROW[:, 0:16], col(PM), 16.0, A.add, A.is_ge, 16, ["ROW", PM], ["BS"])
     act(T.BS[:, :], T.BS[:, :], AF.Identity, 16, ["BS"], ["BS"], bias=-0.5)
     r128 = T.ROW[:, 0:128]
-    S01, N01, Wm, Shb, BD, Inq = [blk(T.Bm, j) for j in range(6)]
-    If, Shf, Iq, S2l, S2h, Inf = [blk(T.Fm, j) for j in range(6)]
+    S01, N01, Wm, Shb, BD, Inq, Ie, Inb = [blk(T.Bm, j) for j in range(8)]
+    If, Shf, Iq, S2l, S2h = [blk(T.Fm, j) for j in range(5)]
     I64b = blk(T.Km, 7)
-    for m, c, k in ((I64b, 64.0, ("K", 8)), (If, 1.0, "If"), (Inq, -0.25, "Inq"), (Iq, 0.25, "Iq"), (Inf, -1.0, "Inf")):
-        scaled(m, Ib, c, 128, ["Ib"], [k])
+    scaled(I64b, Ib, 64.0, 128, ["Ib"], [("K", 8)])
+    for m, c, k in ((If, 1.0, "If"), (Inq, -0.25, "Inq"), (Iq, 0.25, "Iq"), (Ie, 0.125, "Ie"), (Inb, -1.0, "Inb")):
+        diag(m, c, 128, 0, [k])
     ts(Shb, r128, col(SH), None, A.is_equal, None, 128, ["ROW", SH], ["Shb"], f=0.5)
-    scaled(Shf, Shb, 1.0, 128, ["Shb"], ["Shf"])
+    gcopy(Shf, Shb, 128, ["Shb"], ["Shf"])
     ts(BD, T.ROWG[:, :], col(G16), None, A.is_equal, None, 128, ["ROWG", G16], ["BD"], f=0.5)
     for m, c, k in ((S01, M01, "S01"), (N01, NM01, "N01"), (Wm, WC, "Wm")):
         scaled(m, BD, (c,), 128, ["BD"], [k])
@@ -304,10 +311,10 @@ def build(g, core, T, topo):
             u = s if k == "Dm" else 16 - s
             ts(blk(T.TH, 4 * j + i), r128, T.TG[:, u:u + 1], -64.0, A.is_equal, A.mult, 128, ["ROW", "TG"],
                [("sh", j, i)], f=0.5)
-            its += grp(blk(T["p" + bank], i), [(Ib, blk(T.TH, 4 * j + i)), (Ib, I64b)], 128)
+            its += grp(pd(bank, 128 * i, 128), [(Ib, blk(T.TH, 4 * j + i)), (Ib, I64b)], 128)
         mm(its, ["Ib", ("K", 8), ("TH", j)] + [("sh", j, i) for i in range(len(ss))], ["p" + bank], [bank])
         n = 128 * len(ss)
-        act(dst[:, 128 * (ss[0] - 1):128 * ss[-1]], T["p" + bank][:, 0:n], AF.Copy, n, ["p" + bank], [(k, s) for s in ss],
+        act(dst[:, 128 * (ss[0] - 1):128 * ss[-1]], pd(bank, 0, n), AF.Copy, n, ["p" + bank], [(k, s) for s in ss],
             [bank])
     scaled(S2l, Ib, (PIV,), 128, ["Ib"], ["S2l"])
     scaled(S2h, T.WI[:, 17:145], (SUB,), 128, ["Ib"], ["S2h"])
@@ -324,269 +331,308 @@ def build(g, core, T, topo):
     ts(blk(T.Wb, 0, 144), T.ROW[:, 0:144], col(G15), None, A.is_equal, None, 144, ["ROW", G15], ["Cw"], f=0.5)
     for j, c, k in ((1, (M01,), "Cw01"), (2, 2.0, "Cw2"), (3, (M0,), "Cw0")):
         scaled(blk(T.Wb, j, 144), blk(T.Wb, 0, 144), c, 144, ["Cw"], [k])
+    ts(T.IP[:, 3:4], col(PM), 0.5, -0.25, A.mult, A.add, 1, [PM], ["IP3"])
+    half = tmp.pop()
+    ts(col(half), T.IP[:, 3:4], 8.0, col(G16), A.add, A.add, 1, ["IP3", G16], [half])
+    odd = tmp.pop()
+    ts(col(odd), T.IP[:, 3:4], -2.0, col(PM), A.mult, A.add, 1, ["IP3", PM], [odd])
+    for par, w_ in ((0, ln(None, odd, -64.0, 64.0)), (1, ln(None, odd, 64.0))):
+        ts(blk(T.Wp, par, 136), T.ROW[:, 0:136], col(half), col(w_), A.is_equal, A.mult, 136, ["ROW", half, w_],
+           [("Wp", par)], f=0.5)
+        ts(blk(T.V2, par, U), T.VI[:, :], par / 16.0, None, A.add, None, U, ["VI"], [("V2", par)])
+    OC2 = ln(None, PM, 2.0, 16.0 - 8192.0)
     wide = lambda j, k: T.Wb[:, 144 * j + 15 - k:144 * j + 143 - k]
-    scaled(T.VR[:, :], T.ROW[:, :], 1.0 / 512.0, 256, ["ROW"], ["VR"])
     ts(T.KK[:, 0:U], T.ROW[:, 0:U], 0.0, col(KC), A.mult, A.add, U, ["ROW", KC], ["K1"], f=0.5)
     ms(T.KK[:, U:U + CH], 511.5, CH // 2, ["K2"])
     act(T.KB[:, :], T.ROW[:, 0:CH], AF.Identity, CH, ["ROW", KBC], ["KB"], scale=0.0, bias=col(KBC))
     for j in range(2):
         act(blk(T.CK, j, CH), T.ROW[:, 0:CH], AF.Identity, CH, ["ROW", CKC], [("CK", j)], scale=0.0, bias=col(CKC))
     ms(T.MASK[:, :], 1.0, MP // 2, ["MASK"])
-    op("v", vcost(MP // 16), lambda: g.vector.memset(T.MASK[:, 0:MP:16], 0.0), ["MASK"], ["MASK"])
-    for b in range(NB):
-        ms(T["X%d" % b][:, 0:8], 0.0, 8, [("X0", b)])
-    if D_ON_T:
-        mm([(blk(T.pM, j, 512), Ib, T.MASK[:, 0:512], True, False, 512) for j in range(2)], ["Ib", "MASK"], ["M0", "M1"],
-           ["M0", "M1"])
+    ms(T.MASK[:, 0:MP:16], 0.0, U, ["MASK"], ["MASK"])
+    for j in every:
+        iota(T.X[:, XS * j:XS * j + 16], [[0, 16]], 0, 0, 16, [("Xf", j)], True)
 
     cp(T.Rh[:, 0:192], T.R[:, 0:192], 192, ["Rph"], ["Rh"])
     tt(T.Rl[:, 0:192], T.R[:, 0:192], T.Rh[:, 0:192], A.subtract, 192, ["Rph", "Rh"], ["Rl"])
     its = []
     for s, n in ((0, 96), (1, 96), (2, 48)):
         its += grp(T.pB[:, 96 * s:96 * s + n], [(Qhi(s), T.Rh[:, 96:96 + n]), (Qlo(s), T.Rl[:, 96:96 + n])], n)
-    mm(its, ["Rh", "Rl"] + [("Q", s) for s in range(3)], ["pB"], ["B"])
-    act(T.S0P[:, :], T.pB[:, 0:GH], AF.Copy, GH, ["pB"], ["S0P"], ["B"])
-    send(T.S0P[:, :], lambda d: T.Pw[:, V + (d - 1) * GH:V + d * GH], T.sem.arP, ["S0P"],
-         [("Pg", c) for c in range(3)], 5000.0)
-    send(T.S0L[:, :], lghost, T.sem.arL, ["S0L"], ["Lbg"], 8000.0, [(far, fe)])
+    mm(its, ["Rh", "Rl"] + [("Q", s) for s in range(3)], ["Bl"], ["B"])
+    act(T.S0P[:, :], T.pB[:, 0:GH], AF.Copy, GH, ["Bl"], ["S0P"], ["B"])
+    send(T.S0P[:, :], lambda d: T.Pw[:, V + (d - 1) * GH:V + d * GH], T.sem.arP, ["S0P"], ks("Pg", range(3)), LAT_P)
+    send(T.S0L[:, :], lghost, T.sem.arL, ["S0L"], ["Lbg"], LAT_L, [(far, fe)])
     cp(T.Rh[:, 192:288], T.R[:, 192:288], 96, ["Rrb"], ["Rh2"])
     tt(T.Rl[:, 192:288], T.R[:, 192:288], T.Rh[:, 192:288], A.subtract, 96, ["Rrb", "Rh2"], ["Rl2"])
-    own = [("P", c, q) for c in range(3) for q in range(NCH)]
-    for o, dst, ks, keys in ((0, T.Pw, ["Rh", "Rl"], own), (192, T.Rw, ["Rh2", "Rl2"], ["Rw"])):
+    for o, dst, rk, keys in ((0, T.Pw, ["Rh", "Rl"], own("P")), (192, T.Rw, ["Rh2", "Rl2"], ["Rw"])):
         for j in range(4):
             bank = ("D0", "D1")[j % 2]
             its = []
             for s in range(4 * j, 4 * j + 4):
-                its += grp(T["p" + bank][:, 96 * (s % 4):96 * (s % 4) + 96],
+                its += grp(pd(bank, 96 * (s % 4), 96),
                            [(Qhi(s), T.Rh[:, o:o + 96]), (Qlo(s), T.Rl[:, o:o + 96])], 96)
-            mm(its, ks + [("Q", s) for s in range(4 * j, 4 * j + 4)], ["p" + bank], [bank])
+            mm(its, rk + [("Q", s) for s in range(4 * j, 4 * j + 4)], ["p" + bank], [bank])
             kw = [("init", o, j)] + (keys if j == 3 else [])
             kr = ["p" + bank] + ([("init", o, i) for i in range(3)] if j == 3 else [])
-            act(dst[:, 384 * j:384 * j + 384], T["p" + bank][:, 0:384], AF.Copy, 384, kr, kw, [bank])
+            act(dst[:, 384 * j:384 * j + 384], pd(bank, 0, 384), AF.Copy, 384, kr, kw, [bank])
+    for j in every:
+        iota(T.Xb[:, XS * j:XS * j + 16], [[0, 16]], 0, 0, 16, (ks("Q", range(16)) if j < 3 else []) + [("X", j), ("Xz", j)],
+             True)
     for c in range(2):
-        gcopy(T.MN[:, H * c:H * (c + 1)], T.Nw[:, c:V:3], H, [("N", c, q) for q in range(NCH)], [("MN", c)])
-    gcopy(T.Lw[:, 0:V], T.Lb[:, 0:V], V, ["Lb"], [("L", c, q) for c in range(3) for q in range(NCH)])
-    gcopy(T.Lw[:, V:W], T.Lb[:, V:W], W - V, ["Lbg"], [("Lg", c) for c in range(3)])
+        gcopy(T.MN[:, H * c:H * (c + 1)], T.Nw[:, c:V:3], H, kc("N", c, every), [("MN", c)])
+    gcopy(T.Lw[:, 0:V], T.Lb[:, 0:V], V, ["Lb"], own("L"))
+    gcopy(T.Lw[:, V:W], T.Lb[:, V:W], W - V, ["Lbg"], ks("Lg", range(3)))
 
-    def derive(t, qs):
-        c, q0, n = t % 3, qs[0], CH * len(qs)
-        src = T.Nw[:, c + 3 * CH * q0:3 * (CH * q0 + n):3]
-        sl = slice(H * c + CH * q0, H * c + CH * q0 + n)
-        nt, lt = T.NT[:, CH * q0:CH * q0 + n], T.LT[:, CH * q0:CH * q0 + n]
-        k = lambda name: [(name, c, q) for q in qs]
-        kt = lambda name: [(name, q) for q in qs]
-        ts(nt, src, 4095, None, A.bitwise_and, None, n, k("N"), kt("NT"))
-        cp(T.NM[:, sl], nt, n, kt("NT"), k("NM"))
+    def span(t, js):
+        c, v, n = t % 3, U * js[0], U * len(js)
+        return c, v, n, slice(v, v + n), slice(c + 3 * v, 3 * (v + n), 3)
+
+    def derive(t, js):
+        c, v, n, us, vs = span(t, js)
+        src, sl, nt, lt = T.Nw[:, vs], slice(H * c + v, H * c + v + n), T.NT[:, us], T.LT[:, us]
+        k = lambda name: kc(name, c, js)
+        ts(nt, src, 4095, None, A.bitwise_and, None, n, k("N"), ks("NT", js))
+        cp(T.NM[:, sl], nt, n, ks("NT", js), k("NM"))
         ts(T.DL[:, sl], src, 2.0 ** -12, 1024.6, A.mult, A.add, n, k("N"), k("DL"))
         ts(T.HI[:, sl], T.NM[:, sl], 2.0 ** -6, 128.0 + 65.0 / 128.0, A.mult, A.add, n, k("NM"), k("HI"), f=0.5)
         act(T.HI[:, sl], T.HI[:, sl], AF.Identity, n, k("HI"), k("HI"), bias=-128.0)
-        ts(lt, src, 63, None, A.bitwise_and, None, n, k("N"), kt("LT"))
-        gcopy(T.LO[:, sl], lt, n, kt("LT"), k("LO"))
+        ts(lt, src, 63, None, A.bitwise_and, None, n, k("N"), ks("LT", js))
+        gcopy(T.LO[:, sl], lt, n, ks("LT", js), k("LO"))
         act(T.LO[:, sl], T.LO[:, sl], AF.Identity, n, k("LO"), k("LO"), bias=1.0)
 
-    for t in range(3): derive(t, list(range(NCH)))
+    for t in range(3): derive(t, list(every))
 
     def pick(on_v, out, win, r, w):
         if on_v: cp(out, win, MP, r, w, f=GAM)
         else: act(out, win, AF.Copy, MP, r, w, f=GAM)
 
-    def front(t, q):
-        c, z = t % 3, q % 2
+    def front(t, js, z):
+        c, v, n, us, vs = span(t, js)
         bA = "A%d" % z
         pA = T["p" + bA]
-        lo, hi = pA[:, 0:CH], pA[:, 256:256 + CH]
-        o = H * c + CH * q
-        G, SG, RR, A16, VAL, RS = [T["%s%d" % (k, z)] for k in ("G", "SG", "RR", "A16", "VAL", "RS")]
-        for j in range(NP):
-            pick((t, q, j) in P_ON_V, G[:, MP * j:MP * (j + 1)], T.Pw[:, 0:W].indirect(T.NM[:, o + U * j:o + U * (j + 1)]),
-                 Pk() + [("NM", c, q)], [("IND", z, j)])
-            pairs = [(wide(1, k), G[:, MP * j + k:MP * (j + 1):16]) for k in range(16)]
-            pairs += [(Ib, T.DL[:, o + U * j:o + U * (j + 1)]), (BD, T.KK[:, 0:U]),
-                      (N01, T.Pw[:, c + 3 * (CH * q + U * j):3 * (CH * q + U * (j + 1)):3])]
-            mm(grp(pA[:, U * j:U * (j + 1)], pairs, U),
-               [("IND", z, j), "Cw01", "Ib", "BD", ("DL", c, q), "K1", "N01", ("P", c, q)], [bA + "l"], [bA])
-        act(RR[:, :], lo, AF.Copy, CH, [bA + "l"], [("RR", z)], [bA])
-        tt(A16[:, :], lo, RR[:, :], A.subtract, CH, [bA + "l", ("RR", z)], [("A16", z)], [bA])
-        per = 512 // CH
-        for j in range(8 // per):
-            bank = ("D0", "D1")[j % 2]
-            its = []
-            for i in range(per):
-                its += grp(T["p" + bank][:, CH * i:CH * (i + 1)], [(blk(T.Dm, per * j + i), A16[:, :])], CH)
-            mm(its, [("A16", z)] + [("Dm", per * j + i + 1) for i in range(per)], ["p" + bank], [bank])
-            for i in range(per):
-                s = per * j + i + 1
-                act(blk(SG, s - 1, CH), T["p" + bank][:, CH * i:CH * (i + 1)], AF.Sign, CH, ["p" + bank, "BS"],
-                    [("SG", z, s)], [bank], bias=T.BS[:, s:s + 1])
-        for j in range(2):
-            ss = range(4 * j + 1, 4 * j + 5)
-            mm(grp(hi, [(blk(T.Km, s - 1), blk(SG, s - 1, CH)) for s in ss], CH, j == 0, j == 1),
-               [("SG", z, s) for s in ss] + [("K", s) for s in ss], [bA + "h"], [bA])
-        act(lo, hi, AF.Sigmoid, CH, [bA + "h"], [bA + "l"], [bA],
+        lo, hi = pA[:, 0:n], pA[:, 256:256 + n]
+        o = H * c + v
+        RR, A16, VAL, RS = T.RR[:, us], T.A16[:, us], T.VAL[:, 2 * v:2 * (v + n)], T.RS[:, 0:2 * n]
+        for j in js:
+            oj = H * c + U * j
+            pick((t, j) in P_ON_V, T.G[:, MP * j:MP * (j + 1)], T.Pw[:, 0:W].indirect(T.NM[:, oj:oj + U]),
+                 Pk + [("NM", c, j)], [("IND", j)])
+            pairs = [(wide(1, k), T.G[:, MP * j + k:MP * (j + 1):16]) for k in range(16)]
+            pairs += [(Ib, T.DL[:, oj:oj + U]), (BD, T.KK[:, 0:U]), (N01, T.Pw[:, span(t, [j])[4]])]
+            mm(grp(pA[:, U * j - v:U * (j + 1) - v], pairs, U),
+               [("IND", j), "Cw01", "Ib", "BD", ("DL", c, j), "K1", "N01", ("P", c, j)], [bA + "l"], [bA])
+        act(RR, lo, AF.Copy, n, [bA + "l"], ks("RR", js), [bA])
+        tt(A16, lo, RR, A.subtract, n, [bA + "l"] + ks("RR", js), ks("A16", js), [bA])
+        per = 512 // n
+        SG = lambda s, m=1: T.SG[:, CH * (s - 1):CH * (s - 1) + n * m]
+        sk = lambda s: [("SG", s)]
+        for i, s0 in enumerate(range(1, 9, per)):
+            bank, ss, its = ("D0", "D1")[i % 2], range(s0, min(s0 + per, 9)), []
+            for s in ss:
+                its += grp(pd(bank, n * (s - s0), n), [(blk(T.Dm, s - 1), A16)], n)
+            mm(its, ks("A16", js) + ks("Dm", ss), ["p" + bank], [bank])
+            for s in ss:
+                act(SG(s), pd(bank, n * (s - s0), n), AF.Sign, n, ["p" + bank, "BS"], sk(s), [bank], bias=T.BS[:, s:s + 1])
+        for i in range(2):
+            ss = range(4 * i + 1, 4 * i + 5)
+            mm(grp(hi, [(blk(T.Km, s - 1), SG(s)) for s in ss], n, i == 0, i == 1),
+               sum([sk(s) for s in ss], []) + ks("K", ss), [bA + "h"], [bA])
+        act(lo, hi, AF.Sigmoid, n, [bA + "h"], [bA + "l"], [bA],
             bias=-59.0 * math.log(2.0), scale=6.0 * math.log(2.0) / 128.0)
-        act(T["POW%d" % z][:, :], hi, AF.Sigmoid, CH, [bA + "h"], [("POW", z)], [bA],
+        tt(T.VAL[:, 2 * v:2 * v + n], lo, T.LO[:, o:o + n], A.mult, n, [bA + "l"] + kc("LO", c, js), ks("VL", js), [bA])
+        tt(T.VAL[:, 2 * v + n:2 * (v + n)], lo, T.HI[:, o:o + n], A.mult, n, [bA + "l"] + kc("HI", c, js), ks("VH", js), [bA])
+        act(T.POW[:, us], hi, AF.Sigmoid, n, [bA + "h"], ks("POW", js), [bA],
             bias=-37.5 * math.log(2.0), scale=-math.log(2.0) / 128.0)
-        tt(VAL[:, 0:CH], lo, T.LO[:, o:o + CH], A.mult, CH, [bA + "l", ("LO", c, q)], [("VL", z)], [bA])
-        tt(VAL[:, CH:2 * CH], lo, T.HI[:, o:o + CH], A.mult, CH, [bA + "l", ("HI", c, q)], [("VH", z)], [bA])
-        bank = "D%d" % z
-        pS = T["p" + bank][:, :]
-        mm(grp(pS, [(I64b, T.CK[:, :]), (blk(T.Pm, 5), VAL[:, :])], 2 * CH, True, False),
-           [("VL", z), ("VH", z), ("K", 8), ("CK", 0), ("CK", 1), ("Pm", 5)], ["p" + bank], [bank])
-        for j in range(5):
-            th = blk(T.TH, j, 2 * CH)
-            ts(th, VAL[:, :], UNIT[3 * j], UNIT[3 * j + 3], A.max, A.min, 2 * CH, [("VL", z), ("VH", z)], [("TH", j)], f=0.5)
-            mm(grp(pS, [(blk(T.Pm, j), th)], 2 * CH, False, j == 4), [("TH", j), ("Pm", j)], ["p" + bank], [bank])
-        ts(RS[:, :], pS, col(MG1), col(MG2), A.add, A.subtract, 2 * CH, ["p" + bank, MG1, MG2], [("RS", z)], [bank])
-        mm(grp(lo, [(S2h, RS[:, CH:2 * CH]), (S2l, RS[:, 0:CH])], 4 * CH), [("RS", z), "S2l", "S2h"], [bA + "l"], [bA])
-        ts(T.SN[:, CH * q:CH * (q + 1)], lo, col(CC), None, A.add, None, CH, [bA + "l", CC], [("SN", q)], [bA])
+        vk = ks("VL", js) + ks("VH", js)
+        bank, pS, sk_ = ("B", T.pB[:, 0:2 * n], ["Bl", "Bh"]) if v == 0 else ("D1", pd("D1", 0, 2 * n), ["pD1"])
+        mm(grp(pS, [(I64b, T.CK[:, 0:2 * n])], 2 * n, True, False), [("K", 8), ("CK", 0), ("CK", 1)], sk_, [bank])
+        mm(grp(pS, [(blk(T.Pm, 5), VAL)], 2 * n, False, False), vk + [("Pm", 5)], sk_, [bank])
+        for i in range(5):
+            th = T.TH[:, 2 * CH * i:2 * CH * i + 2 * n]
+            ts(th, VAL, UNIT[3 * i], UNIT[3 * i + 3], A.max, A.min, 2 * n, vk, [("TH", i)], f=0.5)
+            mm(grp(pS, [(blk(T.Pm, i), th)], 2 * n, False, i == 4), [("TH", i), ("Pm", i)], sk_, [bank])
+        ts(RS, pS, col(MG1), col(MG2), A.add, A.subtract, 2 * n, sk_ + [MG1, MG2], ["RS"], [bank])
+        mm(grp(lo, [(S2h, T.RS[:, n:2 * n]), (S2l, T.RS[:, 0:n])], 4 * n), ["RS", "S2l", "S2h"], [bA + "l"], [bA])
+        ts(T.SN[:, us], lo, col(CC), None, A.add, None, n, [bA + "l", CC], ks("SN", js), [bA])
 
     def first(t):
         c, n = t % 3, H // 16
-        ts(T.N16[:, :], T.SN[:, :], float(V), None, A.min, None, H, [("SN", q) for q in range(NCH)], ["N16"], f=0.5)
-        p = T.pD0[:, 0:n]
-        mm(grp(p, [(wide(3, i), T.N16[:, i:H:16]) for i in range(16)], n), ["N16", "Cw0"], ["pD0"], ["D0"])
-        ts(T.CT[:, 0:n], p, float(V), None, A.is_equal, None, n, ["pD0"], ["CT"], ["D0"])
+        ts(T.N16[:, :], T.SN[:, :], float(V), None, A.min, None, H, ks("SN", every), ["N16"], f=0.5)
+        p = T.pE[:, 256:256 + n]
+        mm(grp(p, [(wide(3, i), T.N16[:, i:H:16]) for i in range(16)], n), ["N16", "Cw0"], ["Eh"], ["E"])
+        ts(T.CT[:, 0:n], p, float(V), None, A.is_equal, None, n, ["Eh"], ["CT"], ["E"])
         tt(T.CT[:, n:2 * n], T.CT[:, 0:n], T.VT[:, n * c:n * (c + 1)], A.mult, n, ["CT", "VT"], ["CT1"])
-        tt(T.CT[:, 2 * n:3 * n], p, T.CT[:, n:2 * n], A.add, n, ["pD0", "CT1"], ["CT2"], ["D0"])
+        tt(T.CT[:, 2 * n:3 * n], p, T.CT[:, n:2 * n], A.add, n, ["Eh", "CT1"], ["CT2"], ["E"])
         cp(T.CO[:, :], T.CT[:, 2 * n:3 * n], n, ["CT2"], ["CO"])
         tt(T.GD[:, :], T.Nw[:, 0:V].indirect(T.CO[:, :]), T.MN[:, H * c:H * (c + 1)], A.subtract, H,
-           Nk() + ["CO", ("MN", c)], [("GD", q) for q in range(NCH)], f=GAM)
+           own("N") + ["CO", ("MN", c)], ["GD"], f=GAM)
 
-    def gather(t, q):
-        b = (t * NCH + q) % NB
-        X = T["X%d" % b]
-        win, keys = (T.Lb, ["Lb", "Lbg"]) if t == 0 else (T.Lw, Lk())
-        for j in range(NP):
-            pick((t, q, j) in L_ON_V, X[:, 8 + MP * j:8 + MP * (j + 1)],
-                 win[:, 0:W].indirect(T.SN[:, CH * q + U * j:CH * q + U * (j + 1)]), keys + [("SN", q)], [("X", b, j)])
+    xp = lambda t, j, a, b=XS, s=1: (T.X if t else T.Xb)[:, XS * j + a:XS * j + b:s]
 
-    def back(t, q):
-        c, z, b = t % 3, q % 2, (t * NCH + q) % NB
+    room = list(range(NP // 2 + 1))
+    slot = lambda j: 2 * room[j // 2] + j % 2
+
+    def gather(t, js):
+        win, keys = (T.Lb, ["Lb", "Lbg"]) if t == 0 else (T.Lw, Lk)
+        for j in js:
+            pick((t, j) in L_ON_V, xp(t, j, 16), win[:, 0:W].indirect(T.SN[:, U * j:U * (j + 1)]), keys + [("SN", j)], [("X", j)])
+
+    def back(t, js, z, fine):
+        c, v, n, us, vs = span(t, js)
         bA = "A%d" % z
-        pA, X, D, IND = T["p" + bA], T["X%d" % b], T["D%d" % b], T["G%d" % z]
-        top, TP = pA[:, 256:256 + CH], T["TP%d" % z]
-        vs = slice(c + 3 * CH * q, 3 * CH * (q + 1), 3)
-        bM = ["M0", "M1"]
-        lo, hi = T.pB[:, 0:CH], T.pB[:, 256:256 + CH]
-        F, OF = T["F%d" % z], T["OF%d" % b]
+        pA = T["p" + bA]
+        top = pA[:, 256:256 + n]
+        alias.clear()
+        if (t, js[0]) in B_IN_D: alias.update({"B": "D1", "Bl": "pD1", "Bh": "pD1h"})
+        pb = lambda a, m: pd("D1", a, m) if alias else T.pB[:, a:a + m]
+        lo, hi = pb(0, n), pb(256, n)
 
-        def mask(js):
-            sl = slice(U * js[0], U * (js[-1] + 1))
-            n, kf = U * len(js), [("F", z, j) for j in js]
-            if F_ON_S: act(F[:, sl], T.pB[:, sl], AF.Sigmoid, n, ["Bl"], kf, ["B"], bias=1300.0, scale=100.0)
-            else: ts(F[:, sl], T.pB[:, sl], -13.0, None, A.is_ge, None, n, ["Bl"], kf, ["B"])
-            mm(grp(pA[:, sl], [(I64b, F[:, sl]), (I64b, T.VR[:, sl])], n), kf + [("K", 8), "VR"], [bA + "l"], [bA])
-            ts(OF[:, sl], pA[:, sl], 128.0, col(OCOL), A.mult, A.add, n, [bA + "l", OCOL], [("OF", b, j) for j in js], [bA])
-
-        for j in range(NP):
-            o = MP * j
-            M = T.pM[:, :]
-            kx = [("X", b, i) for i in range(max(j - 1, 0), j + 1)] + [("X0", b)]
-            op("v", vcost(MP), lambda o=o: g.vector.tensor_tensor_scan(
-                M, X[:, 7 + o:7 + o + MP], T.MASK[:, :], 0.0, A.max, A.mult), kx + ["MASK"], bM, bM)
-            if (t, q, j) not in D_ON_T:
-                tt(D[:, o:o + MP], X[:, 8 + o:8 + o + MP], M, A.subtract, MP, kx + bM, [("D", b, j)], bM)
-            if t < 3:
-                tt(TP[:, U * j:U * (j + 1)], T.pM[:, 15:MP:16], X[:, 8 + o + 15:8 + o + MP:16], A.max, U, kx + bM,
-                   [("TP", z)], bM)
-            elif t < RO - 1:
-                tt(pA[:, 256 + U * j:256 + U * (j + 1)], T.pM[:, 15:MP:16], X[:, 8 + o + 15:8 + o + MP:16], A.max, U,
-                   kx + bM, [bA + "h"], bM + [bA])
-            ind = IND[:, o:o + MP]
-            wk = 0
-            if (t, q, j) in D_ON_T:
-                for i in range(2):
-                    mm([(blk(T.pM, i, 512), Inf, X[:, 8 + o + 512 * i:8 + o + 512 * (i + 1)], False, False, 2048)],
-                       kx + ["Inf", bM[i]], [bM[i]], [bM[i]])
-                act(ind, M, AF.Sign, MP, bM, [("IND", z, j)], bM, bias=-2.0 ** -27, scale=-1.0)
-                act(D[:, o:o + MP], M, AF.Sigmoid, MP, bM, [("D", b, j)], bM, scale=-1.0)
-            elif (t, q, j) in SIGN_S:
-                act(ind, D[:, o:o + MP], AF.Sign, MP, [("D", b, j)], [("IND", z, j)], bias=-2.0 ** -27)
+        def mask(part):
+            m, sl, ps = U * len(part), span(t, part)[3], slice(U * part[0] - v, U * (part[-1] + 1) - v)
+            if F_ON_S: act(T.F[:, sl], pb(ps.start, m), AF.Sigmoid, m, ["Bl"], ks("F", part), ["B"], bias=1300.0, scale=100.0)
+            else: ts(T.F[:, sl], pb(ps.start, m), -13.0, None, A.is_ge, None, m, ["Bl"], ks("F", part), ["B"])
+            if (t, part[0]) in SPLIT:
+                its, oc = [], OC2
+                for a in range(0, m, 2 * U):
+                    for par in range(2):
+                        b = ps.start + a + U * par
+                        its += grp(pA[:, b:b + U], [(Ie, blk(T.V2, par, U))] + [
+                            (T.Wp[:, 136 * par + 8 - 8 * h:136 * par + 136 - 8 * h],
+                             T.F[:, sl.start + a + h:sl.start + a + 2 * U:2]) for h in range(2)], U)
             else:
-                gcopy(ind, D[:, o:o + MP], MP, [("D", b, j)], [("IND", z, j)])
-                ts(ind, ind, 0.0, 0.5, A.is_gt, A.subtract, MP, [("IND", z, j)], [("IND", z, j)], f=0.5)
+                its, oc = grp(pA[:, ps], [(I64b, T.F[:, sl]), (Ie, T.VR[:, 0:m])], m), OCOL
+            mm(its, ks("F", part) + [("K", 8), "Ie", "VR"] + ks("Wp", range(2)) + ks("V2", range(2)), [bA + "l"], [bA])
+            ts(T.OF[:, sl], pA[:, ps], 128.0, col(oc), A.mult, A.add, m, [bA + "l", oc], ks("OF", part), [bA])
+
+        for j in js:
+            pm, kM, bM = (T.pD, ["pD0", "pD1"], ["D0", "D1"]) if (t, j) in M_IN_D else (T.pM, ["M0", "M1"], ["M0", "M1"])
+            o, M, kx = MP * j, pm[:, :], [("X", j)]
+            d, ind, pj, dk = blk(T.D, slot(j), MP), T.G[:, o:o + MP], U * j - v, [("D", slot(j))]
+            on_t = t == 0 and D_ON_T
+            buf, mk, mb = (T.G, [("IND", j)], []) if on_t else (pm, kM, bM)
+            mo = o if on_t else 0
+            op("v", vcost(MP, 0.5 if on_t and t == 0 else 1.0), lambda j=j, m=buf[:, mo:mo + MP]: g.vector.tensor_tensor_scan(
+                m, xp(t, j, 15, XS - 1), T.MASK[:, :], 0.0, A.max, A.mult), kx + ["MASK", ("Xf", j), ("Xz", j)], mk, mb)
+            if not on_t: tt(d, xp(t, j, 16), M, A.subtract, MP, kx + kM, dk, bM)
+            if t < 3:
+                tt(T.TOP[:, U * j:U * (j + 1)], buf[:, mo + 15:mo + MP:16], xp(t, j, 31, XS, 16), A.max, U, kx + mk,
+                   [("TOP", j)], mb)
+            elif t < RO - 1:
+                tt(pA[:, 256 + pj:256 + pj + U], buf[:, mo + 15:mo + MP:16], xp(t, j, 31, XS, 16), A.max, U, kx + mk,
+                   [bA + "h"], mb + [bA], f=2.0 if on_t else 1.0)
+            wk = 0
+            if on_t:
+                for i in range(2):
+                    mm(grp(blk(pm, i, 512), [(Ib, xp(t, j, 16 + 512 * i, 528 + 512 * i)),
+                                             (Inb, buf[:, o + 512 * i:o + 512 * (i + 1)])], 512),
+                       kx + mk + ["Ib", "Inb"], [kM[i]], [bM[i]])
+                if (t, j) in SIGN_S:
+                    act(ind, M, AF.Sign, MP, kM, [("IND", j)], bM, bias=-2.0 ** -27)
+                else:
+                    ts(ind, M, 0.0, 0.5, A.is_gt, A.subtract, MP, kM, [("IND", j)], bM)
+                    wk = 2
+                act(d, M, AF.Sigmoid, MP, kM, dk, bM)
+            elif (t, j) in SIGN_S:
+                act(ind, d, AF.Sign, MP, dk, [("IND", j)], bias=-2.0 ** -27)
+            else:
+                gcopy(ind, d, MP, dk, [("IND", j)])
+                ts(ind, ind, 0.0, 0.5, A.is_gt, A.subtract, MP, [("IND", j)], [("IND", j)], f=0.5)
                 wk = 2
-            mm(grp(T.pB[:, U * j:U * (j + 1)], [(wide(wk, k), IND[:, o + k:o + MP:16]) for k in range(16)], U),
-               [("IND", z, j), "Cw", "Cw2"], ["Bl"], ["B"])
-            if (t, q) in FINE: mask([j])
-        if (t, q) not in FINE: mask(list(range(NP)))
-        EA, HB, HQ = [T["%s%d" % (k, z)][:, :] for k in ("EA", "HB", "HQ")]
-        mm(grp(hi, [(Wm, F[:, :])], CH), [("F", z, j) for j in range(NP)] + ["Wm"], ["Bh"], ["B"])
-        tt(hi, hi, T["POW%d" % z][:, :], A.mult, CH, ["Bh", ("POW", z)], ["Bh"], ["B"])
-        ts(lo, hi, 2.0 ** 23 - 0.5, 2.0 ** 23 + 1.0, A.add, A.is_equal, CH, ["Bh"], ["Bl"], ["B"])
-        tt(EA, lo, T["A16%d" % z][:, :], A.mult, CH, ["Bl", ("A16", z)], [("EA", z)], ["B"])
-        pairs = [(S01, T.Pw[:, vs]), (S01, T.Rw[:, vs]), (Ib, T.KK[:, U:U + CH])] + ([(I64b, T.KB[:, :])] if t >= 2 else [])
-        mm(grp(lo, pairs + [(BD, EA)], CH),
-           [("EA", z), "S01", ("P", c, q), "Rw", "Ib", "K2", "BD", "KB", ("K", 8)], ["Bl"], ["B"])
-        act(HB, lo, AF.Identity, CH, ["Bl", HS, HBI], [("HB", z)], ["B"], scale=col(HS), bias=col(HBI))
+            mm(grp(pb(pj, U), [(wide(wk, k), T.G[:, o + k:o + MP:16]) for k in range(1, 16)], U),
+               [("IND", j), "Cw", "Cw2"], ["Bl"], ["B"])
+            if fine: mask([j])
+        if not fine: mask(js)
+        EA, HB, HQ = T.EA[:, us], T.HB[:, us], T.HQ[:, 0:n]
+        mm(grp(hi, [(Wm, T.F[:, us])], n), ks("F", js) + ["Wm"], ["Bh"], ["B"])
+        tt(hi, hi, T.POW[:, us], A.mult, n, ["Bh"] + ks("POW", js), ["Bh"], ["B"])
+        ts(lo, hi, 2.0 ** 23 - 0.5, 2.0 ** 23 + 1.0, A.add, A.is_equal, n, ["Bh"], ["Bl"], ["B"])
+        tt(EA, lo, T.A16[:, us], A.mult, n, ["Bl"] + ks("A16", js), ks("EA", js), ["B"])
+        pairs = [(S01, T.Pw[:, vs]), (S01, T.Rw[:, vs]), (Ib, T.KK[:, U:U + n])] + ([(I64b, T.KB[:, 0:n])] if t >= 2 else [])
+        mm(grp(lo, pairs + [(BD, EA)], n),
+           ks("EA", js) + kc("P", c, js) + ["S01", "Rw", "Ib", "K2", "BD", "KB", ("K", 8)], ["Bl"], ["B"])
+        act(HB, lo, AF.Identity, n, ["Bl", HS, HBI], ks("HB", js), ["B"], scale=col(HS), bias=col(HBI))
+        ghosts = v == 0
         if t < RO - 1:
-            tt(T.Pw[:, vs], lo, HB, A.subtract, CH, ["Bl", ("HB", z)], [("P", c, q)], ["B"])
+            tt(T.Pw[:, vs], lo, HB, A.subtract, n, ["Bl"] + ks("HB", js), kc("P", c, js), ["B"])
         if t >= 2:
-            tt(T.YP[:, vs], lo, HB, A.subtract, CH, ["Bl", ("HB", z)], [("YP", c, q)], ["B"])
-        if t < 2:
-            hid, GD = T.pE[:, 256:256 + CH], T.GD[:, CH * q:CH * (q + 1)]
-            ts(HQ, hi, 1.5 * 2.0 ** 24, 1.5 * 2.0 ** 24, A.add, A.subtract, CH, ["Bh"], [("HQ", z)], ["B"])
-            tt(hid, hi, HQ, A.is_gt, CH, ["Bh", ("HQ", z)], ["Eh"], ["B", "E"])
-            tt(hid, hid, GD, A.mult, CH, ["Eh", ("GD", q)], ["Eh"], ["E"])
-            tt(T.Nw[:, vs], hid, T.Nw[:, vs], A.add, CH, ["Eh", ("N", c, q)], [("N", c, q)], ["E"])
+            tt(T.YP[:, vs], lo, HB, A.subtract, n, ["Bl"] + ks("HB", js), kc("YP", c, js), ["B"])
         if t < RO - 1:
             if t < 3:
                 Lo = T.Lb[:, vs]
-                mm(grp(top, [(Iq, TP[:, :])], 4 * CH, True, False) + grp(top, [(Inq, Lo), (Ib, Lo)], CH, False, True),
-                   [("TP", z), "Lb", "Iq", "Inq", "Ib"], [bA + "h"], [bA])
+                mm(grp(top, [(Iq, T.TOP[:, us])], 4 * n, True, False) + grp(top, [(Inq, Lo), (Ib, Lo)], n, False, True),
+                   ks("TOP", js) + ["Lb", "Iq", "Inq", "Ib"], [bA + "h"], [bA])
             else:
-                Lo, lk = T.Lw[:, vs], ("L", c, q)
-                tt(top, top, Lo, A.subtract, CH, [bA + "h", lk], [bA + "h"], [bA])
-                act(top, top, AF.Copy, CH, [bA + "h"], [bA + "h"], [bA], scale=0.25)
-                tt(top, top, Lo, A.add, CH, [bA + "h", lk], [bA + "h"], [bA])
-            tt(T.Lw[:, vs], top, T.Fd[:, vs], A.mult, CH, [bA + "h", "Fd"], [("L", c, q)], [bA])
-            if q == 0:
-                sb = T.SB[:, 2 * NG * t:2 * NG * (t + 1)]
-                mm(grp(pA[:, 0:NG], [(Shf, T.Lw[:, c:GH:3])], 4 * NG) + grp(pA[:, NG:2 * NG], [(Shb, T.Pw[:, c:GH:3])], NG),
-                   [("L", c, 0), ("P", c, 0), "Shf", "Shb"], [bA + "l"], [bA])
-                act(sb, pA[:, 0:2 * NG], AF.Copy, 2 * NG, [bA + "l"], [("SB", t)], [bA])
-                send(sb, lambda d: T.ST[:, 7 * t + d - 1, :], T.sem["ar%d" % t], [("SB", t)], [("ST", t)], 6000.0)
+                Lo, lk = T.Lw[:, vs], kc("L", c, js)
+                tt(top, top, Lo, A.subtract, n, [bA + "h"] + lk, [bA + "h"], [bA])
+                act(top, top, AF.Copy, n, [bA + "h"], [bA + "h"], [bA], scale=0.25)
+                tt(top, top, Lo, A.add, n, [bA + "h"] + lk, [bA + "h"], [bA])
+            if ghosts:
+                tt(T.LN[:, 0:n], top, T.Fd[:, vs], A.mult, n, [bA + "h", "Fd"], ["LN"], [bA])
+                gcopy(T.Lw[:, vs], T.LN[:, 0:n], n, ["LN"], kc("L", c, js))
+                sb = blk(T.SB, t, 2 * NG)
+                mm(grp(pA[:, 256:256 + NG], [(Shf, T.LN[:, 0:NG])], 4 * NG), ["LN", "Shf"], [bA + "h"], [bA])
+                mm(grp(pA[:, 256 + NG:256 + 2 * NG], [(Shb, T.Pw[:, c:GH:3])], NG), kc("P", c, (0, 1)) + ["Shb"],
+                   [bA + "h"], [bA])
+                act(sb, pA[:, 256:256 + 2 * NG], AF.Copy, 2 * NG, [bA + "h"], [("SB", t)], [bA])
+                send(sb, lambda d: T.ST[:, 7 * (t % 2) + d - 1, :], T.sem["ar%d" % t], [("SB", t)], [("ST", t % 2)], LAT_R)
+            else:
+                tt(T.Lw[:, vs], top, T.Fd[:, vs], A.mult, n, [bA + "h", "Fd"], kc("L", c, js), [bA])
+        if t < 2:
+            hid = T.pE[:, 256:256 + n]
+            ts(HQ, hi, 1.5 * 2.0 ** 24, 1.5 * 2.0 ** 24, A.add, A.subtract, n, ["Bh"], ["HQ"], ["B"])
+            tt(hid, hi, HQ, A.is_gt, n, ["Bh", "HQ"], ["Eh"], ["B", "E"])
+            tt(hid, hid, T.GD[:, us], A.mult, n, ["Eh", "GD"], ["Eh"], ["E"])
+            tt(T.Nw[:, vs], hid, T.Nw[:, vs], A.add, n, ["Eh"] + kc("N", c, js), kc("N", c, js), ["E"])
 
-    def rest(t, q):
-        c, b = t % 3, (t * NCH + q) % NB
-        X, D, OF = T["X%d" % b], T["D%d" % b], T["OF%d" % b]
-        vs = slice(c + 3 * CH * q, 3 * CH * (q + 1), 3)
-        if t < 2: derive(t + 3, [q])
-        lo = T.pE[:, 0:CH]
-        xk = [("X", b, i) for i in range(NP)] + [("X0", b)]
-        old = t >= 3 and E_ON_T
-        for j in range(NP):
-            o, dk = MP * j, [("D", b, j)]
-            d, p = D[:, o:o + MP], T.pE[:, U * j:U * (j + 1)]
-            if (t, q, j) not in D_ON_T: act(d, d, AF.Sigmoid, MP, dk, dk)
-            win, wk = (X[:, 0:8 + o + MP], xk[:j + 1] + xk[-1:])
-            tt(d, win.indirect(OF[:, U * j:U * (j + 1)]), d, A.mult, MP, dk + wk + [("OF", b, j)], dk, f=GAM)
-            if old:
-                e = T.E[:, c + 3 * (CH * q + U * j):3 * (CH * q + U * (j + 1)):3]
-                mm(grp(p, [(If, e)], 4 * U, True, False), [("E", c, q), "If"], ["El"], ["E"])
-            for k0 in range(0, 16, EG):
-                mm(grp(p, [(If, D[:, o + k:o + MP:16]) for k in range(k0, k0 + EG)], 4 * U,
-                       k0 == 0 and not old, k0 + EG == 16), dk + ["If"], ["El"], ["E"])
-        if t < 3 or old:
-            act(T.E[:, vs], lo, AF.Copy, CH, ["El"], [("E", c, q)], ["E"])
-        else:
-            tt(T.E[:, vs], lo, T.E[:, vs], A.add, CH, ["El", ("E", c, q)], [("E", c, q)], ["E"])
+    def rest(t, js):
+        c, v, n, us, vs = span(t, js)
+        if t < 2: derive(t + 3, js)
+        for j in js:
+            o, dk = MP * slot(j), [("D", slot(j))]
+            d = T.D[:, o:o + MP]
+            if not (t == 0 and D_ON_T): act(d, d, AF.Sigmoid, MP, dk, dk)
+            if (t, j - j % 2) not in SPLIT:
+                tt(d, xp(t, j, 0).indirect(T.OF[:, U * j:U * (j + 1)]), d, A.mult, MP, dk + [("X", j), ("OF", j)], dk,
+                   f=GAM)
+                part, m, eg = [j], 16, EG
+            elif j % 2 == 0:
+                continue
+            else:
+                part, m, eg = [j - 1, j], 8, EG // 2
+                a, b = 2 * room[j // 2], 2 * room[-1]
+                for par in range(2):
+                    tt(blk(T.D, b + par, MP), xp(t, j - 1, 0, 2 * XS).indirect(blk(T.OF, j - 1 + par, U)),
+                       T.D[:, MP * a + par:MP * (a + 2):2], A.mult, MP,
+                       ks("D", (a, a + 1)) + ks("X", part) + ks("OF", part), [("D", b + par)], f=GAM)
+                dma([(blk(T.D, b, MP), blk(T.D, b + 1, MP))], ks("D", (b, b + 1)), [("D", b)], lat=LAT_A, eng="g")
+                room[j // 2], room[-1] = room[-1], room[j // 2]
+                o, dk = MP * b, [("D", b)]
+            p, w_ = T.pE[:, U * part[0] - v:U * (part[-1] + 1) - v], 4 * U * len(part)
+            if t >= 3:
+                mm(grp(p, [(If, T.E[:, span(t, part)[4]])], w_, True, False), kc("E", c, part) + ["If"], ["El"], ["E"])
+            for k0 in range(0, m, eg):
+                mm(grp(p, [(If, T.D[:, o + k:o + MP:m]) for k in range(k0, k0 + eg)], w_,
+                       k0 == 0 and t < 3, k0 + eg == m), dk + ["If"], ["El"], ["E"])
+        act(T.E[:, vs], T.pE[:, 0:n], AF.Copy, n, ["El"], kc("E", c, js), ["E"])
 
+    cut = lambda sizes: [list(range(sum(sizes[:q]), sum(sizes[:q + 1]))) for q in range(len(sizes))]
     for t in range(RO):
         c = t % 3
-        for q in range(NCH): front(t, q)
+        for q, js in enumerate(cut(FRONTS[t])): front(t, js, q % 2)
         if t < 2: first(t)
-        for q in range(NCH): gather(t, q)
-        for q in range(NCH):
-            back(t, q)
-            rest(t, q)
+        gather(t, every)
+        rests = cut(RESTS[t])
+        for q, js in enumerate(cut(BACKS[t])):
+            back(t, js, BANK[t][q], (t, q) in FINE)
+            alias.clear()
+            while rests and rests[0][-1] <= js[-1]: rest(t, rests.pop(0))
         if t < RO - 1:
-            gcopy(T.Pw[:, V + c:W:3], T.ST[:, 7 * t:7 * t + 7, NG:2 * NG], 7 * NG, [("ST", t)], [("Pg", c)])
-            gcopy(T.Lw[:, V + c:W:3], T.ST[:, 7 * t:7 * t + 7, 0:NG], 7 * NG, [("ST", t)], [("Lg", c)])
-    for q in range(NCH):
-        sl = slice(3 * CH * q, 3 * CH * (q + 1))
-        dma([(T.yp[:, sl], T.YP[2:128:16, sl])], [("YP", c, q) for c in range(3)], (), lat=2500.0)
-        dma([(T.ye[:, sl], T.E[:, sl])], [("E", c, q) for c in range(3)], (), lat=2800.0)
+            u = 7 * (t % 2)
+            gcopy(T.Pw[:, V + c:W:3], T.ST[:, u:u + 7, NG:2 * NG], 7 * NG, [("ST", t % 2)], [("Pg", c)])
+            gcopy(T.Lw[:, V + c:W:3], T.ST[:, u:u + 7, 0:NG], 7 * NG, [("ST", t % 2)], [("Lg", c)])
+    for js in cut(RESTS[RO - 1]):
+        sl = slice(3 * U * js[0], 3 * U * (js[-1] + 1))
+        dma([(T.yp[:, sl], T.YP[2:128:16, sl])], [("YP", c, j) for c in range(3) for j in js], (), lat=2500.0)
+        dma([(T.ye[:, sl], T.E[:, sl])], [("E", c, j) for c in range(3) for j in js], (), lat=2800.0)
     return ops, nleft[0]
 
 
@@ -628,82 +674,132 @@ def schedule(ops):
     return order, end, start
 
 
-def place(ops, seq, pred, back):
-    n = len(ops)
-    start, fin = [0.0] * n, [0.0] * n
-    lines = {e: [] for e in "vstgyx"}
-    for i in seq:
-        o = ops[i]
-        cost, s = o["cost"], 0.0
-        for d, l in pred[i]:
-            lat = (o["lat"] if back else ops[d]["lat"]) if l else 0.0
-            s = max(s, fin[d] + l + lat)
-        if back and not pred[i]: s = o["lat"]
-        line = lines[o["eng"]]
-        k = len(line)
-        while k > 0 and line[k - 1][1] > s: k -= 1
-        while k < len(line) and line[k][0] < s + cost:
-            s = max(s, line[k][1])
-            k += 1
-        line.insert(k, (s, s + cost))
-        start[i], fin[i] = s, s + cost
-    end = max(fin[i] + (0.0 if back else ops[i]["lat"]) for i in range(n))
-    return start, fin, end
-
-
 def refine(ops):
     n = len(ops)
-    pred, succ = [[] for _ in range(n)], [[] for _ in range(n)]
-    for i, o in enumerate(ops):
-        for d in o["hard"] | o["soft"]:
-            l = 0.0 if d in o["soft"] else (LAT_S if ops[d]["eng"] == o["eng"] else LAT_X)
-            pred[i].append((d, l))
-            succ[d].append((i, l))
-    order, end, start = schedule(ops)
+    eng = ["vstgyx".index(o["eng"]) for o in ops]
+    costs = [[o["costs"][k] for o in ops] for k in range(len(SCEN))]
+    hard = [[(d, (LAT_S if eng[d] == eng[i] else LAT_X) + ops[d]["lat"]) for d in sorted(o["hard"])]
+            for i, o in enumerate(ops)]
+    pred = [hard[i] + [(d, 0.0) for d in sorted(o["soft"])] for i, o in enumerate(ops)]
+    succ = [[] for _ in range(n)]
+    for i in range(n):
+        for d, l in pred[i]: succ[d].append((i, l))
+    tail = [o["lat"] for o in ops]
+    ends = [i for i in range(n) if not succ[i]]
+    rng = np.random.default_rng(1)
 
-    def score(order):
-        tot = 0.0
-        for k in range(len(SCEN)):
-            fin, free, last = [0.0] * n, {}, 0.0
-            for i in order:
-                o = ops[i]
-                s = free.get(o["eng"], 0.0)
-                for d, l in pred[i]:
-                    if l and fin[d] + l > s: s = fin[d] + l
-                s += o["costs"][k]
-                free[o["eng"]] = s
-                fin[i] = s + o["lat"]
-                if fin[i] > last: last = fin[i]
-            tot += last / ref[k]
-        return tot
+    def length(order, cs, fin, a=0):
+        free, seen, k = [0.0] * 6, set(), a - 1
+        while k >= 0 and len(seen) < 6:
+            if eng[order[k]] not in seen:
+                seen.add(eng[order[k]])
+                free[eng[order[k]]] = fin[order[k]]
+            k -= 1
+        for k in range(a, n):
+            i = order[k]
+            e = eng[i]
+            s = free[e]
+            for d, l in hard[i]:
+                x = fin[d] + l
+                if x > s: s = x
+            free[e] = fin[i] = s + cs[i]
+        return max(fin[i] + tail[i] for i in ends)
 
-    def shaken(key, links, amp):
-        key = list(key + amp * rng.random(n))
-        for i in (range(n) if links is pred else range(n - 1, -1, -1)):
+    def place(key, links, steps, first):
+        for i in steps:
             for d, l in links[i]:
                 if key[d] >= key[i]: key[i] = key[d] + 1e-3
-        return sorted(range(n), key=lambda i: key[i])
+        fin, a, b = [0.0] * n, [[] for _ in range(6)], [[] for _ in range(6)]
+        for i in sorted(range(n), key=lambda i: key[i]):
+            c, s = costs[0][i], first[i]
+            for d, l in links[i]:
+                if fin[d] + l > s: s = fin[d] + l
+            la, lb = a[eng[i]], b[eng[i]]
+            k = m = len(la)
+            while k > 0 and lb[k - 1] > s: k -= 1
+            while k < m and la[k] < s + c:
+                if lb[k] > s: s = lb[k]
+                k += 1
+            la.insert(k, s)
+            lb.insert(k, s + c)
+            fin[i] = s + c
+        return fin
 
-    rng = np.random.default_rng(1)
-    ref = [sum(o["costs"][k] for o in ops if o["eng"] in "vs") for k in range(len(SCEN))]
-    best = (score(order), order, start, end)
+    def runs_of(order, cs, fin):
+        prev, last = [-1] * n, [-1] * 6
+        for i in order:
+            prev[i] = last[eng[i]]
+            last[eng[i]] = i
+        i = max(ends, key=lambda i: fin[i] + tail[i])
+        runs, run = [], [i]
+        while i >= 0:
+            s = fin[i] - cs[i] - 1e-6
+            if prev[i] >= 0 and fin[prev[i]] >= s:
+                i = prev[i]
+                run.append(i)
+            else:
+                if len(run) > 1: runs.append(run[::-1])
+                i = ([d for d, l in hard[i] if fin[d] + l >= s] + [-1])[0]
+                run = [i]
+        return runs
+
+    order, end, start = schedule(ops)
+    total = lambda order: sum(length(order, cs, [0.0] * n) for cs in costs)
+    ca = np.array(costs[0])
+    best = (total(order), order, np.array(start) + ca)
     for it in range(PASSES):
-        start = best[2]
-        t0 = (best[3] + SPAN) * rng.random() - SPAN
-        amp = AMP * rng.random() * np.array([1.0 if t0 <= s <= t0 + SPAN else 0.0 for s in start])
-        fin = np.array([start[i] + ops[i]["cost"] for i in range(n)])
-        bs, bf_, _e = place(ops, shaken(-fin, succ, amp), succ, True)
-        start, fin, end = place(ops, shaken(-np.array(bf_), pred, 0.0), pred, False)
-        order = sorted(range(n), key=lambda i: (start[i], i))
-        sc = score(order)
-        if sc < best[0]: best = (sc, order, start, end)
-    return best[1], best[3], best[2]
+        fin = best[2]
+        t0 = (fin.max() + SPAN) * rng.random() - SPAN
+        noise = AMP * rng.random() * rng.random(n) * ((fin >= t0) & (fin <= t0 + SPAN))
+        back = place(list(noise - fin), succ, range(n - 1, -1, -1), tail)
+        fin = np.array(place([-x for x in back], pred, range(n), [0.0] * n))
+        order = [int(i) for i in np.lexsort((np.arange(n), fin - ca))]
+        val = total(order)
+        if val < best[0]: best = (val, order, fin)
+    order = list(best[1])
+    fins = [[0.0] * n for _ in costs]
+    cur = sum(length(order, cs, f) for cs, f in zip(costs, fins))
+    best = (cur, list(order))
+    pos = [0] * n
+    for k, i in enumerate(order): pos[i] = k
+    before, after = [[d for d, l in x] for x in pred], [[d for d, l in x] for x in succ]
+    runs, draw, far = None, rng.random((MOVES, 5)).tolist(), rng.exponential(1.0, (MOVES, 2)).tolist()
+    for it in range(MOVES):
+        r = draw[it]
+        if runs is None:
+            k = int(r[0] * len(costs))
+            runs = runs_of(order, costs[k], fins[k])
+        run = runs[int(r[1] * len(runs))]
+        a = int(r[2] * (len(run) - 1))
+        u, v = run[a], run[min(len(run) - 1, a + 1 + int(1.4 * far[it][0]))]
+        pu, pv = pos[u], pos[v]
+        win = order[pu:pv + 1]
+        up = r[3] < 0.5
+        need, engs, ok = {v if up else u}, set(), True
+        for i in (win[-2::-1] if up else win[1:]):
+            if eng[i] in engs or any(j in need for j in (after if up else before)[i]):
+                if eng[i] == eng[u]:
+                    ok = False
+                    break
+                need.add(i)
+                engs.add(eng[i])
+        if not ok: continue
+        order[pu:pv + 1] = [i for i in win if (i in need) == up] + [i for i in win if (i in need) != up]
+        new = [list(f) for f in fins]
+        val = sum(length(order, cs, f, pu) for cs, f in zip(costs, new))
+        if val <= cur + TEMP * (1.0 - it / MOVES) * far[it][1]:
+            cur, fins, runs = val, new, None
+            for k in range(pu, pv + 1): pos[order[k]] = k
+            if val < best[0]: best = (val, list(order))
+        else:
+            order[pu:pv + 1] = win
+            if r[4] < 0.05: runs = None
+    return best[1]
 
 
 SLACK = 150.0
-PASSES = 1500
-AMP = 8000.0
-SPAN = 20000.0
+PASSES, AMP, SPAN = 600, 8000.0, 20000.0
+MOVES, TEMP = 60000, 250.0
 ORDER = {}
 
 
@@ -711,7 +807,7 @@ def rank_program(g, core, T, topo):
     if T.rank_of(core) is None:
         return
     ops, nleft = build(g, core, T, topo)
-    if not ORDER: ORDER[0] = refine(ops)[0]
+    if not ORDER: ORDER[0] = refine(ops)
     order = ORDER[0]
     queue = {"v": g.vector, "s": g.scalar, "t": g.tensor, "g": g, "y": g.sync}
     csem = {"v": "cv", "s": "cs", "t": "ct", "g": "cg"}

import math
import numpy as np
from concourse.bass import DstId, RemoteDMATransfer
from concourse.mybir import AluOpType as A, AxisListType, ActivationFunctionType as AF

N, V, H, GH, W, RO = 8, 1536, 512, 240, 3216, 5
U = 64
MP = 16 * U
NP = H // U
XS = MP + 16
CH = 256
EG = 4
NG = GH // 3
OFF = 1.5 * 2.0 ** 17
UNIT = [2.0 ** (6 * r - 104) for r in range(16)]
f32, bf, f16, i32, u16 = "float32", "bfloat16", "float16", "int32", "uint16"

FRONTS = [(4, 4)] * RO
BACKS = [(2, 2, 4)] * (RO - 1) + [(4, 4)]
BANK = [(0, 0, 1)] * (RO - 1) + [(0, 1)]
RESTS = [(4, 4)] * RO
P_ON_V = {(t, j) for t in range(RO) for j in (1, 3)} | {(0, 5), (0, 7)}
L_ON_V = {(0, j) for j in (1, 3, 5, 7)}
SIGN_S = {(t, j) for t in range(RO) for j in range(NP) if j % 4 or t in (0, RO - 1)}
D_ON_T = True
SPLIT = {(t, j) for t in range(RO) for j in range(0, NP, 2)} - {(RO - 1, 4), (RO - 1, 6)}
LAT_A = 4000.0
M_IN_D = {(t, j) for t in range(RO) for j in (4, 6)} | {(0, 2)}
B_IN_D = set()
FINE = {(RO - 1, 1)}
F_ON_S = True

SCRATCH = {
    "Lw": ("sbuf", [128, W], f32), "Lb": ("sbuf", [128, W], bf), "Pw": ("sbuf", [128, W], bf),
    "Rw": ("sbuf", [128, V], bf), "Fd": ("sbuf", [128, V], bf), "Nw": ("sbuf", [128, V], i32),
    "E": ("sbuf", [128, V], f32), "YP": ("sbuf", [128, V], f32),
    "R": ("sbuf", [128, 288], i32), "Rh": ("sbuf", [128, 288], bf), "Rl": ("sbuf", [128, 288], bf),
    "S0L": ("sbuf", [128, GH], bf), "S0P": ("sbuf", [128, GH], bf),
    "SB": ("sbuf", [128, 4 * 2 * NG], f32), "ST": ("sbuf", [128, 2 * 7, 2 * NG], f32), "LN": ("sbuf", [128, CH], f32),
    "NM": ("sbuf", [128, 3 * H], u16), "DL": ("sbuf", [128, 3 * H], f16),
    "LO": ("sbuf", [128, 3 * H], bf), "HI": ("sbuf", [128, 3 * H], bf), "MN": ("sbuf", [128, 2 * H], i32),
    "NT": ("sbuf", [128, H], i32), "LT": ("sbuf", [128, H], i32),
    "TH": ("sbuf", [128, 5 * 2 * CH], bf), "MASK": ("sbuf", [128, MP], bf),
    "ROW": ("sbuf", [128, 256], bf), "ROWG": ("sbuf", [128, 128], bf), "VR": ("sbuf", [128, CH], bf),
    "JR": ("sbuf", [128, 128], i32), "HQ": ("sbuf", [128, CH], f32),
    "IP": ("sbuf", [128, 4], i32), "IT": ("sbuf", [128, 32], i32), "C": ("sbuf", [128, 64], f32),
    "TG": ("sbuf", [128, 16], f32), "BS": ("sbuf", [128, 16], f32), "QT": ("sbuf", [128, 16], f32),
    "PT": ("sbuf", [128, 16], f32), "PJ": ("sbuf", [128, 8], f32), "VT": ("sbuf", [128, 64], f32),
    "Dm": ("sbuf", [128, 8 * 128], bf), "Km": ("sbuf", [128, 8 * 128], bf), "Xb": ("sbuf", [128, NP * XS], bf),
    "Bm": ("sbuf", [128, 8 * 128], bf), "Fm": ("sbuf", [128, 5 * 128], f32), "Pm": ("sbuf", [128, 6 * 128], bf),
    "ZR": ("sbuf", [128, 160], bf), "WI": ("sbuf", [128, 160], bf),
    "Wb": ("sbuf", [128, 4 * 144], bf), "KK": ("sbuf", [128, U + CH], f16),
    "CK": ("sbuf", [128, 2 * CH], bf), "KB": ("sbuf", [128, CH], bf),
    "GD": ("sbuf", [128, H], f32), "CT": ("sbuf", [128, 96], f32), "CO": ("sbuf", [128, 32], u16),
    "X": ("sbuf", [128, NP * XS], f32), "D": ("sbuf", [128, (NP + 2) * MP], f32), "G": ("sbuf", [128, NP * MP], bf),
    "Wp": ("sbuf", [128, 2 * 136], bf), "VI": ("sbuf", [128, U], f32), "V2": ("sbuf", [128, 2 * U], f16),
    "SG": ("sbuf", [128, 8 * CH], bf), "VAL": ("sbuf", [128, 2 * H], bf), "RS": ("sbuf", [128, 2 * CH], f32),
    "pA0": ("psum", [128, 512], f32), "pA1": ("psum", [128, 512], f32), "pB": ("psum", [128, 512], f32),
    "pE": ("psum", [128, 512], f32), "pD": ("psum", [128, 1024], f32), "pM": ("psum", [128, 1024], f32),
}
for _n, _d in (("SN", u16), ("OF", u16), ("N16", f16), ("RR", bf), ("A16", f16), ("POW", bf), ("F", bf), ("EA", f16),
               ("HB", bf), ("TOP", f32)):
    SCRATCH[_n] = ("sbuf", [128, H], _d)
NDMA = 32
SEMAPHORES = ["cv", "cs", "ct", "cg", "left", "arL", "arP"] + ["ar%d" % _b for _b in range(4)] + \
             ["d%d" % _b for _b in range(NDMA)]

CYC = 0.83
PCYC = [0.42, 0.52, 0.42]
GAM = 1.56
VO, SO = 55.0, 80.0
SCEN = [(VO, GAM), (VO, 1.15), (VO, 1.95)]
LAT_X, LAT_S = 160.0, 90.0
LAT_P, LAT_L, LAT_R = 5000.0, 14000.0, 16000.0


def masks(topo, T, src):
    far = [c for c in T.cores if topo.chip(c) != topo.chip(src)]
    near = [c for c in T.cores if c != src and topo.chip(c) == topo.chip(src)]
    fe = topo.engines(src, far[0])
    ne = [e for e in topo.engines(src, near[0]) if e not in fe]
    return far, near, fe, ne


def build(g, core, T, topo):
    rank = T.rank_of(core)
    ops = []
    lastw, readers, lastbank = {}, {}, {}
    ndma = [0]
    alias = {}

    def op(eng, cost, fn, r=(), w=(), banks=(), sem=None, val=0, lat=0.0, after=()):
        me = len(ops)
        r, w, banks = [[alias.get(k, k) for k in x] for x in (r, w, banks)]
        hard, soft = set(after), set()
        for k in r:
            if k in lastw: hard.add(lastw[k])
        for k in w:
            for o in readers.get(k, []) + ([lastw[k]] if k in lastw else []):
                if eng == "t" and ops[o]["eng"] == "t": soft.add(o)
                else: hard.add(o)
        for b in banks:
            for e, o in lastbank.setdefault(b, {}).items():
                (soft if e == eng else hard).add(o)
            lastbank[b][eng] = me
        for k in r: readers.setdefault(k, []).append(me)
        for k in w:
            lastw[k] = me
            readers[k] = []
        if not isinstance(cost, list): cost = [cost] * len(SCEN)
        ops.append({"eng": eng, "cost": cost[0], "costs": cost, "fn": fn, "hard": hard, "soft": soft - hard, "sem": sem,
                    "val": val, "lat": lat, "name": w[-1] if w else None})
        return me

    def vcost(n, f=1.0):
        if f == GAM: return [50 + n * ga * CYC for vo, ga in SCEN]
        return [vo + max(64, n * f) * CYC for vo, ga in SCEN]

    def ts(out, in0, s1, s2, o0, o1, n, r, w, banks=(), f=1.0):
        if o1 is None:
            return op("v", vcost(n, f), lambda: g.vector.tensor_scalar(out, in0, s1, None, o0), r, w, banks)
        return op("v", vcost(n, f), lambda: g.vector.tensor_scalar(out, in0, s1, s2, o0, o1), r, w, banks)

    def tt(out, a, b, o, n, r, w, banks=(), f=None):
        if f is None: f = 1.0 if banks else 2.0
        return op("v", vcost(n, f), lambda: g.vector.tensor_tensor(out, a, b, o), r, w, banks)

    def cp(out, a, n, r, w, banks=(), f=1.0):
        return op("v", vcost(n, f), lambda: g.vector.tensor_copy(out, a), r, w, banks)

    def ms(out, c, n, w, r=()):
        return op("v", vcost(n), lambda: g.vector.memset(out, c), r, w)

    def act(out, a, func, n, r, w, banks=(), f=1.0, bias=None, scale=None):
        kw = {}
        if bias is not None: kw["bias"] = bias
        if scale is not None: kw["scale"] = scale
        cost = [SO + n * (ga if f == GAM else f) * CYC for vo, ga in SCEN]
        return op("s", cost, lambda: g.scalar.activation(out, a, func, **kw), r, w, banks)

    def mm(items, r, w, banks):
        def fn():
            ins = None
            for o, l, x, st, sp, _ in items:
                ins = g.tensor.matmul(o, l, x, st, sp)
            return ins
        return op("t", [30 + sum(max(64, it[5]) for it in items) * pc for pc in PCYC], fn, r, w, banks)

    def grp(out, pairs, n, first=True, last=True):
        return [(out, l, x, first and i == 0, last and i == len(pairs) - 1, n) for i, (l, x) in enumerate(pairs)]

    def gcopy(out, a, n, r, w):
        return op("g", 170 + 2 * n * CYC, lambda: g.affine_select(out, a, [[0, n]], A.is_ge, 0.0, 0, 0), r, w)

    def iota(out, pat, base, cm, n, w, flag):
        if flag:
            return op("g", 130 + 2 * n * CYC,
                      lambda: g.iota(out, pat, base, cm, allow_small_or_imprecise_dtypes=True), (), w)
        return op("g", 130 + 2 * n * CYC, lambda: g.iota(out, pat, base, cm), (), w)

    def dma(pairs, r, w, lat=2200.0, eng="y"):
        sem = T.sem["d%d" % ndma[0]]
        ndma[0] += 1
        q = g.sync if eng == "y" else g.scalar

        def fn():
            for o, a in pairs:
                (g.dma_start(o, a, accum_op=A.add) if eng == "g" else q.dma_start(o, a)).then_inc(sem, 16)
        return op(eng, (1000.0 if eng == "g" else 60.0) * len(pairs), fn, r, w, sem=sem, val=16 * len(pairs), lat=lat)

    far, near, fe, ne = masks(topo, T, core)
    nleft = [0]
    sent = []

    def send(src, dst_of, sem, r, w, lat, parts=((far, fe), (near, ne))):
        trs = []
        for cores, en in parts:
            ids = [DstId(rid=topo.addr(c)[0], pnc=topo.addr(c)[1]) for c in cores]
            ds = [dst_of((T.rank_of(c) - rank) % N) for c in cores]
            trs.append(RemoteDMATransfer(dst_ids=ids, dma_engine_mask=sum(1 << e for e in en), remote_sem=sem,
                                         srcs=[src], dsts=ds))
            nleft[0] += len(en)

        def fn():
            g.remote_dma_fused(trs, local_sem=T.sem.left)
        s = op("g", 400.0, fn, r, (), sem=T.sem.left, val=-1, lat=0.0)
        ops[s]["soft"] |= set(sent)
        sent.append(s)
        if not w: return s
        got = 0
        for c in T.cores:
            if c != core:
                cf, cn, cfe, cne = masks(topo, T, c)
                got += len(cfe) if core in cf else len(cne)
        return op("x", 0.0, None, (), w, sem=sem, val=got, lat=lat, after=[s])

    col = lambda j: T.C[:, j:j + 1]
    (PF, PM, G16, G15, M01, NM01, M0, OCOL, CC, WC, SH, M1, PM3, J3, PI, I1, I2, I12, L15, P64, PIV, MG1, MG2,
     SUB, CKC, M02, KC, KBC, HS, HBI, P2) = range(31)
    tmp = list(range(31, 64))
    sc = lambda x: col(x[0]) if isinstance(x, tuple) else x

    def cs(out, a, s1, s2, o0, o1=None):
        if out is None: out = tmp.pop()
        ts(col(out), col(a), sc(s1), sc(s2), o0, o1, 1, [a] + [x[0] for x in (s1, s2) if isinstance(x, tuple)], [out])
        return out

    def ln(out, a, s, b=0.0):
        if out is None: out = tmp.pop()
        act(col(out), col(a), AF.Identity, 1, [a] + [x[0] for x in (s, b) if isinstance(x, tuple)], [out],
            scale=sc(s), bias=sc(b))
        return out

    def scaled(out, a, s, n, r, w):
        act(out, a, AF.Identity, n, r + ([s[0]] if isinstance(s, tuple) else []), w, scale=sc(s))

    def diag(out, c, n, base, w):
        op("g", 170 + 2 * n * CYC, lambda: g.affine_select(out, T.ZR[:, 0:n], [[-1, n]], A.not_equal, c, base, 1),
           ["ZR"], w)

    pd = lambda bank, a, n: T.pD[:, 512 * int(bank[1]) + a:512 * int(bank[1]) + a + n]
    every = range(NP)
    ks = lambda name, js: [(name, j) for j in js]
    kc = lambda name, c, js: [(name, c, j) for j in js]
    own = lambda name: [(name, c, j) for c in range(3) for j in every]
    Lk, Pk = own("L") + ks("Lg", range(3)), own("P") + ks("Pg", range(3))

    dma([(T.R[0:112, 96:192], T.ph0[1:8, :]), (T.R[112:128, 96:192], T.ph0[0:1, :]), (T.R[:, 0:96], T.ph0[:, :])],
        (), ["Rph"])
    dma([(T.S0L[0:112, :], T.loud[16:128, 0:GH]), (T.S0L[112:128, :], T.loud[0:16, 0:GH])], (), ["S0L"], eng="s")
    dma([(T.Nw[:, :], T.nb[:, :])], (), own("N"), lat=3200.0, eng="s")
    dma([(T.R[:, 192:288], T.rb[:, :])], (), ["Rrb"])
    dma([(T.Lb[:, 0:V], T.loud[:, :])], (), ["Lb"], lat=3000.0)
    dma([(T.Fd[:, :], T.fade[:, :])], (), ["Fd"], lat=3000.0)
    lghost = lambda d: T.Lb[:, V + (d - 1) * GH:V + d * GH]
    send(T.S0L[:, :], lghost, T.sem.arL, ["S0L"], (), 0.0, [(near, ne)])

    iota(T.IP[:, 0:1], [[0, 1]], 0, 1, 1, ["IP"], False)
    iota(T.ROW[:, :], [[1, 256]], 0, 0, 256, ["ROW"], True)
    iota(T.ROWG[:, :], [[16, 8], [0, 16]], 0, 0, 128, ["ROWG"], True)
    iota(T.IT[:, 0:16], [[-1, 16]], 16, 1, 16, ["IT"], False)
    iota(T.VT[:, :], [[1, 2], [48, 32]], -V, 0, 64, ["VT"], True)
    iota(T.JR[:, :], [[48, 8], [1, 16]], 0, 0, 128, ["JR"], False)
    iota(T.VR[:, :], [[0, CH // U], [1, U]], 0, 0, CH, ["VR"], True)
    iota(T.VI[:, :], [[U + 1, 2], [2, U // 2]], 0, 0, U, ["VI"], True)
    ts(T.IP[:, 1:2], T.IP[:, 0:1], 15, None, A.bitwise_and, None, 1, ["IP"], ["IP1"])
    cp(col(PM), T.IP[:, 1:2], 1, ["IP1"], [PM])
    cp(col(PF), T.IP[:, 0:1], 1, ["IP"], [PF])
    blk = lambda t, j, n=128: t[:, n * j:n * j + n]
    ms(T.ZR[:, :], 0.0, 80, ["ZR"])
    diag(T.WI[:, :], 1.0, 160, 16, ["Ib"])
    Ib = T.WI[:, 16:144]
    ln(G16, PM, -1.0, (PF,))
    ts(T.QT[:, :], T.ROW[:, 0:16], col(PM), None, A.is_equal, None, 16, ["ROW", PM], ["QT"])
    for s in range(16):
        act(T.Xb[:, 136 * s:136 * s + 130], T.WI[:, 15 + s:145 + s], AF.Identity, 130, ["Ib", "QT"], [("Q", s)],
            scale=T.QT[:, s:s + 1])
    Qhi = lambda s: T.Xb[:, 136 * s + 1:136 * s + 129]
    Qlo = lambda s: T.Xb[:, 136 * s:136 * s + 128]
    for k, s in ((M0, 0), (M1, 1), (M02, 2), (L15, 15)):
        act(col(k), T.QT[:, s:s + 1], AF.Copy, 1, ["QT"], [k])
    ln(G15, G16, 1.0, 15.0)
    ln(M01, M0, 1.0, (M1,))
    ln(NM01, M01, -1.0)
    ln(OCOL, PM, 1.0, 16.0 - 8192.0)
    ln(PM3, PM, 3.0)
    act(T.VT[:, :], T.VT[:, :], AF.Identity, 64, ["VT", PM3], ["VT"], bias=col(PM3))
    ts(T.PT[:, :], T.ROW[:, 0:16], col(PM), 1.0, A.is_lt, A.add, 16, ["ROW", PM], ["PT"])
    op("v", vcost(16), lambda: g.vector.tensor_reduce(col(P2), T.PT[:, :], AxisListType.X, A.mult), ["PT"], [P2])
    ln(WC, ln(None, M0, 0.5, (P2,)), 2.0 ** 30)
    ln(SH, cs(None, PF, 16.0, 128.0, A.is_lt, A.mult), 1.0, (ln(None, PF, 1.0, -16.0),))
    ln(KC, M0, 15.5 - 13072.0, 13072.0)
    ln(KBC, M02, OFF / 64.0)
    ln(HBI, M02, -511.5)
    ln(HS, M1, 1.0, (M02,))
    ts(T.IP[:, 2:3], col(PM), 1.0 / 3.0, -1.0 / 3.0, A.mult, A.add, 1, [PM], ["IP2"])
    ts(col(J3), T.IP[:, 2:3], 3.0, None, A.mult, None, 1, ["IP2"], [J3])
    ln(PI, J3, -1.0, (PM,))
    cs(I1, PI, 1.0, None, A.is_equal)
    cs(I2, PI, 2.0, None, A.is_equal)
    ln(I12, I1, 1.0, (I2,))
    for out, k in ((P64, 64.0), (PIV, 1.0 / 64.0)):
        ln(out, L15, k ** 3 - 1.0, (ln(None, I2, k ** 2 - 1.0, (ln(None, I1, k - 1.0, 1.0),)),))
    a = ln(None, L15, 2.0 ** 22, 2.0 ** 23)
    ln(MG2, a, (P64,))
    ln(MG1, ln(None, I12, -0.5, (a,)), (P64,))
    ln(SUB, ln(None, I12, -64.0), (PIV,))
    ln(CKC, ln(None, I2, 64.0, (ln(None, ln(None, J3, 1.0, 0.5), (I12,)),)), -1.0 / 64.0)
    a = ln(None, L15, -16.0, (ln(None, ln(None, I12, -1.0, 1.0), (J3,), 1.0),))
    ln(CC, ln(None, ln(None, J3, -64.0, 64.0 * 13.0), (I2,), (a,)), -65.0)
    ts(T.IT[:, 16:32], T.IT[:, 0:16], 15, None, A.bitwise_and, None, 16, ["IT"], ["IT1"])
    ts(T.TG[:, :], T.IT[:, 16:32], col(G16), None, A.add, None, 16, ["IT1", G16], ["TG"])
    ts(T.BS[:, :], T.ROW[:, 0:16], col(PM), 16.0, A.add, A.is_ge, 16, ["ROW", PM], ["BS"])
    act(T.BS[:, :], T.BS[:, :], AF.Identity, 16, ["BS"], ["BS"], bias=-0.5)
    r128 = T.ROW[:, 0:128]
    S01, N01, Wm, Shb, BD, Inq, Ie, Inb = [blk(T.Bm, j) for j in range(8)]
    If, Shf, Iq, S2l, S2h = [blk(T.Fm, j) for j in range(5)]
    I64b = blk(T.Km, 7)
    scaled(I64b, Ib, 64.0, 128, ["Ib"], [("K", 8)])
    for m, c, k in ((If, 1.0, "If"), (Inq, -0.25, "Inq"), (Iq, 0.25, "Iq"), (Ie, 0.125, "Ie"), (Inb, -1.0, "Inb")):
        diag(m, c, 128, 0, [k])
    ts(Shb, r128, col(SH), None, A.is_equal, None, 128, ["ROW", SH], ["Shb"], f=0.5)
    gcopy(Shf, Shb, 128, ["Shb"], ["Shf"])
    ts(BD, T.ROWG[:, :], col(G16), None, A.is_equal, None, 128, ["ROWG", G16], ["BD"], f=0.5)
    for m, c, k in ((S01, M01, "S01"), (N01, NM01, "N01"), (Wm, WC, "Wm")):
        scaled(m, BD, (c,), 128, ["BD"], [k])
    for j, (dst, k, ss) in enumerate(((T.Dm, "Dm", (1, 2, 3, 4)), (T.Dm, "Dm", (5, 6, 7, 8)),
                                      (T.Km, "K", (1, 2, 3, 4)), (T.Km, "K", (5, 6, 7)))):
        bank, its = "D%d" % (j % 2), []
        for i, s in enumerate(ss):
            u = s if k == "Dm" else 16 - s
            ts(blk(T.TH, 4 * j + i), r128, T.TG[:, u:u + 1], -64.0, A.is_equal, A.mult, 128, ["ROW", "TG"],
               [("sh", j, i)], f=0.5)
            its += grp(pd(bank, 128 * i, 128), [(Ib, blk(T.TH, 4 * j + i)), (Ib, I64b)], 128)
        mm(its, ["Ib", ("K", 8), ("TH", j)] + [("sh", j, i) for i in range(len(ss))], ["p" + bank], [bank])
        n = 128 * len(ss)
        act(dst[:, 128 * (ss[0] - 1):128 * ss[-1]], pd(bank, 0, n), AF.Copy, n, ["p" + bank], [(k, s) for s in ss],
            [bank])
    scaled(S2l, Ib, (PIV,), 128, ["Ib"], ["S2l"])
    scaled(S2h, T.WI[:, 17:145], (SUB,), 128, ["Ib"], ["S2h"])
    tt(S2l, S2l, S2h, A.add, 128, ["S2l", "S2h"], ["S2l"])
    scaled(S2h, S2l, 64.0, 128, ["S2l"], ["S2h"])
    ts(T.JR[:, :], T.JR[:, :], 1.0 / 3.0, -1.0 / 3.0, A.mult, A.add, 128, ["JR"], ["JR"])
    act(T.PJ[:, :], T.ROW[:, 0:8], AF.Identity, 8, ["ROW", G16], ["PJ"], bias=col(G16))
    for j in range(6):
        w_ = 1.0 / UNIT[3 * min(j, 4)]
        ts(blk(T.Pm, j), T.JR[:, :], T.PJ[:, j:j + 1], w_ if j else math.sqrt(w_), A.is_equal, A.mult, 128,
           ["JR", "PJ"], [("Pm", j)])
    scaled(blk(T.Pm, 0), blk(T.Pm, 0), math.sqrt(1.0 / UNIT[0]), 128, [("Pm", 0)], [("Pm", 0)])
    tt(blk(T.Pm, 4), blk(T.Pm, 4), blk(T.Pm, 5), A.subtract, 128, [("Pm", 4), ("Pm", 5)], [("Pm", 4)])
    ts(blk(T.Wb, 0, 144), T.ROW[:, 0:144], col(G15), None, A.is_equal, None, 144, ["ROW", G15], ["Cw"], f=0.5)
    for j, c, k in ((1, (M01,), "Cw01"), (2, 2.0, "Cw2"), (3, (M0,), "Cw0")):
        scaled(blk(T.Wb, j, 144), blk(T.Wb, 0, 144), c, 144, ["Cw"], [k])
    ts(T.IP[:, 3:4], col(PM), 0.5, -0.25, A.mult, A.add, 1, [PM], ["IP3"])
    half = tmp.pop()
    ts(col(half), T.IP[:, 3:4], 8.0, col(G16), A.add, A.add, 1, ["IP3", G16], [half])
    odd = tmp.pop()
    ts(col(odd), T.IP[:, 3:4], -2.0, col(PM), A.mult, A.add, 1, ["IP3", PM], [odd])
    for par, w_ in ((0, ln(None, odd, -64.0, 64.0)), (1, ln(None, odd, 64.0))):
        ts(blk(T.Wp, par, 136), T.ROW[:, 0:136], col(half), col(w_), A.is_equal, A.mult, 136, ["ROW", half, w_],
           [("Wp", par)], f=0.5)
        ts(blk(T.V2, par, U), T.VI[:, :], par / 16.0, None, A.add, None, U, ["VI"], [("V2", par)])
    OC2 = ln(None, PM, 2.0, 16.0 - 8192.0)
    wide = lambda j, k: T.Wb[:, 144 * j + 15 - k:144 * j + 143 - k]
    ts(T.KK[:, 0:U], T.ROW[:, 0:U], 0.0, col(KC), A.mult, A.add, U, ["ROW", KC], ["K1"], f=0.5)
    ms(T.KK[:, U:U + CH], 511.5, CH // 2, ["K2"])
    act(T.KB[:, :], T.ROW[:, 0:CH], AF.Identity, CH, ["ROW", KBC], ["KB"], scale=0.0, bias=col(KBC))
    for j in range(2):
        act(blk(T.CK, j, CH), T.ROW[:, 0:CH], AF.Identity, CH, ["ROW", CKC], [("CK", j)], scale=0.0, bias=col(CKC))
    ms(T.MASK[:, :], 1.0, MP // 2, ["MASK"])
    ms(T.MASK[:, 0:MP:16], 0.0, U, ["MASK"], ["MASK"])
    for j in every:
        iota(T.X[:, XS * j:XS * j + 16], [[0, 16]], 0, 0, 16, [("Xf", j)], True)

    cp(T.Rh[:, 0:192], T.R[:, 0:192], 192, ["Rph"], ["Rh"])
    tt(T.Rl[:, 0:192], T.R[:, 0:192], T.Rh[:, 0:192], A.subtract, 192, ["Rph", "Rh"], ["Rl"])
    its = []
    for s, n in ((0, 96), (1, 96), (2, 48)):
        its += grp(T.pB[:, 96 * s:96 * s + n], [(Qhi(s), T.Rh[:, 96:96 + n]), (Qlo(s), T.Rl[:, 96:96 + n])], n)
    mm(its, ["Rh", "Rl"] + [("Q", s) for s in range(3)], ["Bl"], ["B"])
    act(T.S0P[:, :], T.pB[:, 0:GH], AF.Copy, GH, ["Bl"], ["S0P"], ["B"])
    send(T.S0P[:, :], lambda d: T.Pw[:, V + (d - 1) * GH:V + d * GH], T.sem.arP, ["S0P"], ks("Pg", range(3)), LAT_P)
    send(T.S0L[:, :], lghost, T.sem.arL, ["S0L"], ["Lbg"], LAT_L, [(far, fe)])
    cp(T.Rh[:, 192:288], T.R[:, 192:288], 96, ["Rrb"], ["Rh2"])
    tt(T.Rl[:, 192:288], T.R[:, 192:288], T.Rh[:, 192:288], A.subtract, 96, ["Rrb", "Rh2"], ["Rl2"])
    for o, dst, rk, keys in ((0, T.Pw, ["Rh", "Rl"], own("P")), (192, T.Rw, ["Rh2", "Rl2"], ["Rw"])):
        for j in range(4):
            bank = ("D0", "D1")[j % 2]
            its = []
            for s in range(4 * j, 4 * j + 4):
                its += grp(pd(bank, 96 * (s % 4), 96),
                           [(Qhi(s), T.Rh[:, o:o + 96]), (Qlo(s), T.Rl[:, o:o + 96])], 96)
            mm(its, rk + [("Q", s) for s in range(4 * j, 4 * j + 4)], ["p" + bank], [bank])
            kw = [("init", o, j)] + (keys if j == 3 else [])
            kr = ["p" + bank] + ([("init", o, i) for i in range(3)] if j == 3 else [])
            act(dst[:, 384 * j:384 * j + 384], pd(bank, 0, 384), AF.Copy, 384, kr, kw, [bank])
    for j in every:
        iota(T.Xb[:, XS * j:XS * j + 16], [[0, 16]], 0, 0, 16, (ks("Q", range(16)) if j < 3 else []) + [("X", j), ("Xz", j)],
             True)
    for c in range(2):
        gcopy(T.MN[:, H * c:H * (c + 1)], T.Nw[:, c:V:3], H, kc("N", c, every), [("MN", c)])
    gcopy(T.Lw[:, 0:V], T.Lb[:, 0:V], V, ["Lb"], own("L"))
    gcopy(T.Lw[:, V:W], T.Lb[:, V:W], W - V, ["Lbg"], ks("Lg", range(3)))

    def span(t, js):
        c, v, n = t % 3, U * js[0], U * len(js)
        return c, v, n, slice(v, v + n), slice(c + 3 * v, 3 * (v + n), 3)

    def derive(t, js):
        c, v, n, us, vs = span(t, js)
        src, sl, nt, lt = T.Nw[:, vs], slice(H * c + v, H * c + v + n), T.NT[:, us], T.LT[:, us]
        k = lambda name: kc(name, c, js)
        ts(nt, src, 4095, None, A.bitwise_and, None, n, k("N"), ks("NT", js))
        cp(T.NM[:, sl], nt, n, ks("NT", js), k("NM"))
        ts(T.DL[:, sl], src, 2.0 ** -12, 1024.6, A.mult, A.add, n, k("N"), k("DL"))
        ts(T.HI[:, sl], T.NM[:, sl], 2.0 ** -6, 128.0 + 65.0 / 128.0, A.mult, A.add, n, k("NM"), k("HI"), f=0.5)
        act(T.HI[:, sl], T.HI[:, sl], AF.Identity, n, k("HI"), k("HI"), bias=-128.0)
        ts(lt, src, 63, None, A.bitwise_and, None, n, k("N"), ks("LT", js))
        gcopy(T.LO[:, sl], lt, n, ks("LT", js), k("LO"))
        act(T.LO[:, sl], T.LO[:, sl], AF.Identity, n, k("LO"), k("LO"), bias=1.0)

    for t in range(3): derive(t, list(every))

    def pick(on_v, out, win, r, w):
        if on_v: cp(out, win, MP, r, w, f=GAM)
        else: act(out, win, AF.Copy, MP, r, w, f=GAM)

    def front(t, js, z):
        c, v, n, us, vs = span(t, js)
        bA = "A%d" % z
        pA = T["p" + bA]
        lo, hi = pA[:, 0:n], pA[:, 256:256 + n]
        o = H * c + v
        RR, A16, VAL, RS = T.RR[:, us], T.A16[:, us], T.VAL[:, 2 * v:2 * (v + n)], T.RS[:, 0:2 * n]
        for j in js:
            oj = H * c + U * j
            pick((t, j) in P_ON_V, T.G[:, MP * j:MP * (j + 1)], T.Pw[:, 0:W].indirect(T.NM[:, oj:oj + U]),
                 Pk + [("NM", c, j)], [("IND", j)])
            pairs = [(wide(1, k), T.G[:, MP * j + k:MP * (j + 1):16]) for k in range(16)]
            pairs += [(Ib, T.DL[:, oj:oj + U]), (BD, T.KK[:, 0:U]), (N01, T.Pw[:, span(t, [j])[4]])]
            mm(grp(pA[:, U * j - v:U * (j + 1) - v], pairs, U),
               [("IND", j), "Cw01", "Ib", "BD", ("DL", c, j), "K1", "N01", ("P", c, j)], [bA + "l"], [bA])
        act(RR, lo, AF.Copy, n, [bA + "l"], ks("RR", js), [bA])
        tt(A16, lo, RR, A.subtract, n, [bA + "l"] + ks("RR", js), ks("A16", js), [bA])
        per = 512 // n
        SG = lambda s, m=1: T.SG[:, CH * (s - 1):CH * (s - 1) + n * m]
        sk = lambda s: [("SG", s)]
        for i, s0 in enumerate(range(1, 9, per)):
            bank, ss, its = ("D0", "D1")[i % 2], range(s0, min(s0 + per, 9)), []
            for s in ss:
                its += grp(pd(bank, n * (s - s0), n), [(blk(T.Dm, s - 1), A16)], n)
            mm(its, ks("A16", js) + ks("Dm", ss), ["p" + bank], [bank])
            for s in ss:
                act(SG(s), pd(bank, n * (s - s0), n), AF.Sign, n, ["p" + bank, "BS"], sk(s), [bank], bias=T.BS[:, s:s + 1])
        for i in range(2):
            ss = range(4 * i + 1, 4 * i + 5)
            mm(grp(hi, [(blk(T.Km, s - 1), SG(s)) for s in ss], n, i == 0, i == 1),
               sum([sk(s) for s in ss], []) + ks("K", ss), [bA + "h"], [bA])
        act(lo, hi, AF.Sigmoid, n, [bA + "h"], [bA + "l"], [bA],
            bias=-59.0 * math.log(2.0), scale=6.0 * math.log(2.0) / 128.0)
        tt(T.VAL[:, 2 * v:2 * v + n], lo, T.LO[:, o:o + n], A.mult, n, [bA + "l"] + kc("LO", c, js), ks("VL", js), [bA])
        tt(T.VAL[:, 2 * v + n:2 * (v + n)], lo, T.HI[:, o:o + n], A.mult, n, [bA + "l"] + kc("HI", c, js), ks("VH", js), [bA])
        act(T.POW[:, us], hi, AF.Sigmoid, n, [bA + "h"], ks("POW", js), [bA],
            bias=-37.5 * math.log(2.0), scale=-math.log(2.0) / 128.0)
        vk = ks("VL", js) + ks("VH", js)
        bank, pS, sk_ = ("B", T.pB[:, 0:2 * n], ["Bl", "Bh"]) if v == 0 else ("D1", pd("D1", 0, 2 * n), ["pD1"])
        mm(grp(pS, [(I64b, T.CK[:, 0:2 * n])], 2 * n, True, False), [("K", 8), ("CK", 0), ("CK", 1)], sk_, [bank])
        mm(grp(pS, [(blk(T.Pm, 5), VAL)], 2 * n, False, False), vk + [("Pm", 5)], sk_, [bank])
        for i in range(5):
            th = T.TH[:, 2 * CH * i:2 * CH * i + 2 * n]
            ts(th, VAL, UNIT[3 * i], UNIT[3 * i + 3], A.max, A.min, 2 * n, vk, [("TH", i)], f=0.5)
            mm(grp(pS, [(blk(T.Pm, i), th)], 2 * n, False, i == 4), [("TH", i), ("Pm", i)], sk_, [bank])
        ts(RS, pS, col(MG1), col(MG2), A.add, A.subtract, 2 * n, sk_ + [MG1, MG2], ["RS"], [bank])
        mm(grp(lo, [(S2h, T.RS[:, n:2 * n]), (S2l, T.RS[:, 0:n])], 4 * n), ["RS", "S2l", "S2h"], [bA + "l"], [bA])
        ts(T.SN[:, us], lo, col(CC), None, A.add, None, n, [bA + "l", CC], ks("SN", js), [bA])

    def first(t):
        c, n = t % 3, H // 16
        ts(T.N16[:, :], T.SN[:, :], float(V), None, A.min, None, H, ks("SN", every), ["N16"], f=0.5)
        p = T.pE[:, 256:256 + n]
        mm(grp(p, [(wide(3, i), T.N16[:, i:H:16]) for i in range(16)], n), ["N16", "Cw0"], ["Eh"], ["E"])
        ts(T.CT[:, 0:n], p, float(V), None, A.is_equal, None, n, ["Eh"], ["CT"], ["E"])
        tt(T.CT[:, n:2 * n], T.CT[:, 0:n], T.VT[:, n * c:n * (c + 1)], A.mult, n, ["CT", "VT"], ["CT1"])
        tt(T.CT[:, 2 * n:3 * n], p, T.CT[:, n:2 * n], A.add, n, ["Eh", "CT1"], ["CT2"], ["E"])
        cp(T.CO[:, :], T.CT[:, 2 * n:3 * n], n, ["CT2"], ["CO"])
        tt(T.GD[:, :], T.Nw[:, 0:V].indirect(T.CO[:, :]), T.MN[:, H * c:H * (c + 1)], A.subtract, H,
           own("N") + ["CO", ("MN", c)], ["GD"], f=GAM)

    xp = lambda t, j, a, b=XS, s=1: (T.X if t else T.Xb)[:, XS * j + a:XS * j + b:s]

    room = list(range(NP // 2 + 1))
    slot = lambda j: 2 * room[j // 2] + j % 2

    def gather(t, js):
        win, keys = (T.Lb, ["Lb", "Lbg"]) if t == 0 else (T.Lw, Lk)
        for j in js:
            pick((t, j) in L_ON_V, xp(t, j, 16), win[:, 0:W].indirect(T.SN[:, U * j:U * (j + 1)]), keys + [("SN", j)], [("X", j)])

    def back(t, js, z, fine):
        c, v, n, us, vs = span(t, js)
        bA = "A%d" % z
        pA = T["p" + bA]
        top = pA[:, 256:256 + n]
        alias.clear()
        if (t, js[0]) in B_IN_D: alias.update({"B": "D1", "Bl": "pD1", "Bh": "pD1h"})
        pb = lambda a, m: pd("D1", a, m) if alias else T.pB[:, a:a + m]
        lo, hi = pb(0, n), pb(256, n)

        def mask(part):
            m, sl, ps = U * len(part), span(t, part)[3], slice(U * part[0] - v, U * (part[-1] + 1) - v)
            if F_ON_S: act(T.F[:, sl], pb(ps.start, m), AF.Sigmoid, m, ["Bl"], ks("F", part), ["B"], bias=1300.0, scale=100.0)
            else: ts(T.F[:, sl], pb(ps.start, m), -13.0, None, A.is_ge, None, m, ["Bl"], ks("F", part), ["B"])
            if (t, part[0]) in SPLIT:
                its, oc = [], OC2
                for a in range(0, m, 2 * U):
                    for par in range(2):
                        b = ps.start + a + U * par
                        its += grp(pA[:, b:b + U], [(Ie, blk(T.V2, par, U))] + [
                            (T.Wp[:, 136 * par + 8 - 8 * h:136 * par + 136 - 8 * h],
                             T.F[:, sl.start + a + h:sl.start + a + 2 * U:2]) for h in range(2)], U)
            else:
                its, oc = grp(pA[:, ps], [(I64b, T.F[:, sl]), (Ie, T.VR[:, 0:m])], m), OCOL
            mm(its, ks("F", part) + [("K", 8), "Ie", "VR"] + ks("Wp", range(2)) + ks("V2", range(2)), [bA + "l"], [bA])
            ts(T.OF[:, sl], pA[:, ps], 128.0, col(oc), A.mult, A.add, m, [bA + "l", oc], ks("OF", part), [bA])

        for j in js:
            pm, kM, bM = (T.pD, ["pD0", "pD1"], ["D0", "D1"]) if (t, j) in M_IN_D else (T.pM, ["M0", "M1"], ["M0", "M1"])
            o, M, kx = MP * j, pm[:, :], [("X", j)]
            d, ind, pj, dk = blk(T.D, slot(j), MP), T.G[:, o:o + MP], U * j - v, [("D", slot(j))]
            on_t = t == 0 and D_ON_T
            buf, mk, mb = (T.G, [("IND", j)], []) if on_t else (pm, kM, bM)
            mo = o if on_t else 0
            op("v", vcost(MP, 0.5 if on_t and t == 0 else 1.0), lambda j=j, m=buf[:, mo:mo + MP]: g.vector.tensor_tensor_scan(
                m, xp(t, j, 15, XS - 1), T.MASK[:, :], 0.0, A.max, A.mult), kx + ["MASK", ("Xf", j), ("Xz", j)], mk, mb)
            if not on_t: tt(d, xp(t, j, 16), M, A.subtract, MP, kx + kM, dk, bM)
            if t < 3:
                tt(T.TOP[:, U * j:U * (j + 1)], buf[:, mo + 15:mo + MP:16], xp(t, j, 31, XS, 16), A.max, U, kx + mk,
                   [("TOP", j)], mb)
            elif t < RO - 1:
                tt(pA[:, 256 + pj:256 + pj + U], buf[:, mo + 15:mo + MP:16], xp(t, j, 31, XS, 16), A.max, U, kx + mk,
                   [bA + "h"], mb + [bA], f=2.0 if on_t else 1.0)
            wk = 0
            if on_t:
                for i in range(2):
                    mm(grp(blk(pm, i, 512), [(Ib, xp(t, j, 16 + 512 * i, 528 + 512 * i)),
                                             (Inb, buf[:, o + 512 * i:o + 512 * (i + 1)])], 512),
                       kx + mk + ["Ib", "Inb"], [kM[i]], [bM[i]])
                if (t, j) in SIGN_S:
                    act(ind, M, AF.Sign, MP, kM, [("IND", j)], bM, bias=-2.0 ** -27)
                else:
                    ts(ind, M, 0.0, 0.5, A.is_gt, A.subtract, MP, kM, [("IND", j)], bM)
                    wk = 2
                act(d, M, AF.Sigmoid, MP, kM, dk, bM)
            elif (t, j) in SIGN_S:
                act(ind, d, AF.Sign, MP, dk, [("IND", j)], bias=-2.0 ** -27)
            else:
                gcopy(ind, d, MP, dk, [("IND", j)])
                ts(ind, ind, 0.0, 0.5, A.is_gt, A.subtract, MP, [("IND", j)], [("IND", j)], f=0.5)
                wk = 2
            mm(grp(pb(pj, U), [(wide(wk, k), T.G[:, o + k:o + MP:16]) for k in range(1, 16)], U),
               [("IND", j), "Cw", "Cw2"], ["Bl"], ["B"])
            if fine: mask([j])
        if not fine: mask(js)
        EA, HB, HQ = T.EA[:, us], T.HB[:, us], T.HQ[:, 0:n]
        mm(grp(hi, [(Wm, T.F[:, us])], n), ks("F", js) + ["Wm"], ["Bh"], ["B"])
        tt(hi, hi, T.POW[:, us], A.mult, n, ["Bh"] + ks("POW", js), ["Bh"], ["B"])
        ts(lo, hi, 2.0 ** 23 - 0.5, 2.0 ** 23 + 1.0, A.add, A.is_equal, n, ["Bh"], ["Bl"], ["B"])
        tt(EA, lo, T.A16[:, us], A.mult, n, ["Bl"] + ks("A16", js), ks("EA", js), ["B"])
        pairs = [(S01, T.Pw[:, vs]), (S01, T.Rw[:, vs]), (Ib, T.KK[:, U:U + n])] + ([(I64b, T.KB[:, 0:n])] if t >= 2 else [])
        mm(grp(lo, pairs + [(BD, EA)], n),
           ks("EA", js) + kc("P", c, js) + ["S01", "Rw", "Ib", "K2", "BD", "KB", ("K", 8)], ["Bl"], ["B"])
        act(HB, lo, AF.Identity, n, ["Bl", HS, HBI], ks("HB", js), ["B"], scale=col(HS), bias=col(HBI))
        ghosts = v == 0
        if t < RO - 1:
            tt(T.Pw[:, vs], lo, HB, A.subtract, n, ["Bl"] + ks("HB", js), kc("P", c, js), ["B"])
        if t >= 2:
            tt(T.YP[:, vs], lo, HB, A.subtract, n, ["Bl"] + ks("HB", js), kc("YP", c, js), ["B"])
        if t < RO - 1:
            if t < 3:
                Lo = T.Lb[:, vs]
                mm(grp(top, [(Iq, T.TOP[:, us])], 4 * n, True, False) + grp(top, [(Inq, Lo), (Ib, Lo)], n, False, True),
                   ks("TOP", js) + ["Lb", "Iq", "Inq", "Ib"], [bA + "h"], [bA])
            else:
                Lo, lk = T.Lw[:, vs], kc("L", c, js)
                tt(top, top, Lo, A.subtract, n, [bA + "h"] + lk, [bA + "h"], [bA])
                act(top, top, AF.Copy, n, [bA + "h"], [bA + "h"], [bA], scale=0.25)
                tt(top, top, Lo, A.add, n, [bA + "h"] + lk, [bA + "h"], [bA])
            if ghosts:
                tt(T.LN[:, 0:n], top, T.Fd[:, vs], A.mult, n, [bA + "h", "Fd"], ["LN"], [bA])
                gcopy(T.Lw[:, vs], T.LN[:, 0:n], n, ["LN"], kc("L", c, js))
                sb = blk(T.SB, t, 2 * NG)
                mm(grp(pA[:, 256:256 + NG], [(Shf, T.LN[:, 0:NG])], 4 * NG), ["LN", "Shf"], [bA + "h"], [bA])
                mm(grp(pA[:, 256 + NG:256 + 2 * NG], [(Shb, T.Pw[:, c:GH:3])], NG), kc("P", c, (0, 1)) + ["Shb"],
                   [bA + "h"], [bA])
                act(sb, pA[:, 256:256 + 2 * NG], AF.Copy, 2 * NG, [bA + "h"], [("SB", t)], [bA])
                send(sb, lambda d: T.ST[:, 7 * (t % 2) + d - 1, :], T.sem["ar%d" % t], [("SB", t)], [("ST", t % 2)], LAT_R)
            else:
                tt(T.Lw[:, vs], top, T.Fd[:, vs], A.mult, n, [bA + "h", "Fd"], kc("L", c, js), [bA])
        if t < 2:
            hid = T.pE[:, 256:256 + n]
            ts(HQ, hi, 1.5 * 2.0 ** 24, 1.5 * 2.0 ** 24, A.add, A.subtract, n, ["Bh"], ["HQ"], ["B"])
            tt(hid, hi, HQ, A.is_gt, n, ["Bh", "HQ"], ["Eh"], ["B", "E"])
            tt(hid, hid, T.GD[:, us], A.mult, n, ["Eh", "GD"], ["Eh"], ["E"])
            tt(T.Nw[:, vs], hid, T.Nw[:, vs], A.add, n, ["Eh"] + kc("N", c, js), kc("N", c, js), ["E"])

    def rest(t, js):
        c, v, n, us, vs = span(t, js)
        if t < 2: derive(t + 3, js)
        for j in js:
            o, dk = MP * slot(j), [("D", slot(j))]
            d = T.D[:, o:o + MP]
            if not (t == 0 and D_ON_T): act(d, d, AF.Sigmoid, MP, dk, dk)
            if (t, j - j % 2) not in SPLIT:
                tt(d, xp(t, j, 0).indirect(T.OF[:, U * j:U * (j + 1)]), d, A.mult, MP, dk + [("X", j), ("OF", j)], dk,
                   f=GAM)
                part, m, eg = [j], 16, EG
            elif j % 2 == 0:
                continue
            else:
                part, m, eg = [j - 1, j], 8, EG // 2
                a, b = 2 * room[j // 2], 2 * room[-1]
                for par in range(2):
                    tt(blk(T.D, b + par, MP), xp(t, j - 1, 0, 2 * XS).indirect(blk(T.OF, j - 1 + par, U)),
                       T.D[:, MP * a + par:MP * (a + 2):2], A.mult, MP,
                       ks("D", (a, a + 1)) + ks("X", part) + ks("OF", part), [("D", b + par)], f=GAM)
                dma([(blk(T.D, b, MP), blk(T.D, b + 1, MP))], ks("D", (b, b + 1)), [("D", b)], lat=LAT_A, eng="g")
                room[j // 2], room[-1] = room[-1], room[j // 2]
                o, dk = MP * b, [("D", b)]
            p, w_ = T.pE[:, U * part[0] - v:U * (part[-1] + 1) - v], 4 * U * len(part)
            if t >= 3:
                mm(grp(p, [(If, T.E[:, span(t, part)[4]])], w_, True, False), kc("E", c, part) + ["If"], ["El"], ["E"])
            for k0 in range(0, m, eg):
                mm(grp(p, [(If, T.D[:, o + k:o + MP:m]) for k in range(k0, k0 + eg)], w_,
                       k0 == 0 and t < 3, k0 + eg == m), dk + ["If"], ["El"], ["E"])
        act(T.E[:, vs], T.pE[:, 0:n], AF.Copy, n, ["El"], kc("E", c, js), ["E"])

    cut = lambda sizes: [list(range(sum(sizes[:q]), sum(sizes[:q + 1]))) for q in range(len(sizes))]
    for t in range(RO):
        c = t % 3
        for q, js in enumerate(cut(FRONTS[t])): front(t, js, q % 2)
        if t < 2: first(t)
        gather(t, every)
        rests = cut(RESTS[t])
        for q, js in enumerate(cut(BACKS[t])):
            back(t, js, BANK[t][q], (t, q) in FINE)
            alias.clear()
            while rests and rests[0][-1] <= js[-1]: rest(t, rests.pop(0))
        if t < RO - 1:
            u = 7 * (t % 2)
            gcopy(T.Pw[:, V + c:W:3], T.ST[:, u:u + 7, NG:2 * NG], 7 * NG, [("ST", t % 2)], [("Pg", c)])
            gcopy(T.Lw[:, V + c:W:3], T.ST[:, u:u + 7, 0:NG], 7 * NG, [("ST", t % 2)], [("Lg", c)])
    for js in cut(RESTS[RO - 1]):
        sl = slice(3 * U * js[0], 3 * U * (js[-1] + 1))
        dma([(T.yp[:, sl], T.YP[2:128:16, sl])], [("YP", c, j) for c in range(3) for j in js], (), lat=2500.0)
        dma([(T.ye[:, sl], T.E[:, sl])], [("E", c, j) for c in range(3) for j in js], (), lat=2800.0)
    return ops, nleft[0]


def schedule(ops):
    n = len(ops)
    succ = [[] for _ in range(n)]
    for i, o in enumerate(ops):
        for d in o["hard"]: succ[d].append((i, LAT_S if ops[d]["eng"] == o["eng"] else LAT_X))
        for d in o["soft"]: succ[d].append((i, 0.0))
    prio = [0.0] * n
    for i in range(n - 1, -1, -1):
        prio[i] = ops[i]["cost"] + ops[i]["lat"] + max([prio[j] + l for j, l in succ[i]] + [0.0])
    left = [len(o["hard"]) + len(o["soft"]) for o in ops]
    est = [0.0] * n
    free = {e: 0.0 for e in "vstgyx"}
    ready = {e: [] for e in free}
    for i in range(n):
        if left[i] == 0: ready[ops[i]["eng"]].append(i)
    order, end, start = [], 0.0, [0.0] * n
    while len(order) < n:
        best = None
        for e in free:
            if ready[e]:
                s0 = max(free[e], min(est[i] for i in ready[e]))
                if best is None or s0 < best[0]: best = (s0, e)
        s0, e = best
        i = max((j for j in ready[e] if est[j] <= s0 + SLACK), key=lambda j: (prio[j], -j))
        ready[e].remove(i)
        s = max(free[e], est[i])
        start[i] = s
        free[e] = s + ops[i]["cost"]
        fin = free[e] + ops[i]["lat"]
        end = max(end, fin)
        order.append(i)
        for j, l in succ[i]:
            est[j] = max(est[j], (fin + l) if l else free[e])
            left[j] -= 1
            if left[j] == 0: ready[ops[j]["eng"]].append(j)
    return order, end, start


def refine(ops):
    n = len(ops)
    eng = ["vstgyx".index(o["eng"]) for o in ops]
    costs = [[o["costs"][k] for o in ops] for k in range(len(SCEN))]
    hard = [[(d, (LAT_S if eng[d] == eng[i] else LAT_X) + ops[d]["lat"]) for d in sorted(o["hard"])]
            for i, o in enumerate(ops)]
    pred = [hard[i] + [(d, 0.0) for d in sorted(o["soft"])] for i, o in enumerate(ops)]
    succ = [[] for _ in range(n)]
    for i in range(n):
        for d, l in pred[i]: succ[d].append((i, l))
    tail = [o["lat"] for o in ops]
    ends = [i for i in range(n) if not succ[i]]
    rng = np.random.default_rng(1)

    def length(order, cs, fin, a=0):
        free, seen, k = [0.0] * 6, set(), a - 1
        while k >= 0 and len(seen) < 6:
            if eng[order[k]] not in seen:
                seen.add(eng[order[k]])
                free[eng[order[k]]] = fin[order[k]]
            k -= 1
        for k in range(a, n):
            i = order[k]
            e = eng[i]
            s = free[e]
            for d, l in hard[i]:
                x = fin[d] + l
                if x > s: s = x
            free[e] = fin[i] = s + cs[i]
        return max(fin[i] + tail[i] for i in ends)

    def place(key, links, steps, first):
        for i in steps:
            for d, l in links[i]:
                if key[d] >= key[i]: key[i] = key[d] + 1e-3
        fin, a, b = [0.0] * n, [[] for _ in range(6)], [[] for _ in range(6)]
        for i in sorted(range(n), key=lambda i: key[i]):
            c, s = costs[0][i], first[i]
            for d, l in links[i]:
                if fin[d] + l > s: s = fin[d] + l
            la, lb = a[eng[i]], b[eng[i]]
            k = m = len(la)
            while k > 0 and lb[k - 1] > s: k -= 1
            while k < m and la[k] < s + c:
                if lb[k] > s: s = lb[k]
                k += 1
            la.insert(k, s)
            lb.insert(k, s + c)
            fin[i] = s + c
        return fin

    def runs_of(order, cs, fin):
        prev, last = [-1] * n, [-1] * 6
        for i in order:
            prev[i] = last[eng[i]]
            last[eng[i]] = i
        i = max(ends, key=lambda i: fin[i] + tail[i])
        runs, run = [], [i]
        while i >= 0:
            s = fin[i] - cs[i] - 1e-6
            if prev[i] >= 0 and fin[prev[i]] >= s:
                i = prev[i]
                run.append(i)
            else:
                if len(run) > 1: runs.append(run[::-1])
                i = ([d for d, l in hard[i] if fin[d] + l >= s] + [-1])[0]
                run = [i]
        return runs

    order, end, start = schedule(ops)
    total = lambda order: sum(length(order, cs, [0.0] * n) for cs in costs)
    ca = np.array(costs[0])
    best = (total(order), order, np.array(start) + ca)
    for it in range(PASSES):
        fin = best[2]
        t0 = (fin.max() + SPAN) * rng.random() - SPAN
        noise = AMP * rng.random() * rng.random(n) * ((fin >= t0) & (fin <= t0 + SPAN))
        back = place(list(noise - fin), succ, range(n - 1, -1, -1), tail)
        fin = np.array(place([-x for x in back], pred, range(n), [0.0] * n))
        order = [int(i) for i in np.lexsort((np.arange(n), fin - ca))]
        val = total(order)
        if val < best[0]: best = (val, order, fin)
    order = list(best[1])
    fins = [[0.0] * n for _ in costs]
    cur = sum(length(order, cs, f) for cs, f in zip(costs, fins))
    best = (cur, list(order))
    pos = [0] * n
    for k, i in enumerate(order): pos[i] = k
    before, after = [[d for d, l in x] for x in pred], [[d for d, l in x] for x in succ]
    runs, draw, far = None, rng.random((MOVES, 5)).tolist(), rng.exponential(1.0, (MOVES, 2)).tolist()
    for it in range(MOVES):
        r = draw[it]
        if runs is None:
            k = int(r[0] * len(costs))
            runs = runs_of(order, costs[k], fins[k])
        run = runs[int(r[1] * len(runs))]
        a = int(r[2] * (len(run) - 1))
        u, v = run[a], run[min(len(run) - 1, a + 1 + int(1.4 * far[it][0]))]
        pu, pv = pos[u], pos[v]
        win = order[pu:pv + 1]
        up = r[3] < 0.5
        need, engs, ok = {v if up else u}, set(), True
        for i in (win[-2::-1] if up else win[1:]):
            if eng[i] in engs or any(j in need for j in (after if up else before)[i]):
                if eng[i] == eng[u]:
                    ok = False
                    break
                need.add(i)
                engs.add(eng[i])
        if not ok: continue
        order[pu:pv + 1] = [i for i in win if (i in need) == up] + [i for i in win if (i in need) != up]
        new = [list(f) for f in fins]
        val = sum(length(order, cs, f, pu) for cs, f in zip(costs, new))
        if val <= cur + TEMP * (1.0 - it / MOVES) * far[it][1]:
            cur, fins, runs = val, new, None
            for k in range(pu, pv + 1): pos[order[k]] = k
            if val < best[0]: best = (val, list(order))
        else:
            order[pu:pv + 1] = win
            if r[4] < 0.05: runs = None
    return best[1]


SLACK = 150.0
PASSES, AMP, SPAN = 600, 8000.0, 20000.0
MOVES, TEMP = 60000, 250.0
ORDER = {}


def rank_program(g, core, T, topo):
    if T.rank_of(core) is None:
        return
    ops, nleft = build(g, core, T, topo)
    if not ORDER: ORDER[0] = refine(ops)
    order = ORDER[0]
    queue = {"v": g.vector, "s": g.scalar, "t": g.tensor, "g": g, "y": g.sync}
    csem = {"v": "cv", "s": "cs", "t": "ct", "g": "cg"}
    need = set()
    for o in ops: need |= o["hard"]
    count = {e: 0 for e in csem}
    tick = {}
    for i in order:
        o = ops[i]
        if o["sem"] is None and i in need:
            count[o["eng"]] += 1
            tick[i] = (csem[o["eng"]], T.sem[csem[o["eng"]]], count[o["eng"]])
        elif o["sem"] is not None and o["val"] > 0:
            tick[i] = ("a%d" % i, o["sem"], o["val"])
    seen = {e: {} for e in queue}
    for i in order:
        o = ops[i]
        e = o["eng"]
        if e == "x": continue
        want = {}
        for d in o["hard"]:
            k, sem, v = tick[d]
            if v > seen[e].get(k, 0) and v > want.get(k, (None, 0))[1]: want[k] = (sem, v)
        for k in sorted(want):
            queue[e].wait_ge(want[k][0], want[k][1])
            seen[e][k] = want[k][1]
        ins = o["fn"]()
        if o["sem"] is None and i in tick: ins.then_inc(tick[i][1], 1)
    for e in csem:
        if count[e]: g.sync.wait_ge(T.sem[csem[e]], count[e])
    for i in order:
        if ops[i]["sem"] is not None and ops[i]["val"] > 0: g.sync.wait_ge(ops[i]["sem"], ops[i]["val"])
    g.sync.wait_ge(T.sem.left, nleft)
